import numpy as np, ml_dtypes
CORES = [1,5,17,21,33,37,49,53]
N = 8
import mx_ref
BF = ml_dtypes.bfloat16
def gentries(a):
    return np.ascontiguousarray(a.reshape(8, 16, -1).transpose(0, 2, 1)).reshape(8, -1)
def gtable(e):
    e = np.asarray(e); return np.ascontiguousarray(e.reshape(8, -1, 16).transpose(0, 2, 1)).reshape(128, -1).astype(np.int32)
def gcols(t, e):
    v = np.concatenate([t.reshape(8, 16, -1, 4), np.zeros((8, 16, 1, 4), BF)], axis=2)
    return np.ascontiguousarray(np.stack([v[g][:, e[g]] for g in range(8)])).reshape(128, -1)
def tile(rs):
    return np.stack(rs, axis=2).reshape(128, -1).astype(BF)
def pick(q, e):
    c = np.concatenate([q[0].reshape(128, -1, 4), np.zeros((128, 1, 4), np.uint8)], axis=1); s = np.concatenate([q[1], np.ones((16, 1), np.uint8)], axis=1)
    return (np.ascontiguousarray(c[:, e].reshape(128, -1)), np.ascontiguousarray(s[:, e]))
def join(*qs):
    return (np.concatenate([q[0] for q in qs], axis=1), np.concatenate([q[1] for q in qs], axis=1))
def put(q, e, v):
    c, s = q[0].reshape(128, -1, 4).copy(), q[1].copy(); c[:, e] = v[0].reshape(128, -1, 4); s[:, e] = v[1]
    return (c.reshape(128, -1), s)
def pk(c, s):
    return (np.ascontiguousarray(c), mx_ref.live(s))
def emit(q):
    return q[0], q[1]
def packed(v, rng):
    q = [mx_ref.quantize(np.ascontiguousarray(v[r])) for r in range(N)]
    return np.stack([a for a, b in q]), np.stack([mx_ref.plane(b, rng) for a, b in q])
def values_of_codes():
    e, c = np.zeros((128, 128, 4), np.float32), np.zeros((128, 2, 4), np.uint8)
    e[np.arange(128), np.arange(128), 0] = 1
    c[:127, :, 0] = np.arange(256).reshape(2, 128).T[:127]
    return mx_ref.matmul(mx_ref.quantize(e.reshape(128, 512).astype(BF)), (c.reshape(128, 8), np.full((16, 2), 127, np.uint8))).T.reshape(-1).astype(np.float64)
CODE_VALUE, SCALE_VALUE = values_of_codes(), 2.0 ** (np.arange(256) - 127.0)
def decode(q):
    return (CODE_VALUE[q[0]].reshape(16, 8, -1, 4) * SCALE_VALUE[q[1]][:, None, :, None] + 0.0).reshape(128, -1).astype(np.float32)
def f(rng, *shape):
    return mx_ref.flush((rng.standard_normal(shape, dtype=np.float32) * np.exp2(rng.integers(-2, 3, shape[:-1] + (1,)))).astype(BF))
def wide(rng, *shape, cols=0):
    v = rng.standard_normal(shape, dtype=np.float32) * np.exp2(rng.integers(-12, 13, shape)).astype(np.float32)
    if cols: v *= np.repeat(np.exp2(rng.integers(-cols, cols + 1, shape[:-2] + (1, shape[-1] // 4))) * (rng.random(shape[:-2] + (1, shape[-1] // 4)) > 0.0625), 4, axis=-1).astype(np.float32)
    return mx_ref.flush(v.astype(BF))
C, K, M, R = 512, 32, 16, 3
BASE = M * np.concatenate([np.arange(K), np.arange(K)])
def matrices(a):
    return a.reshape(8, 16, K // 16, M, M).transpose(0, 2, 1, 3, 4).reshape(8, K, M, M).astype(np.int64)
def stored(m):
    return np.ascontiguousarray(m.reshape(8, K // 16, 16, M, M).transpose(0, 2, 1, 3, 4)).reshape(128, -1)
def numbers_of(rng):
    return {"x": np.array(f(rng, N, 128, 4 * C)), "u": np.array(f(rng, N, 128, 512)), "v": np.array(f(rng, N, 128, 512))}
def nodes(rng):
    return np.stack([gtable(np.stack([rng.permutation(C) for g in range(8)])) for r in range(N)])
def arrows(a):
    a = np.triu(a, 1)
    a = a - a.swapaxes(-1, -2)
    return np.stack([stored(a[r]) for r in range(N)]).astype(np.int32)
def some_arrows(rng):
    return rng.integers(-3, 4, (N, 8, K, M, M)) * (rng.random((N, 8, K, M, M)) < 0.6)
def laid(w, nd):
    w = w.reshape(N, 8, 16, C, 4)
    t = np.zeros_like(w)
    for r in range(N):
        e = gentries(nd[r])
        for g in range(8): t[r, g][:, e[g]] = w[r, g]
    return t.reshape(N, 128, 4 * C).astype(BF)
def weights(rng, still=[], by=1.0):
    w = np.array(f(rng, N, 128, 2048)).reshape(N, 8, 16, 4, 8, 16, 4)
    for i in still:
        w[:, :, i] = 0
        w[:, :, :, :, :, i] = 0
    w = mx_ref.flush((w.astype(np.float32) * np.float32(by)).astype(BF))
    c, s = packed(np.ascontiguousarray(w).reshape(N, 128, 2048), rng)
    return {"wc": c, "ws": s}
def setup_inputs(rng):
    return {**numbers_of(rng), "nd": nodes(rng), "ar": arrows(some_arrows(rng)), **weights(rng)}
def setup_inputs_ties(rng):
    d = numbers_of(rng)
    nd = nodes(rng)
    w = d["x"].reshape(N, 8, 16, C, 4)
    w[:, :, 0] = 0
    w[:, :, 0, :, 0] = rng.integers(1, 4, (N, 8, C)).astype(np.float32).astype(BF)
    u = d["u"].reshape(N, 128, 128, 4)
    u[:, :, ::16] = 0
    o = rng.permutation(N)
    for r in range(N):
        for h in range(0, 128, 16): u[r, h, h, 0] = 0.0 if r == o[0] else -1.0 if r == o[1] else 1.0
    return {"x": laid(w, nd), "u": u.reshape(N, 128, 512), "v": d["v"], "nd": nd, "ar": arrows(some_arrows(rng)), **weights(rng, [0])}
def setup_inputs_near(rng):
    d = numbers_of(rng)
    nd = nodes(rng)
    w = d["x"].astype(np.float32).reshape(N, 8, 16, K, M, 4)
    w[:, :, 0] = 0
    w[:, :, 8:] = 0
    s = rng.integers(0, 16, (N, 8, K, M))
    w[:, :, 8] = ((s[..., None] >> np.arange(4)) & 1) * np.exp2(np.arange(4) - 23.0)
    u = d["u"].reshape(N, 128, 128, 4)
    u[:, :, ::16] = 0
    o = rng.permutation(N) % 4
    for r in range(N):
        k = 1.0 if o[r] == 0 else 2.0 ** -30
        c = rng.choice([-1.0, 1.0], (8, K, 1))
        if o[r] < 2:
            w[r, :, 0, :, :, 0] = c
            w[r, :, 11, :, :, 0] = 2.0 ** -10
        elif o[r] == 2:
            far = np.argsort(rng.random((8, K, M)), axis=2)
            w[r, :, 0, :, :, 0] = 1.0 * (far == 0) - 1.0 * (far == 1)
            for g in rng.permutation(8)[:4]: w[r, g, 0, rng.integers(K), rng.integers(M), 0] = 2.0 ** 26
        else:
            w[r, :, 8] = 0
            w[r, :, 8, :, :, 0] = c * rng.integers(8, 16, (8, K, M)) * 2.0 ** -27
        for h in range(0, 128, 16):
            if o[r] < 2:
                u[r, h, h, 0] = k
                u[r, h + 11, h, 0] = k
            if o[r] == 2: u[r, h, h, 0] = 16.0
            if o[r] < 3: u[r, h + 8, h] = k
            else: u[r, h + 8, h, 0] = k
    return {"x": laid(w, nd), "u": u.reshape(N, 128, 512), "v": d["v"], "nd": nd, "ar": arrows(some_arrows(rng)), **weights(rng, [0, 8, 9, 10, 11, 12, 13, 14, 15])}
def setup_inputs_huge(rng):
    d = numbers_of(rng)
    o = rng.permutation(N)
    a = some_arrows(rng)
    x = 0.8 + 0.1 * rng.random((N, 128, C, 4))
    u = d["u"].reshape(N, 128, 128, 4)
    for r in range(N):
        c = rng.choice([-1.0, 1.0], (C, 1))
        k = 2.0 ** 30 * (1.0 - 0.1 * rng.random((128, 8, 4)))
        if o[r] < 2: c = -np.ones((C, 1))
        if o[r] == 3:
            c = -np.ones((C, 1))
            c[rng.permutation(C)[:K]] = 1.0
            x[r] = 0.9375
            k[:] = 2.0 ** 30
        if o[r] % 2 == 1: a[r] = 0
        x[r] *= c * (2.0 ** 30 if o[r] % 2 == 1 else 2.0 ** 28 if o[r] == 0 else 2.0 ** 27)
        u[r, :, ::16] = k.astype(np.float32).astype(BF)
    return {"x": x.astype(np.float32).reshape(N, 128, 4 * C).astype(BF), "u": u.reshape(N, 128, 512), "v": d["v"], "nd": nodes(rng), "ar": arrows(a), **weights(rng, [], 2.0 ** -14)}
def setup_inputs_knots(rng):
    d = numbers_of(rng)
    e = rng.permutation(N)
    kind = rng.integers(0, 4, (N, 8, K, 1, 1))
    kind[e[0]] = 0
    kind[e[1]] = 1
    sign = rng.choice([-1, 1], (N, 8, K, M, M))
    half = sign * (rng.random((N, 8, K, M, M)) < 0.5)
    a = np.where(kind == 0, 0, np.where(kind == 1, sign * rng.integers(1, 4, (N, 8, K, M, M)), np.where(kind == 2, half, 3 * half)))
    place = np.arange(8)[:, None, None] * 4 + np.arange(4)
    most = place == rng.integers(0, 32, (N, 16, 1, C, 1))
    x = (129.0 + 2.0 * rng.integers(0, 64, (N, 16, 8, C, 4))) * np.exp2(-7.0 - rng.integers(8, 15, (N, 16, 8, C, 4)))
    x = np.where(most, 1.96875, x) * rng.choice([-1.0, 1.0], (N, 16, 8, C, 4)) * np.exp2(rng.integers(-2, 3, (N, 16, 1, C, 1)))
    return {"x": x.astype(np.float32).reshape(N, 128, 4 * C).astype(BF), "u": d["u"], "v": d["v"], "nd": nodes(rng), "ar": arrows(a), **weights(rng)}
def setup_inputs_spread(rng):
    d = setup_inputs(rng)
    d["x"] = wide(rng, N, 128, 4 * C, cols=6)
    return d
def check_inputs(d):
    b = []
    for k in ("x", "u", "v"):
        a = np.abs(d[k].astype(np.float32))
        if not (np.isfinite(a).all() and ((a == 0) | (a >= 2.0 ** -30) & (a <= 2.0 ** 30)).all()): b.append("a value of " + k)
    none, least, most = [emit(mx_ref.quantize(np.full((128, 16), k, np.float32).astype(BF)))[1][0, 0] for k in (0.0, 2.0 ** -30, 2.0 ** 30)]
    for r in range(N):
        if (np.sort(gentries(d["nd"][r]), axis=1) != np.arange(C)).any(): b.append("nd: a group without every column once")
        a = matrices(d["ar"][r])
        if (np.abs(a) > 3).any(): b.append("an entry of ar")
        if (a != -a.swapaxes(-1, -2)).any(): b.append("ar: B[j, i] isn't -B[i, j]")
        if ((d["wc"][r] & 0x7F) == 0x7F).any(): b.append("wc: a code that is no number")
        s = mx_ref.live(d["ws"][r])
        if ((s != none) & ((s < least) | (s > most))).any(): b.append("ws: a scale out of range")
    return b
def parts(t, n, e):
    return gcols(t, np.where(e < 0, -1, np.take_along_axis(n, BASE + np.maximum(e, 0), axis=1))).astype(np.float32)
def pair(t, n, w):
    e = np.argsort(-w, axis=2, kind="stable")[:, :, :2]
    e = np.where(np.take_along_axis(w, e, axis=2) > 0, e, -1)
    return ((parts(t, n, e[:, :, 0]) + parts(t, n, e[:, :, 1])) * np.float32(0.5)).astype(BF).astype(np.float32)
def reference(x, u, v, nd, ar, wc, ws):
    qu = [mx_ref.quantize(u[r]) for r in range(N)]
    lay = [pk(wc[r], ws[r]) for r in range(N)]
    now = [x[r] for r in range(N)]
    node = [gentries(nd[r]) for r in range(N)]
    arrow = [matrices(ar[r]) for r in range(N)]
    for t in range(R):
        held, made, sent, into = [], [], [], []
        for r in range(N):
            q = mx_ref.quantize(now[r])
            own = decode(q).astype(BF)
            s = mx_ref.matmul(qu[r], q)[::16] + np.float32(0.0)
            s = np.take_along_axis(s, node[r], axis=1).reshape(8, K, M)
            first = np.argmax(s, axis=2)
            row = np.take_along_axis(arrow[r], first[:, :, None, None], axis=2)[:, :, 0]
            free = (row == 0) & (np.arange(M) != first[:, :, None])
            second = np.argmax(np.where(free, s, -np.inf), axis=2)
            k = np.concatenate([first, second], axis=1)
            full = np.concatenate([np.ones((8, K), bool), free.any(axis=2)], axis=1)
            row = np.concatenate([row, np.take_along_axis(arrow[r], second[:, :, None, None], axis=2)[:, :, 0]], axis=1) * full[:, :, None]
            y = (np.maximum(pair(own, node[r], -row), pair(own, node[r], row)) - parts(own, node[r], np.where(full, k, -1))).astype(BF)
            held.append(own)
            made.append(y)
            sent.append(mx_ref.quantize(y))
            e = np.tile(np.arange(C), (8, 1))
            g, i = np.nonzero(full)
            e[g, np.take_along_axis(node[r], BASE + k, axis=1)[g, i]] = C + i
            into.append(e)
            more = (np.abs(row)[:, :, :, None] * row[:, :, None, :] - row[:, :, :, None] * np.abs(row)[:, :, None, :]) // 2
            turn = np.ones((8, 2 * K, M), np.int64)
            np.put_along_axis(turn, k[:, :, None], np.where(full, -1, 1)[:, :, None], axis=2)
            turn = turn[:, :K] * turn[:, K:]
            arrow[r] = np.clip(arrow[r] + more[:, :K] + more[:, K:], -3, 3) * turn[:, :, :, None] * turn[:, :, None, :]
        for r in range(N):
            q = sent[(r - 1) % N]
            new = tile([mx_ref.matmul(pick(lay[r], np.arange(128 * b, 128 * b + 128)), q) * np.float32(0.03125) + made[r][:, b::4].astype(np.float32) for b in range(4)])
            now[r] = gcols(np.concatenate([held[r], new], axis=1), into[r])
    y, oa = np.zeros((N, 128, C), np.float32), np.zeros(ar.shape, np.float32)
    oc, osc = np.zeros((N, 128, 4 * C), np.uint8), np.zeros((N, 16, C), np.uint8)
    for r in range(N):
        q = mx_ref.quantize(now[r])
        y[r] = mx_ref.matmul(mx_ref.quantize(v[r]), q)
        oa[r] = stored(arrow[r])
        oc[r], osc[r] = emit(q)
    return {"y": y, "oa": oa, "oc": oc, "osc": osc}

@@ -1,0 +1,510 @@
+from concourse.bass import DstId, RemoteDMATransfer
+from concourse.mybir import dt, AluOpType, AxisListType, ActivationFunctionType
+
+OP = AluOpType
+AF = ActivationFunctionType
+R = 3
+W = 2176
+ROW, BLK = 17, 323
+SEL = 2 * BLK
+SQ3 = 867
+UNIT = 131072.0
+BIG = 1.0e29
+
+CODES, PLANE, BF, F32, I32, U16 = "float8_e4m3fn_x4", "uint8", "bfloat16", "float32", "int32", "uint16"
+SCRATCH = {"PS": ("psum", [128, 3072], F32)}
+for _n, _w, _d in (
+    ("XT", 2048, BF), ("UT", 512, BF), ("VT", 512, BF), ("ET", 528, BF),
+    ("UQ", 128, CODES), ("US", 128, PLANE), ("UQR", 128, CODES), ("USR", 128, PLANE), ("VQ", 128, CODES), ("VS", 128, PLANE),
+    ("WQ", 512, CODES), ("WS", 512, PLANE), ("EQ", 512, CODES), ("ES", 512, PLANE),
+    ("NDI", 32, I32), ("NDX", 32, I32), ("NDF", 32, F32), ("ARI", 512, I32), ("IA", 360, I32), ("FA", 400, F32),
+    ("ONE", 592, BF), ("KI", 512, F32), ("OWN", 512, F32),
+    ("L32", 32, U16), ("UL", 8, U16), ("SL", 36, U16), ("AL", 38, U16), ("OUTL", 38, U16), ("OL", 32, U16),
+    ("N4", 32, F32), ("HL", 80, F32),
+    ("CM", 512, F32), ("PW", 528, F32), ("FOLD", 544, BF), ("YC", 323, BF), ("KEEP", 578, BF), ("RS0", 34, F32), ("RST", 34, F32),
+    ("SEG", 152, F32), ("PRI", 152, F32), ("CC", 152, F32), ("ZK", 16, F32), ("ARB", 528, BF),
+    ("SG", 544, F32), ("Z", 544, F32), ("RX", 34, F32), ("TT", 34, F32), ("IX", 4, F32), ("KAP", SEL, BF), ("DM", SEL, BF),
+    ("RS", 2 * SEL, BF), ("GT", 34, F32), ("S2", 34, F32), ("KEY", 152, F32), ("RK", 308, F32),
+    ("DEC", 16, I32), ("DCM", 16, I32), ("LL", 64, U16), ("KC", 4, F32), ("KL", 16, U16),
+    ("KF", 256, BF), ("AB", 512, BF), ("IO2", 512, BF), ("M2", 256, BF), ("MH", 256, BF), ("YT", 512, BF), ("YW", 256, BF),
+    ("V32", 256, BF), ("VV", 256, BF), ("CLN", 68, BF), ("RVF", 48, BF), ("RVS", 48, BF), ("FV", 48, BF), ("FG", 68, BF),
+    ("FS", 68, BF), ("FH", 34, BF), ("SPF", 578, BF), ("SPS", 578, BF), ("SPA", 578, BF), ("SPX", 578, BF),
+    ("D0F", 1776, BF), ("D0S", 1776, BF), ("D0X", 1776, BF), ("TA", 1784, BF), ("TB", 1744, BF), ("TC", 1744, BF), ("TD", 1744, BF),
+    ("OAO", 512, F32), ("YO", 512, F32),
+) + tuple(("F%d" % t, W, BF) for t in range(R)) + tuple((n + "%d" % t, 128, d) for t in range(R) for n, d in (("SQ", CODES), ("SS", PLANE), ("LQ", CODES), ("LS", PLANE))) \
+  + tuple((n + "%d" % t, 512, d) for t in range(R + 1) for n, d in (("XQ", CODES), ("XS", PLANE))):
+    SCRATCH[_n] = ("sbuf", [128, _w], _d)
+
+SEMAPHORES = ["cv", "cs", "ct", "cp", "left"] + ["arr%d" % t for t in range(R)] + ["dm%d" % i for i in range(48)]
+COUNTER = {"v": "cv", "s": "cs", "t": "ct", "p": "cp"}
+PART = {n: ("IA", a, w) for n, a, w in (("PI", 0, 1), ("PMI", 8, 1), ("ULI", 16, 8), ("EI", 24, 38), ("EE", 64, 38), ("EM", 104, 38), ("QD", 144, 38),
+                                       ("OLI", 184, 32), ("OLX", 216, 32), ("NI", 248, 32), ("NHI", 280, 32), ("NLO", 312, 32))}
+PART.update({n: ("FA", a, w) for n, a, w in (("PM", 0, 1), ("H17", 8, 38), ("H256", 48, 38), ("YE", 88, 38), ("XE", 128, 38), ("T1", 168, 38),
+                                            ("T2", 208, 38), ("T3", 248, 38), ("T4", 288, 38), ("T5", 328, 38))})
+
+
+def make_tracker(g, T):
+    eng = {"v": g.vector, "s": g.scalar, "t": g.tensor, "p": g, "y": g.sync}
+    count = {}
+    known = {q: {} for q in eng}
+    hist = {}
+
+    def view(name, lo=0, hi=None, step=1, ind=None, cast=None):
+        if name in PART:
+            name, at, width = PART[name]
+            lo, hi = lo + at, (width if hi is None else hi) + at
+        t = T[name]
+        hi = int(t.shape[1]) if hi is None else hi
+        ap = t[:, lo:hi:step] if step != 1 else t[:, lo:hi]
+        deps = [(name, lo, hi, step)]
+        if cast is not None:
+            ap = ap.bitcast(cast)
+        if ind is not None:
+            ap = ap.indirect(T[ind[0]][:, ind[1]:ind[2]])
+            deps.append((ind[0], ind[1], ind[2], 1))
+        return ap, deps
+
+    def wait(q, sem, val):
+        if known[q].get(sem, 0) < val:
+            known[q][sem] = val
+            eng[q].wait_ge(T.sem[sem], val)
+
+    def before(q, reads, writes):
+        need = {}
+        for acc, wr in ((reads, False), (writes, True)):
+            for name, lo, hi, st in acc:
+                for (a, b, w, sem, val, oq, s2) in hist.get(name, []):
+                    if a < hi and lo < b and (w or wr) and (st != s2 or (lo - a) % st == 0):
+                        need[sem] = max(need.get(sem, 0), val)
+        for sem in need:
+            wait(q, sem, need[sem])
+
+    def after(q, reads, writes, sem, val):
+        def covered(h, lo, hi, st):
+            return lo <= h[0] and h[1] <= hi and (st == 1 or st == h[6] and (lo - h[0]) % st == 0)
+        for name, lo, hi, st in writes:
+            hist[name] = [h for h in hist.get(name, []) if not covered(h, lo, hi, st)] + [(lo, hi, True, sem, val, q, st)]
+        for name, lo, hi, st in reads:
+            hist[name] = [h for h in hist.get(name, []) if h[2] or h[5] != q or not covered(h, lo, hi, st)] + [(lo, hi, False, sem, val, q, st)]
+
+    def bank(d):
+        return (d[0], d[1] // 512 * 512, (d[2] + 511) // 512 * 512, 1) if d[0] == "PS" else d
+
+    def call(q, fn, outs, ins):
+        reads = [d for v in ins for d in v[1] if d[0] != "PS"] + [d for v in outs for d in v[1][1:]]
+        writes = [bank(v[1][0]) for v in outs] + [bank(d) for v in ins for d in v[1] if d[0] == "PS"]
+        before(q, reads, writes)
+        sem = COUNTER[q]
+        count[sem] = count.get(sem, 0) + 1
+        fn(eng[q]).then_inc(T.sem[sem], 1)
+        after(q, reads, writes, sem, count[sem])
+
+    def dma(q, out, in_):
+        before(q, in_[1], out[1])
+        n = count.get("dma", 0)
+        count["dma"] = n + 1
+        eng[q].dma_start(out[0], in_[0]).then_inc(T.sem["dm%d" % n], 16)
+        after("dma%d" % n, in_[1], out[1], "dm%d" % n, 16)
+        count["dm%d" % n] = 16
+        return "dm%d" % n
+
+    return view, wait, before, after, call, dma, count
+
+
+def rank_program(g, core, T, topo):
+    rank = T.rank_of(core)
+    if rank is None:
+        return
+    f, wait, before, after, call, dma, count = make_tracker(g, T)
+
+    def tt(out, a, b, op):
+        call("v", lambda e: e.tensor_tensor(out[0], a[0], b[0], op), [out], [a, b])
+
+    def ts(out, a, s1, op0, s2=None, op1=None):
+        ins = [a] + [s for s in (s1, s2) if isinstance(s, tuple)]
+        x1 = s1[0] if isinstance(s1, tuple) else s1
+        x2 = s2[0] if isinstance(s2, tuple) else s2
+        if op1 is None:
+            call("v", lambda e: e.tensor_scalar(out[0], a[0], x1, None, op0), [out], ins)
+        else:
+            call("v", lambda e: e.tensor_scalar(out[0], a[0], x1, x2, op0, op1), [out], ins)
+
+    def cp(out, a):
+        call("v", lambda e: e.tensor_copy(out[0], a[0]), [out], [a])
+
+    def fill(out, c):
+        call("v", lambda e: e.memset(out[0], c), [out], [])
+
+    def scan(out, d0, d1, init, op0, op1):
+        call("v", lambda e: e.tensor_tensor_scan(out[0], d0[0], d1[0], init, op0, op1), [out], [d0, d1])
+
+    def total(out, a):
+        call("v", lambda e: e.tensor_reduce(out[0], a[0], AxisListType.X, OP.add), [out], [a])
+
+    def quant(qn, sn, lo, hi, a):
+        q, s = f(qn, lo, hi), f(sn, lo, hi)
+        call("v", lambda e: e.quantize_mx(q[0], s[0], a[0]), [q, s], [a])
+
+    def act(out, a, func=AF.Copy, scale=1.0, bias=None):
+        if bias is None:
+            call("s", lambda e: e.activation(out[0], a[0], func, scale=scale), [out], [a])
+        elif isinstance(bias, tuple):
+            call("s", lambda e: e.activation(out[0], a[0], func, bias=bias[0], scale=scale), [out], [a, bias])
+        else:
+            call("s", lambda e: e.activation(out[0], a[0], func, bias=bias, scale=scale), [out], [a])
+
+    def mm(out, l, ls, r, rs):
+        call("t", lambda e: e.matmul_mx(out[0], l[0], ls[0], r[0], rs[0], True, True), [out], [l, ls, r, rs])
+
+    def iota(out, pattern, base=0, cm=0, small=True):
+        if small:
+            call("p", lambda e: e.iota(out[0], pattern, base, cm, allow_small_or_imprecise_dtypes=True), [out], [])
+        else:
+            call("p", lambda e: e.iota(out[0], pattern, base, cm), [out], [])
+
+    def affine(out, a, pattern, op, fillv, base, cm):
+        call("p", lambda e: e.affine_select(out[0], a[0], pattern, op, fillv, base, cm), [out], [a])
+
+    dma("y", f("NDI"), (T.nd[:, :], []))
+    dma("s", f("UT"), (T.u[:, :], []))
+    dma("y", f("XT", 0, 1024), (T.x[:, 0:1024], []))
+    dma("s", f("XT", 1024, 2048), (T.x[:, 1024:2048], []))
+    blocks = []
+    for i in range(16):
+        a, p, h = 32 * (i // 4), 16 * (i % 4 // 2), 16 * (i % 2)
+        blocks.append(dma("y" if i % 2 else "s", (T.NDX[a + p:a + p + 16, h:h + 16], []), (T.nd[a + h:a + h + 16, p:p + 16], [])))
+    dma("y", f("ARI"), (T.ar[:, :], []))
+    dma("s", f("WQ", cast=dt.uint8), (T.wc[:, :], []))
+    dma("y", f("WS"), (T.ws[:, :], []))
+    dma("s", f("VT"), (T.v[:, :], []))
+
+    fill(f("ONE"), 1.0)
+    fill(f("RS0"), BIG)
+    iota(f("PI"), [[0, 1]], 0, 1, small=False)
+    iota(f("EI"), [[16, 38]], small=False)
+    iota(f("KI"), [[1, 16], [0, 32]])
+    iota(f("ULI"), [[16, 8]], small=False)
+    affine(f("ET"), f("ONE", 0, 528), [[-1, 528]], OP.is_equal, 0.0, 3, 4)
+    affine(f("FOLD"), f("ONE", 0, 544), [[0, 34], [1, 16]], OP.not_equal, 0.0, 0, 0)
+    affine(f("RST"), f("RS0"), [[0, 2], [1, 17]], OP.not_equal, -BIG, 0, 0)
+    iota(f("TA", 1734, 1784), [[0, 50]])
+    iota(f("YC"), [[0, 19], [1, 17]])
+    iota(f("SEG"), [[1, 8], [0, 19]], 1)
+    iota(f("PRI"), [[0, 8], [-4096, 19]], 65536)
+    iota(f("F0", 2048, W), [[0, 128]])
+    affine(f("KEEP"), f("ONE", 0, 578), [[0, 34], [1, 17]], OP.not_equal, 0.0, 0, 0)
+    iota(f("YT", 256, 512), [[0, 256]])
+    for t in range(1, R):
+        iota(f("F%d" % t, 2048, W), [[0, 128]])
+    iota(f("OLI"), [[867, 2], [51, 16]], 56, small=False)
+    iota(f("OLX"), [[0, 2], [1, 16]], small=False)
+    for n in ("SPF", "SPS", "SPA", "SPX"):
+        act(f(n), f("ONE", 0, 578), AF.Copy, 0.0)
+    for n in ("D0F", "D0S", "D0X"):
+        act(f(n, 0, 1776, 3), f("ONE"), AF.Copy, 0.0)
+    for j in (1, 2):
+        act(f("TD", j, 1734, 3), f("ONE", 0, 578), AF.Copy, 0.0)
+
+    ts(f("PMI"), f("PI"), 15, OP.bitwise_and)
+    cp(f("PM"), f("PMI"))
+    pm = f("PM")
+    ts(f("EE"), f("EI"), pm, OP.add)
+    ts(f("EM"), f("EE"), 3856.0, OP.mult)
+    ts(f("QD"), f("EM"), 16, OP.logical_shift_right)
+    ts(f("H17"), f("QD"), 17.0, OP.is_ge, 17.0, OP.mult)
+    ts(f("T1"), f("QD"), -17.0, OP.mult)
+    ts(f("H256"), f("QD"), 17.0, OP.is_ge, 256.0, OP.mult)
+    tt(f("XE"), f("QD"), f("H17"), OP.subtract)
+    tt(f("YE"), f("T1"), f("EE"), OP.add)
+    ts(f("OWN"), f("KI"), pm, OP.is_equal)
+    for h in range(2):
+        cp(f("L32", h, 32, 2), f("NDI", 16 * h, 16 * h + 16))
+    ts(f("T1"), f("XE"), 0.0, OP.is_equal, 1000.0, OP.mult)
+    ts(f("T3"), f("YE"), 0.0, OP.is_equal, 1000.0, OP.mult)
+    cp(f("CM", ind=("L32", 0, 32)), f("OWN"))
+    ts(f("T2"), f("XE"), 16.0, OP.mult, -17.0, OP.add)
+    tt(f("T4"), f("XE"), f("T1"), OP.add)
+    tt(f("T5"), f("T1"), f("T3"), OP.add)
+    cp(f("UL"), f("ULI"))
+    tt(f("T1"), f("T2"), f("YE"), OP.add)
+    quant("UQ", "US", 0, 128, f("UT"))
+    tt(f("T3"), f("H256"), f("T5"), OP.add)
+    tt(f("T2"), f("T4"), f("YE"), OP.is_equal)
+    cp(f("UQR", cast=dt.uint32), f("UQ", cast=dt.uint32, ind=("UL", 0, 8)))
+    cp(f("USR"), f("US", ind=("UL", 0, 8)))
+    for s in blocks:
+        wait("v", s, 16)
+    ts(f("NDF"), f("NDX"), 4.0, OP.mult)
+    tt(f("T5"), f("T1"), f("T3"), OP.add)
+    ts(f("T4"), f("T2"), 520.0, OP.mult)
+    call("v", lambda e: e.transpose(T.N4[:, :], T.NDF[:, :]), [f("N4")], [f("NDF")])
+    fill(f("SL", 0, 36, 18), 512)
+    fill(f("SL", 17, 18), 512)
+    fill(f("SL", 35, 36), 512)
+    for h in range(2):
+        ts(f("SL", 18 * h + 1, 18 * h + 17), f("N4", 16 * h, 16 * h + 16), 0.25, OP.mult)
+    fill(f("PW", 512, 528), -BIG / 32)
+
+    def scores(t, src):
+        for a in range(2):
+            quant("XQ%d" % t, "XS%d" % t, 256 * a, 256 * a + 256, f(src, 1024 * a, 1024 * a + 1024))
+            mm(f("PS", 512 * a, 512 * a + 256), f("UQR"), f("USR"), f("XQ%d" % t, 256 * a, 256 * a + 256), f("XS%d" % t, 256 * a, 256 * a + 256))
+        for a in range(2):
+            tt(f("PW", 256 * a, 256 * a + 256), f("PS", 512 * a, 512 * a + 256), f("CM", 256 * a, 256 * a + 256), OP.mult)
+        act(f("SG", 0, 272), f("PW", 0, 528, ind=("SL", 0, 17)))
+        act(f("SG", 272, 544), f("PW", 0, 528, ind=("SL", 18, 35)))
+
+    def unpack(t):
+        for b in range(4):
+            mm(f("PS", 1024 + 512 * b, 1536 + 512 * b), f("EQ", 128 * b, 128 * b + 128), f("ES", 128 * b, 128 * b + 128), f("XQ%d" % t), f("XS%d" % t))
+        for b in range(4):
+            act(f("F%d" % t, b, 2048, 4), f("PS", 1024 + 512 * b, 1536 + 512 * b))
+
+    def differences(h):
+        scan(f("DM", BLK * h + 1, BLK * h + 289), f("TA", SQ3 * h + 2, SQ3 * h + 864, 3), f("TA", SQ3 * h + 8, SQ3 * h + 870, 3), 0.0, OP.subtract, OP.subtract)
+
+    scores(0, "XT")
+
+    ts(f("T1"), f("T5"), 512.0, OP.min)
+    ts(f("ARB", 0, 512), f("ARI"), -UNIT, OP.mult)
+    fill(f("ARB", 512, 520), 0.0)
+    tt(f("T3"), f("T1"), f("T4"), OP.max)
+    fill(f("ARB", 520, 528), UNIT / 64)
+    cp(f("NI"), f("N4"))
+    cp(f("AL"), f("T3"))
+    act(f("TA", 2, 1778, 3), f("ARB", ind=("AL", 0, 37)))
+    fill(f("HL"), 0.0)
+    for b in range(4):
+        quant("EQ", "ES", 128 * b, 128 * b + 128, f("ET", 3 - b, 515 - b))
+    unpack(0)
+    ts(f("NHI"), f("NI"), 1920, OP.bitwise_and)
+    ts(f("NLO"), f("NI"), 127, OP.bitwise_and)
+    for h in range(2):
+        fill(f("HL", 36 * h, 36 * h + 1), 2048.0)
+        ts(f("HL", 36 * h + 18, 36 * h + 19), pm, 4.0, OP.mult, 64.0 * h, OP.add)
+    for h in range(2):
+        cp(f("HL", 36 * h + 1, 36 * h + 17), f("NHI", 16 * h, 16 * h + 16))
+        cp(f("HL", 36 * h + 19, 36 * h + 35), f("NLO", 16 * h, 16 * h + 16))
+    for h in range(2):
+        fill(f("DM", BLK * h, BLK * h + 1), 0.0)
+    for h in range(2):
+        for j in range(2):
+            tt(f("DM", BLK * h + 289 + 17 * j, BLK * h + 306 + 17 * j), f("HL", 36 * h + 18 * j, 36 * h + 18 * j + 17), f("HL", 36 * h + 18 * j + 1, 36 * h + 18 * j + 18), OP.subtract)
+
+    def outer_list():
+        tt(f("T2"), f("YE"), f("H17"), OP.add)
+        cp(f("OUTL"), f("T2"))
+
+    def bases():
+        ts(f("CC"), f("SEG"), 1048576.0, OP.mult)
+        for j in range(2):
+            ts(f("ZK", 8 * j, 8 * j + 8), f("SEG", 0, 152, 19), 1048576.0, OP.mult, 71680.0, OP.add)
+
+    def priorities():
+        tt(f("CC"), f("CC"), f("PRI"), OP.add)
+        fill(f("RK", 0, 1), -BIG)
+
+    def member_columns(lo):
+        for s in range(lo, lo + 4):
+            a = 19 * s + 1
+            tt(f("CC", a, a + 16), f("CC", a, a + 16), f("N4", 16 * (s % 2), 16 * (s % 2) + 16), OP.add)
+
+    def output_list():
+        ts(f("T1", 0, 1), pm, 3.0, OP.mult)
+        ts(f("QD", 0, 32), f("OLX"), pm, OP.is_equal, 1736.0, OP.mult)
+        ts(f("EM", 0, 32), f("OLI"), f("T1", 0, 1), OP.add)
+        tt(f("EE", 0, 32), f("EM", 0, 32), f("QD", 0, 32), OP.max)
+        cp(f("OL"), f("EE", 0, 32))
+
+    def choose(s, j, slots):
+        def slot():
+            if slots:
+                slots.pop(0)()
+        for h in range(2):
+            scan(f("RX", ROW * h, ROW * h + ROW), f("RST", 0, ROW), s(h), 0.0, OP.min, OP.max)
+        slot()
+        for h in range(2):
+            ts(f("TT", ROW * h, ROW * h + ROW), f("RX", ROW * h, ROW * h + ROW), f("RX", ROW * h + 16, ROW * h + 17), OP.is_lt)
+        slot()
+        for h in range(2):
+            total(f("IX", 2 * j + h, 2 * j + h + 1), f("TT", ROW * h, ROW * h + ROW))
+        slot()
+        for h in range(2):
+            ts(f("KAP", BLK * h, BLK * h + BLK), f("YC"), f("IX", 2 * j + h, 2 * j + h + 1), OP.is_gt)
+        for h in range(2):
+            at = SEL * j + BLK * h
+            scan(f("RS", at, at + BLK), f("KAP", BLK * h, BLK * h + BLK), f("DM", BLK * h, BLK * h + BLK), 0.0, OP.mult, OP.add)
+
+    def key(j, io):
+        a = 76 * io + 38 * j
+        tt(f("KEY", a, a + 38), f("CC", a, a + 38), f("RS", SEL * j + 16, SEL * j + SEL, 17), OP.add if io else OP.subtract)
+
+    def member_row(j, h):
+        at = SEL * j + BLK * h
+        return f("RS", at + 16, at + 289, 17)
+
+    nxt = T.cores[(rank + 1) % len(T.cores)]
+    rid, pid, _ = topo.addr(nxt)
+    mask = sum(1 << e for e in topo.engines(core, nxt)[:8])
+    engines = 8
+
+    def send(t):
+        q, s = f("SQ%d" % t, 0, 64, cast=dt.uint8), f("SS%d" % t, 0, 64)
+        before("p", q[1] + s[1], [])
+        g.remote_dma(T["LQ%d" % t][:, 0:64].bitcast(dt.uint8), q[0], T.sem["arr%d" % t], T.sem["left"], pid, rid, mask)
+        g.remote_dma(T["LS%d" % t][:, 0:64], s[0], T.sem["arr%d" % t], T.sem["left"], pid, rid, mask)
+        after("in%d" % t, [], [("LQ%d" % t, 0, 64, 1), ("LS%d" % t, 0, 64, 1)], "arr%d" % t, 2 * engines)
+        count["arr%d" % t] = 2 * engines
+        count["left"] = count.get("left", 0) + 2 * engines
+
+    def clean(j):
+        for h in range(2):
+            act(f("CLN", 34 * j + ROW * h, 34 * j + ROW * h + ROW), member_row(j, h), AF.Identity, 1.0 / UNIT, 192.0)
+
+    def scaled(j, out):
+        act(out, f("CLN", 34 * j, 34 * j + 34), AF.Identity, UNIT, -192.0 * UNIT)
+
+    def place_marks(j):
+        for h in range(2):
+            act(f("FG", 34 * j + ROW * h, 34 * j + ROW * h + ROW), f("YC", 0, ROW), AF.Abs, -1.0, f("IX", 2 * j + h, 2 * j + h + 1))
+
+    def rows(sp, out, lo, h):
+        scan(f(out, lo + SQ3 * h, SQ3 * h + SQ3, 3), f("KEEP", 0, 289), f(sp, 289 * h, 289 * h + 289), 0.0, OP.mult, OP.add)
+
+    def columns(rv, d0):
+        act(f(d0, 2, 1776, 3), f(rv, 0, 34, ind=("OUTL", 0, 37)), AF.Copy, -0.5 / UNIT)
+
+    def column_signs(d0):
+        act(f(d0, 1, 1776, 3), f(d0, 2, 1776, 3), AF.Sign)
+
+    def steps(dst, d0, src, h):
+        lo, hi = SQ3 * h, SQ3 * h + SQ3
+        scan(f(dst, lo, hi), f(d0, lo, hi), f(src, lo, hi), 0.0, OP.mult, OP.add)
+
+    for t in range(R):
+        ft = "F%d" % t
+        if t:
+            scores(t, "F%d" % (t - 1))
+            for h in range(2):
+                steps("TA", "D0X", "TD", h)
+            unpack(t)
+        for h in range(2):
+            scan(f("Z", 272 * h, 272 * h + 272), f("FOLD", 0, 272), f("SG", 272 * h, 272 * h + 272), 0.0, OP.mult, OP.add)
+        choose(lambda h: f("Z", 272 * h + 15, 272 * h + 272, 16), 0, [lambda: differences(0), lambda: differences(1)] + ([outer_list] if t == 0 else []))
+        for h in range(2):
+            ts(f("GT", ROW * h, ROW * h + ROW), member_row(0, h), 0.0, OP.not_equal, -BIG, OP.mult)
+        clean(0)
+        scaled(0, f("RVF", 0, 34))
+        scaled(0, f("SPF", 0, 578, 17))
+        columns("RVF", "D0F")
+        column_signs("D0F")
+        if t == 0:
+            bases()
+        for h in range(2):
+            tt(f("S2", ROW * h, ROW * h + ROW), f("Z", 272 * h + 15, 272 * h + 272, 16), f("GT", ROW * h, ROW * h + ROW), OP.add)
+        if t == 0:
+            choose(lambda h: f("S2", ROW * h, ROW * h + ROW), 1, [priorities, lambda: member_columns(0), lambda: member_columns(4)])
+            key(0, 0)
+            key(0, 1)
+        else:
+            choose(lambda h: f("S2", ROW * h, ROW * h + ROW), 1, [lambda: key(0, 0), lambda: key(0, 1)])
+        rows("SPF", "TA", 0, 0)
+        tt(f("KC"), f("RS", 305, 2 * SEL, BLK), f("RS", 322, 2 * SEL, BLK), OP.add)
+        key(1, 0)
+        key(1, 1)
+        for b in range(4):
+            ts(f("KL", 4 * b, 4 * b + 4), f("KC"), float(b), OP.add)
+        act(f("KF"), f(ft, ind=("KL", 0, 16)))
+        for io in range(2):
+            scan(f("RK", 76 * io + 1, 76 * io + 77), f("KEY", 76 * io, 76 * io + 76), f("KEY", 76 * io, 76 * io + 76), -BIG, OP.max, OP.max)
+        scan(f("RK", 153, 229), f("KEY", 0, 76), f("RK", 0, 76), -BIG, OP.max, OP.min)
+        tt(f("DEC", 0, 8), f("RK", 19, 153, 19), f("ZK", 0, 8), OP.max)
+        scan(f("RK", 229, 305), f("KEY", 76, 152), f("RK", 76, 152), -BIG, OP.max, OP.min)
+        ts(f("DCM", 0, 8), f("DEC", 0, 8), 4095, OP.bitwise_and)
+        tt(f("DEC", 8, 16), f("RK", 171, 305, 19), f("ZK", 8, 16), OP.max)
+        for b in range(4):
+            ts(f("LL", 8 * b, 8 * b + 8), f("DCM", 0, 8), float(b), OP.add)
+            act(f("AB", 128 * b, 128 * b + 128), f(ft, ind=("LL", 8 * b, 8 * b + 8)))
+            if b == 1:
+                ts(f("DCM", 8, 16), f("DEC", 8, 16), 4095, OP.bitwise_and)
+        for b in range(4):
+            ts(f("LL", 32 + 8 * b, 40 + 8 * b), f("DCM", 8, 16), float(b), OP.add)
+        rows("SPF", "TA", 0, 1)
+        clean(1)
+        place_marks(0)
+        scaled(1, f("RVS", 0, 34))
+        scaled(1, f("SPS", 0, 578, 17))
+        place_marks(1)
+        act(f("SPA", 0, 578, 17), f("RVS", 0, 34), AF.Abs)
+        act(f("TA", 1, 1734, 3), f("TA", 0, 1734, 3), AF.Abs)
+        act(f("FS"), f("FG"), AF.Sign)
+        columns("RVS", "D0S")
+        column_signs("D0S")
+        for b in range(4):
+            tt(f("IO2", 128 * b, 128 * b + 128), f(ft, ind=("LL", 32 + 8 * b, 40 + 8 * b)), f("AB", 128 * b, 128 * b + 128), OP.add)
+
+        def larger(b):
+            tt(f("M2", 64 * b, 64 * b + 64), f("IO2", 128 * b, 128 * b + 64), f("IO2", 128 * b + 64, 128 * b + 128), OP.max)
+
+        def half(a):
+            ts(f("MH", 128 * a, 128 * a + 128), f("M2", 128 * a, 128 * a + 128), 0.5, OP.mult)
+
+        def less(b):
+            tt(f("YT", b, 256, 4), f("MH", 64 * b, 64 * b + 64), f("KF", 64 * b, 64 * b + 64), OP.subtract)
+
+        for fn, b in ((larger, 0), (larger, 1), (larger, 2), (half, 0), (larger, 3), (less, 0), (half, 1), (less, 1), (less, 2), (less, 3)):
+            fn(b)
+        quant("SQ%d" % t, "SS%d" % t, 0, 128, f("YT"))
+        send(t)
+        if t == 0:
+            for i in range(R):
+                dma("y", f("LQ%d" % i, 64, 128, cast=dt.uint8), f("SQ0", 64, 128, cast=dt.uint8))
+                dma("y", f("LS%d" % i, 64, 128), f("SS0", 64, 128))
+        for h in range(2):
+            steps("TB", "D0F", "TA", h)
+        tt(f("FH"), f("FS", 0, 34), f("FS", 34, 68), OP.add)
+        act(f("FV", 0, 34), f("FH"), AF.Identity, 2.0, -3.0)
+        act(f("SPX", 0, 578, 17), f("FH"), AF.Identity, 2.0, -3.0)
+        act(f("D0X", 1, 1776, 3), f("FV", 0, 34, ind=("OUTL", 0, 37)))
+        act(f("YW"), f("YT", 0, 256), AF.Copy, 32.0)
+        for h in range(2):
+            rows("SPS", "TB", 0, h)
+        for h in range(2):
+            rows("SPA", "TB", 1, h)
+        for h in range(2):
+            steps("TC", "D0S", "TB", h)
+        rows("SPX", "D0X", 2, 0)
+        for h in range(2):
+            ts(f("TD", SQ3 * h, SQ3 * h + SQ3, 3), f("TC", SQ3 * h + 2, SQ3 * h + SQ3, 3), 3.0 * UNIT, OP.min, -3.0 * UNIT, OP.max)
+        if t == 1:
+            output_list()
+        if t == R - 1:
+            rows("SPX", "D0X", 2, 1)
+            quant("VQ", "VS", 0, 128, f("VT"))
+            for h in range(2):
+                steps("TA", "D0X", "TD", h)
+            act(f("OAO"), f("TA", ind=("OL", 0, 32)), AF.Copy, -1.0 / UNIT)
+            dma("y", (T.oa[:, :], []), f("OAO"))
+        for b in range(4):
+            mm(f("PS", 1024 + 512 * b, 1152 + 512 * b), f("WQ", 128 * b, 128 * b + 128), f("WS", 128 * b, 128 * b + 128), f("LQ%d" % t), f("LS%d" % t))
+        for b in range(4):
+            tt(f("V32", 64 * b, 64 * b + 64), f("PS", 1024 + 512 * b, 1088 + 512 * b), f("YW", b, 256, 4), OP.add)
+        ts(f("VV"), f("V32"), 0.03125, OP.mult)
+        if t < R - 1:
+            rows("SPX", "D0X", 2, 1)
+        cp(f(ft, ind=("KL", 0, 16)), f("VV"))
+
+    for a in range(2):
+        lo, hi = 256 * a, 256 * a + 256
+        quant("XQ3", "XS3", lo, hi, f("F2", 1024 * a, 1024 * a + 1024))
+        mm(f("PS", 512 * a, 512 * a + 256), f("VQ"), f("VS"), f("XQ3", lo, hi), f("XS3", lo, hi))
+        dma("y", (T.oc[:, 4 * lo:4 * hi], []), f("XQ3", lo, hi, cast=dt.uint8))
+    act(f("YO", 0, 256), f("PS", 0, 256))
+    dma("s", (T.y[:, 0:256], []), f("YO", 0, 256))
+    cp(f("YO", 256, 512), f("PS", 512, 768))
+    dma("y", (T.y[:, 256:512], []), f("YO", 256, 512))
+    for k in range(4):
+        dma("s" if k % 2 else "y", (T.osc[4 * k:4 * k + 4, :], []), (T.XS3[32 * k:32 * k + 4, 0:512], [("XS3", 0, 512, 1)]))
+    for sem in count:
+        if sem != "dma":
+            wait("p", sem, count[sem])

@@ -1,52 +1,58 @@
-from concourse.bass import DstId, RemoteDMATransfer
 from concourse.mybir import dt, AluOpType, AxisListType, ActivationFunctionType
 
 OP = AluOpType
 AF = ActivationFunctionType
 R = 3
 W = 2176
-ROW, BLK = 17, 323
-SEL = 2 * BLK
-SQ3 = 867
-UNIT = 131072.0
+U = 131072.0
+MARK = 0.125
 BIG = 1.0e29
+KS = 66
 
 CODES, PLANE, BF, F32, I32, U16 = "float8_e4m3fn_x4", "uint8", "bfloat16", "float32", "int32", "uint16"
-SCRATCH = {"PS": ("psum", [128, 3072], F32)}
+SCRATCH = {"PS": ("psum", [128, 4096], F32)}
 for _n, _w, _d in (
-    ("XT", 2048, BF), ("UT", 512, BF), ("VT", 512, BF), ("ET", 528, BF),
+    ("XT", 2048, BF), ("UT", 512, BF), ("VT", 512, BF), ("ET", 528, BF), ("ONE", 528, BF),
     ("UQ", 128, CODES), ("US", 128, PLANE), ("UQR", 128, CODES), ("USR", 128, PLANE), ("VQ", 128, CODES), ("VS", 128, PLANE),
     ("WQ", 512, CODES), ("WS", 512, PLANE), ("EQ", 512, CODES), ("ES", 512, PLANE),
-    ("NDI", 32, I32), ("NDX", 32, I32), ("NDF", 32, F32), ("ARI", 512, I32), ("IA", 360, I32), ("FA", 400, F32),
-    ("ONE", 592, BF), ("KI", 512, F32), ("OWN", 512, F32),
-    ("L32", 32, U16), ("UL", 8, U16), ("SL", 36, U16), ("AL", 38, U16), ("OUTL", 38, U16), ("OL", 32, U16),
-    ("N4", 32, F32), ("HL", 80, F32),
-    ("CM", 512, F32), ("PW", 528, F32), ("FOLD", 544, BF), ("YC", 323, BF), ("KEEP", 578, BF), ("RS0", 34, F32), ("RST", 34, F32),
-    ("SEG", 152, F32), ("PRI", 152, F32), ("CC", 152, F32), ("ZK", 16, F32), ("ARB", 528, BF),
-    ("SG", 544, F32), ("Z", 544, F32), ("RX", 34, F32), ("TT", 34, F32), ("IX", 4, F32), ("KAP", SEL, BF), ("DM", SEL, BF),
-    ("RS", 2 * SEL, BF), ("GT", 34, F32), ("S2", 34, F32), ("KEY", 152, F32), ("RK", 308, F32),
-    ("DEC", 16, I32), ("DCM", 16, I32), ("LL", 64, U16), ("KC", 4, F32), ("KL", 16, U16),
-    ("KF", 256, BF), ("AB", 512, BF), ("IO2", 512, BF), ("M2", 256, BF), ("MH", 256, BF), ("YT", 512, BF), ("YW", 256, BF),
-    ("V32", 256, BF), ("VV", 256, BF), ("CLN", 68, BF), ("RVF", 48, BF), ("RVS", 48, BF), ("FV", 48, BF), ("FG", 68, BF),
-    ("FS", 68, BF), ("FH", 34, BF), ("SPF", 578, BF), ("SPS", 578, BF), ("SPA", 578, BF), ("SPX", 578, BF),
-    ("D0F", 1776, BF), ("D0S", 1776, BF), ("D0X", 1776, BF), ("TA", 1784, BF), ("TB", 1744, BF), ("TC", 1744, BF), ("TD", 1744, BF),
+    ("NDI", 32, I32), ("ARI", 512, I32), ("ARB", 512, BF), ("IA", 160, I32), ("FA", 1280, F32), ("SC", 32, F32),
+    ("KI", 256, BF), ("OWN", 512, BF), ("CM", 512, BF), ("FOLD", 256, BF), ("KEEP", 256, BF),
+    ("UL", 8, U16), ("SL", 32, U16), ("SM", 32, U16), ("CIRC", 16, U16), ("COLG", 16, U16), ("EXP", 34, U16), ("OUT", 32, U16),
+    ("PW", 512, F32), ("SG", 512, F32), ("Z", 528, F32), ("ZW", 64, F32), ("RX", 104, F32), ("FL", 104, F32), ("SE", 104, F32), ("SK", 104, F32),
+    ("L4", 8, U16), ("GM", 64, BF), ("GMT", 64, BF), ("S2", 64, F32), ("TAB", 1120, BF), ("EX", 528, BF),
+    ("GK0", 128, F32), ("GK1", 128, F32), ("KY0", 128, F32), ("KY1", 128, F32), ("RK0", 400, F32), ("RK1", 400, F32),
+    ("DI", 96, I32), ("DM", 96, I32), ("LL", 96, U16), ("KL", 16, U16),
+    ("AB", 512, BF), ("D0Y", 768, BF), ("D1Y", 768, BF), ("YS", 768, BF), ("YT", 512, BF), ("YW", 256, BF), ("V32", 256, BF), ("VV", 256, BF),
+    ("XG", 128, BF), ("X2", 128, BF), ("DD", 128, BF), ("SN", 64, BF), ("SP0", 256, BF), ("SP1", 256, BF), ("SPX", 256, BF),
+    ("D0F", 768, BF), ("D0S", 768, BF), ("D0X", 768, BF), ("TA", 1040, BF), ("TB", 768, BF), ("TC", 768, BF), ("TD", 768, BF),
     ("OAO", 512, F32), ("YO", 512, F32),
 ) + tuple(("F%d" % t, W, BF) for t in range(R)) + tuple((n + "%d" % t, 128, d) for t in range(R) for n, d in (("SQ", CODES), ("SS", PLANE), ("LQ", CODES), ("LS", PLANE))) \
   + tuple((n + "%d" % t, 512, d) for t in range(R + 1) for n, d in (("XQ", CODES), ("XS", PLANE))):
     SCRATCH[_n] = ("sbuf", [128, _w], _d)
 
-SEMAPHORES = ["cv", "cs", "ct", "cp", "left"] + ["arr%d" % t for t in range(R)] + ["dm%d" % i for i in range(48)]
+SEMAPHORES = ["cv", "cs", "ct", "cp", "left"] + ["arr%d" % t for t in range(R)] + ["dm%d" % i for i in range(32)]
 COUNTER = {"v": "cv", "s": "cs", "t": "ct", "p": "cp"}
-PART = {n: ("IA", a, w) for n, a, w in (("PI", 0, 1), ("PMI", 8, 1), ("ULI", 16, 8), ("EI", 24, 38), ("EE", 64, 38), ("EM", 104, 38), ("QD", 144, 38),
-                                       ("OLI", 184, 32), ("OLX", 216, 32), ("NI", 248, 32), ("NHI", 280, 32), ("NLO", 312, 32))}
-PART.update({n: ("FA", a, w) for n, a, w in (("PM", 0, 1), ("H17", 8, 38), ("H256", 48, 38), ("YE", 88, 38), ("XE", 128, 38), ("T1", 168, 38),
-                                            ("T2", 208, 38), ("T3", 248, 38), ("T4", 288, 38), ("T5", 328, 38))})
+PART = {}
+for _b, _names in (
+    ("IA", (("PI", 8), ("BITS", 8), ("DDI", 32), ("DI4", 32), ("JI", 16), ("JJ", 16))),
+    ("FA", (("N", 72), ("E64", 64), ("K32", 32), ("DU", 64), ("HE", 8), ("W1", 32), ("BP", 48), ("ISO", 64), ("NIS", 64), ("DUM", 64), ("CB", 128), ("CC", 128),
+            ("NDD", 64), ("NDM", 64), ("NWI", 64), ("NW", 64), ("N4", 32), ("T1", 40), ("T2", 40), ("T3", 40), ("T4", 40), ("T5", 40))),
+    ("SC", tuple((n, 1) for n in ("pm", "e", "p31", "qh", "ql", "h1", "a1", "n1", "A", "B", "e16", "kb0", "kb1", "sO", "sI", "pm16", "sb", "s1", "qh16", "t66",
+                                  "dl", "kl", "zb"))),
+    ("SM", (("SPG", 2), ("DL", 4), ("NDL", 4), ("ZWL", 4), ("KLL", 2))),
+):
+    _a = 0
+    for _n, _w in _names:
+        PART[_n] = (_b, _a, _w)
+        _a += _w
+SCRATCH["KT"] = ("sbuf", [128, 208], F32)
+CYC = 0.00104
+WAKE = 0.11
 
 
-def make_tracker(g, T):
+def make_plan(g, T):
     eng = {"v": g.vector, "s": g.scalar, "t": g.tensor, "p": g, "y": g.sync}
-    count = {}
-    known = {q: {} for q in eng}
+    ops = []
     hist = {}
 
     def view(name, lo=0, hi=None, step=1, ind=None, cast=None):
@@ -57,454 +63,465 @@ def make_tracker(g, T):
         hi = int(t.shape[1]) if hi is None else hi
         ap = t[:, lo:hi:step] if step != 1 else t[:, lo:hi]
         deps = [(name, lo, hi, step)]
+        n = (hi - lo + step - 1) // step
         if cast is not None:
             ap = ap.bitcast(cast)
         if ind is not None:
-            ap = ap.indirect(T[ind[0]][:, ind[1]:ind[2]])
-            deps.append((ind[0], ind[1], ind[2], 1))
-        return ap, deps
-
-    def wait(q, sem, val):
-        if known[q].get(sem, 0) < val:
-            known[q][sem] = val
-            eng[q].wait_ge(T.sem[sem], val)
-
-    def before(q, reads, writes):
-        need = {}
-        for acc, wr in ((reads, False), (writes, True)):
-            for name, lo, hi, st in acc:
-                for (a, b, w, sem, val, oq, s2) in hist.get(name, []):
-                    if a < hi and lo < b and (w or wr) and (st != s2 or (lo - a) % st == 0):
-                        need[sem] = max(need.get(sem, 0), val)
-        for sem in need:
-            wait(q, sem, need[sem])
-
-    def after(q, reads, writes, sem, val):
-        def covered(h, lo, hi, st):
-            return lo <= h[0] and h[1] <= hi and (st == 1 or st == h[6] and (lo - h[0]) % st == 0)
-        for name, lo, hi, st in writes:
-            hist[name] = [h for h in hist.get(name, []) if not covered(h, lo, hi, st)] + [(lo, hi, True, sem, val, q, st)]
-        for name, lo, hi, st in reads:
-            hist[name] = [h for h in hist.get(name, []) if h[2] or h[5] != q or not covered(h, lo, hi, st)] + [(lo, hi, False, sem, val, q, st)]
+            o = view(*ind)
+            ap = ap.indirect(o[0])
+            deps.append(o[1][0])
+            n = -16 * o[2]
+        return ap, deps, n, SCRATCH[name][2] in (BF, U16), name == "PS"
 
     def bank(d):
         return (d[0], d[1] // 512 * 512, (d[2] + 511) // 512 * 512, 1) if d[0] == "PS" else d
 
-    def call(q, fn, outs, ins):
+    def note(q, fn, outs, ins, dur, lat=0.0, kind="call"):
         reads = [d for v in ins for d in v[1] if d[0] != "PS"] + [d for v in outs for d in v[1][1:]]
-        writes = [bank(v[1][0]) for v in outs] + [bank(d) for v in ins for d in v[1] if d[0] == "PS"]
-        before(q, reads, writes)
-        sem = COUNTER[q]
-        count[sem] = count.get(sem, 0) + 1
-        fn(eng[q]).then_inc(T.sem[sem], 1)
-        after(q, reads, writes, sem, count[sem])
+        writes = [bank(v[1][0]) for v in outs if v[1]] + [bank(d) for v in ins for d in v[1] if d[0] == "PS"]
+        me = len(ops)
+        need = set()
+        for acc, wr in ((reads, False), (writes, True)):
+            for name, lo, hi, st in acc:
+                for (a, b, s2, w, k) in hist.get(name, []):
+                    if a < hi and lo < b and (w or wr) and (st != s2 or (lo - a) % st == 0):
+                        need.add(k)
+        for name, lo, hi, st in writes:
+            hist[name] = [h for h in hist.get(name, []) if not (lo <= h[0] and h[1] <= hi and (st == 1 or st == h[2] and (lo - h[0]) % st == 0))] + [(lo, hi, st, True, me)]
+        for name, lo, hi, st in reads:
+            hist.setdefault(name, []).append((lo, hi, st, False, me))
+        ops.append({"q": q, "fn": fn, "need": need, "dur": dur, "lat": lat, "kind": kind})
 
-    def dma(q, out, in_):
-        before(q, in_[1], out[1])
-        n = count.get("dma", 0)
-        count["dma"] = n + 1
-        eng[q].dma_start(out[0], in_[0]).then_inc(T.sem["dm%d" % n], 16)
-        after("dma%d" % n, in_[1], out[1], "dm%d" % n, 16)
-        count["dm%d" % n] = 16
-        return "dm%d" % n
+    def cost(q, out, ins, per):
+        if out[2] < 0:
+            return 0.05 - out[2] * 0.0032
+        for v in ins:
+            if v[2] < 0:
+                return 0.06 - v[2] * 0.0013
+        return max(64, max(v[2] for v in [out] + ins) * per) * CYC
 
-    return view, wait, before, after, call, dma, count
+    def order():
+        n = len(ops)
+        tail = [0.0] * n
+        users = [[] for _ in ops]
+        for i, o in enumerate(ops):
+            for k in o["need"]:
+                users[k].append(i)
+        for i in range(n - 1, -1, -1):
+            tail[i] = ops[i]["dur"] + ops[i]["lat"] + max([tail[u] + WAKE for u in users[i]] + [0.0])
+        free = {q: 0.0 for q in eng}
+        done = [None] * n
+        left = [len(o["need"]) for o in ops]
+        ready = [i for i in range(n) if not left[i]]
+        seq = []
+        while ready:
+            start = {i: max([free[ops[i]["q"]]] + [done[k] + WAKE for k in ops[i]["need"]]) for i in ready}
+            first = min(ready, key=lambda i: (start[i], -tail[i]))
+            q, t0 = ops[first]["q"], start[first]
+            mine = [i for i in ready if ops[i]["q"] == q]
+            now = max((i for i in mine if start[i] <= t0 + 0.01), key=lambda i: tail[i])
+            soon = [i for i in mine if tail[i] > tail[now] + ops[now]["dur"] and 2 * (start[i] - t0) < ops[now]["dur"]]
+            if soon:
+                now = max(soon, key=lambda i: tail[i])
+            free[q] = start[now] + ops[now]["dur"]
+            done[now] = free[q] + ops[now]["lat"]
+            ready.remove(now)
+            seq.append(now)
+            for u in users[now]:
+                left[u] -= 1
+                if not left[u]:
+                    ready.append(u)
+        return seq
+
+    def issue():
+        count = {}
+        known = {q: {} for q in eng}
+        mark = {}
+
+        def wait(q, sem, val):
+            if known[q].get(sem, 0) < val:
+                known[q][sem] = val
+                eng[q].wait_ge(T.sem[sem], val)
+
+        ndma = 0
+        for i in order():
+            o = ops[i]
+            q = o["q"]
+            need = {}
+            for k in o["need"]:
+                sem, val = mark[k]
+                need[sem] = max(need.get(sem, 0), val)
+            for sem in need:
+                wait(q, sem, need[sem])
+            if o["kind"] == "call":
+                sem = COUNTER[q]
+                count[sem] = count.get(sem, 0) + 1
+                o["fn"](eng[q]).then_inc(T.sem[sem], 1)
+            elif o["kind"] == "dma":
+                sem = "dm%d" % ndma
+                ndma += 1
+                count[sem] = 16
+                o["fn"](eng[q]).then_inc(T.sem[sem], 16)
+            else:
+                sem, n = o["fn"](eng[q])
+                count[sem] = n
+                count["left"] = count.get("left", 0) + n
+            mark[i] = (sem, count[sem])
+        for sem in count:
+            wait("p", sem, count[sem])
+
+    return view, note, cost, issue
 
 
 def rank_program(g, core, T, topo):
     rank = T.rank_of(core)
     if rank is None:
         return
-    f, wait, before, after, call, dma, count = make_tracker(g, T)
+    f, note, cost, issue = make_plan(g, T)
+
+    def rate(*vs):
+        return 0.5 if all(v[3] for v in vs) else 1.0
 
     def tt(out, a, b, op):
-        call("v", lambda e: e.tensor_tensor(out[0], a[0], b[0], op), [out], [a, b])
+        note("v", lambda e: e.tensor_tensor(out[0], a[0], b[0], op), [out], [a, b], cost("v", out, [a, b], 1.0 if a[4] or b[4] else 2.0))
 
     def ts(out, a, s1, op0, s2=None, op1=None):
         ins = [a] + [s for s in (s1, s2) if isinstance(s, tuple)]
         x1 = s1[0] if isinstance(s1, tuple) else s1
         x2 = s2[0] if isinstance(s2, tuple) else s2
+        c = cost("v", out, [a], rate(out, a))
         if op1 is None:
-            call("v", lambda e: e.tensor_scalar(out[0], a[0], x1, None, op0), [out], ins)
+            note("v", lambda e: e.tensor_scalar(out[0], a[0], x1, None, op0), [out], ins, c)
         else:
-            call("v", lambda e: e.tensor_scalar(out[0], a[0], x1, x2, op0, op1), [out], ins)
+            note("v", lambda e: e.tensor_scalar(out[0], a[0], x1, x2, op0, op1), [out], ins, c)
 
     def cp(out, a):
-        call("v", lambda e: e.tensor_copy(out[0], a[0]), [out], [a])
+        note("v", lambda e: e.tensor_copy(out[0], a[0]), [out], [a], cost("v", out, [a], rate(out, a)))
 
     def fill(out, c):
-        call("v", lambda e: e.memset(out[0], c), [out], [])
+        note("v", lambda e: e.memset(out[0], c), [out], [], cost("v", out, [], rate(out)))
 
     def scan(out, d0, d1, init, op0, op1):
-        call("v", lambda e: e.tensor_tensor_scan(out[0], d0[0], d1[0], init, op0, op1), [out], [d0, d1])
+        note("v", lambda e: e.tensor_tensor_scan(out[0], d0[0], d1[0], init, op0, op1), [out], [d0, d1], cost("v", out, [d0, d1], rate(out, d0, d1)))
 
-    def total(out, a):
-        call("v", lambda e: e.tensor_reduce(out[0], a[0], AxisListType.X, OP.add), [out], [a])
+    def turn(out, a):
+        note("v", lambda e: e.transpose(out[0], a[0]), [out], [a], cost("v", out, [a], rate(out, a)))
 
     def quant(qn, sn, lo, hi, a):
         q, s = f(qn, lo, hi), f(sn, lo, hi)
-        call("v", lambda e: e.quantize_mx(q[0], s[0], a[0]), [q, s], [a])
+        note("v", lambda e: e.quantize_mx(q[0], s[0], a[0]), [q, s], [a], 0.015 + 0.000275 * a[2])
 
     def act(out, a, func=AF.Copy, scale=1.0, bias=None):
-        if bias is None:
-            call("s", lambda e: e.activation(out[0], a[0], func, scale=scale), [out], [a])
-        elif isinstance(bias, tuple):
-            call("s", lambda e: e.activation(out[0], a[0], func, bias=bias[0], scale=scale), [out], [a, bias])
+        ins = [a] + [s for s in (scale, bias) if isinstance(s, tuple)]
+        sc = scale[0] if isinstance(scale, tuple) else scale
+        c = cost("s", out, [a], 1.0)
+        if bias is None and not isinstance(scale, tuple) and scale == 1.0:
+            note("s", lambda e: e.activation(out[0], a[0], func), [out], ins, c)
+        elif bias is None:
+            note("s", lambda e: e.activation(out[0], a[0], func, scale=sc), [out], ins, c)
         else:
-            call("s", lambda e: e.activation(out[0], a[0], func, bias=bias, scale=scale), [out], [a])
+            bi = bias[0] if isinstance(bias, tuple) else bias
+            note("s", lambda e: e.activation(out[0], a[0], func, bias=bi, scale=sc), [out], ins, c)
+
+    def aff(out, a, scale, bias):
+        act(out, a, AF.Identity, scale, bias)
 
     def mm(out, l, ls, r, rs):
-        call("t", lambda e: e.matmul_mx(out[0], l[0], ls[0], r[0], rs[0], True, True), [out], [l, ls, r, rs])
+        note("t", lambda e: e.matmul_mx(out[0], l[0], ls[0], r[0], rs[0], True, True), [out], [l, ls, r, rs], (r[2] + 16) * 0.0005)
 
     def iota(out, pattern, base=0, cm=0, small=True):
         if small:
-            call("p", lambda e: e.iota(out[0], pattern, base, cm, allow_small_or_imprecise_dtypes=True), [out], [])
+            note("p", lambda e: e.iota(out[0], pattern, base, cm, allow_small_or_imprecise_dtypes=True), [out], [], 0.16 + 2 * CYC * out[2])
         else:
-            call("p", lambda e: e.iota(out[0], pattern, base, cm), [out], [])
+            note("p", lambda e: e.iota(out[0], pattern, base, cm), [out], [], 0.16 + 2 * CYC * out[2])
 
-    def affine(out, a, pattern, op, fillv, base, cm):
-        call("p", lambda e: e.affine_select(out[0], a[0], pattern, op, fillv, base, cm), [out], [a])
+    def zero(out):
+        iota(out, [[0, out[2]]])
 
-    dma("y", f("NDI"), (T.nd[:, :], []))
-    dma("s", f("UT"), (T.u[:, :], []))
-    dma("y", f("XT", 0, 1024), (T.x[:, 0:1024], []))
-    dma("s", f("XT", 1024, 2048), (T.x[:, 1024:2048], []))
-    blocks = []
-    for i in range(16):
-        a, p, h = 32 * (i // 4), 16 * (i % 4 // 2), 16 * (i % 2)
-        blocks.append(dma("y" if i % 2 else "s", (T.NDX[a + p:a + p + 16, h:h + 16], []), (T.nd[a + h:a + h + 16, p:p + 16], [])))
-    dma("y", f("ARI"), (T.ar[:, :], []))
-    dma("s", f("WQ", cast=dt.uint8), (T.wc[:, :], []))
-    dma("y", f("WS"), (T.ws[:, :], []))
-    dma("s", f("VT"), (T.v[:, :], []))
+    def dma(q, out, in_, lat=2.2):
+        note(q, lambda e: e.dma_start(out[0], in_[0]), [out], [in_], 0.05, lat, "dma")
 
+    def hbm(ap):
+        return (ap, [])
+
+    dma("y", f("NDI"), hbm(T.nd[:, :]))
+    dma("s", f("UT"), hbm(T.u[:, :]))
+    dma("y", f("XT", 0, 1024), hbm(T.x[:, 0:1024]), 3.0)
+    dma("s", f("XT", 1024, 2048), hbm(T.x[:, 1024:2048]), 3.0)
+    dma("y", f("ARI"), hbm(T.ar[:, :]), 3.5)
+    dma("s", f("WQ", cast=dt.uint8), hbm(T.wc[:, :]), 4.0)
+    dma("y", f("WS"), hbm(T.ws[:, :]), 4.0)
+    dma("s", f("VT"), hbm(T.v[:, :]), 4.0)
+
+    iota(f("PI", 0, 1), [[0, 1]], 0, 1, small=False)
+    iota(f("N"), [[1, 72]])
+    iota(f("E64"), [[0, 2], [1, 2], [0, 16]])
+    iota(f("HE", 0, 4), [[1, 2], [0, 2]])
+    iota(f("KI"), [[0, 16], [1, 16]])
+    iota(f("K32"), [[0, 2], [1, 16]])
+    iota(f("DU"), [[64, 2], [0, 2], [4, 16]], 2048)
+    iota(f("W1"), [[384, 2], [24, 16]], -1)
+    iota(f("BP"), [[0, 6], [1, 4], [0, 2]])
     fill(f("ONE"), 1.0)
-    fill(f("RS0"), BIG)
-    iota(f("PI"), [[0, 1]], 0, 1, small=False)
-    iota(f("EI"), [[16, 38]], small=False)
-    iota(f("KI"), [[1, 16], [0, 32]])
-    iota(f("ULI"), [[16, 8]], small=False)
-    affine(f("ET"), f("ONE", 0, 528), [[-1, 528]], OP.is_equal, 0.0, 3, 4)
-    affine(f("FOLD"), f("ONE", 0, 544), [[0, 34], [1, 16]], OP.not_equal, 0.0, 0, 0)
-    affine(f("RST"), f("RS0"), [[0, 2], [1, 17]], OP.not_equal, -BIG, 0, 0)
-    iota(f("TA", 1734, 1784), [[0, 50]])
-    iota(f("YC"), [[0, 19], [1, 17]])
-    iota(f("SEG"), [[1, 8], [0, 19]], 1)
-    iota(f("PRI"), [[0, 8], [-4096, 19]], 65536)
-    iota(f("F0", 2048, W), [[0, 128]])
-    affine(f("KEEP"), f("ONE", 0, 578), [[0, 34], [1, 17]], OP.not_equal, 0.0, 0, 0)
-    iota(f("YT", 256, 512), [[0, 256]])
-    for t in range(1, R):
-        iota(f("F%d" % t, 2048, W), [[0, 128]])
-    iota(f("OLI"), [[867, 2], [51, 16]], 56, small=False)
-    iota(f("OLX"), [[0, 2], [1, 16]], small=False)
-    for n in ("SPF", "SPS", "SPA", "SPX"):
-        act(f(n), f("ONE", 0, 578), AF.Copy, 0.0)
-    for n in ("D0F", "D0S", "D0X"):
-        act(f(n, 0, 1776, 3), f("ONE"), AF.Copy, 0.0)
-    for j in (1, 2):
-        act(f("TD", j, 1734, 3), f("ONE", 0, 578), AF.Copy, 0.0)
+    et, one = f("ET"), f("ONE")
+    note("p", lambda e: e.affine_select(et[0], one[0], [[-1, 528]], OP.is_equal, 0.0, 3, 4), [et], [one], 1.3)
+    for n, k in (("FOLD", 16), ("KEEP", 8)):
+        act(f(n), f("ONE", 0, 256))
+        fill(f(n, 0, 256, k), 0.0)
+    for t in range(R):
+        zero(f("F%d" % t, 2048, W))
+    zero(f("YT", 256, 512))
+    for a in (0, 544, 1088):
+        zero(f("TAB", a, a + 32))
+    for n in ("SP0", "SP1", "SPX"):
+        act(f(n), f("ONE", 0, 256), AF.Copy, 0.0)
+    for n, j in (("D0F", 0), ("D0S", 0), ("D0X", 0), ("TD", 1), ("TD", 2), ("TA", 0), ("TA", 1), ("D0Y", 0), ("D1Y", 1)):
+        act(f(n, j, 768, 3), f("ONE", 0, 256), AF.Copy, 0.0)
+    act(f("D1Y", 0, 768, 3), f("ONE", 0, 256), AF.Copy, -BIG)
+    fill(f("TA", 1024, 1040), MARK)
+    fill(f("Z", 512, 528), -BIG / 32)
+    fill(f("RX", 0, 34, 17), -2 * BIG)
+    fill(f("RX", 36, 102, 33), -2 * BIG)
+    for n in ("RK0", "RK1"):
+        zero(f(n))
+        fill(f(n, 0, 1), BIG)
+        fill(f(n, KS, KS + 1), -BIG)
 
-    ts(f("PMI"), f("PI"), 15, OP.bitwise_and)
-    cp(f("PM"), f("PMI"))
-    pm = f("PM")
-    ts(f("EE"), f("EI"), pm, OP.add)
-    ts(f("EM"), f("EE"), 3856.0, OP.mult)
-    ts(f("QD"), f("EM"), 16, OP.logical_shift_right)
-    ts(f("H17"), f("QD"), 17.0, OP.is_ge, 17.0, OP.mult)
-    ts(f("T1"), f("QD"), -17.0, OP.mult)
-    ts(f("H256"), f("QD"), 17.0, OP.is_ge, 256.0, OP.mult)
-    tt(f("XE"), f("QD"), f("H17"), OP.subtract)
-    tt(f("YE"), f("T1"), f("EE"), OP.add)
-    ts(f("OWN"), f("KI"), pm, OP.is_equal)
+    pi = f("PI", 0, 1)
+    for j, (sh, m) in enumerate(((0, 15), (4, 1), (0, 31), (3, 1), (0, 7), (0, 1), (1, 7), (1, 1))):
+        ts(f("BITS", j, j + 1), pi, sh, OP.logical_shift_right, m, OP.bitwise_and)
+    cp(f("SC", 0, 8), f("BITS"))
+    pm, e = f("pm"), f("e")
+    for n, src, sc, bi in (("A", "e", -4096.0, 4096.0), ("B", "e", 4096.0, 0.0), ("e16", "e", 16.0, 0.0), ("kb0", "p31", 1 / 4096.0, 32 / 4096.0),
+                           ("kb1", "p31", 1 / 4096.0, 576 / 4096.0), ("sO", "pm", -4096.0, 61440.0 - 67584.0), ("sI", "pm", 4096.0, 63488.0),
+                           ("pm16", "pm", 1.0, 16.0), ("sb", "pm", 8.0, 783.0), ("s1", "qh", 1.0, f("ql")), ("qh16", "qh", 16.0, 0.0),
+                           ("t66", "qh", float(KS), 32.0), ("dl", "h1", 32.0, f("t66")), ("kl", "n1", 47.0, 32.0), ("zb", "pm", 16.0, -497.0)):
+        aff(f(n), f(src), sc, bi)
+    ts(f("UL"), f("N", 0, 8), 16.0, OP.mult)
+    ts(f("NDL"), f("HE", 0, 4), 16.0, OP.mult, pm, OP.add)
+    ts(f("SPG"), f("N", 0, 64, 32), f("p31"), OP.add)
+    ts(f("DL", 0, 3), f("N", 0, 3), 2.0 * KS, OP.mult, f("dl"), OP.add)
+    ts(f("KLL", 0, 1), f("kl"), f("a1"), OP.add, f("h1"), OP.add)
+    ts(f("ISO"), f("E64"), e, OP.is_equal)
+    aff(f("NIS"), f("ISO"), -1.0, 1.0)
+    tt(f("DUM"), f("DU"), f("NIS"), OP.mult)
+    ts(f("OWN", 0, 256), f("KI"), pm, OP.is_equal)
+    act(f("OWN", 256, 512), f("OWN", 0, 256))
     for h in range(2):
-        cp(f("L32", h, 32, 2), f("NDI", 16 * h, 16 * h + 16))
-    ts(f("T1"), f("XE"), 0.0, OP.is_equal, 1000.0, OP.mult)
-    ts(f("T3"), f("YE"), 0.0, OP.is_equal, 1000.0, OP.mult)
-    cp(f("CM", ind=("L32", 0, 32)), f("OWN"))
-    ts(f("T2"), f("XE"), 16.0, OP.mult, -17.0, OP.add)
-    tt(f("T4"), f("XE"), f("T1"), OP.add)
-    tt(f("T5"), f("T1"), f("T3"), OP.add)
-    cp(f("UL"), f("ULI"))
-    tt(f("T1"), f("T2"), f("YE"), OP.add)
-    quant("UQ", "US", 0, 128, f("UT"))
-    tt(f("T3"), f("H256"), f("T5"), OP.add)
-    tt(f("T2"), f("T4"), f("YE"), OP.is_equal)
-    cp(f("UQR", cast=dt.uint32), f("UQ", cast=dt.uint32, ind=("UL", 0, 8)))
-    cp(f("USR"), f("US", ind=("UL", 0, 8)))
-    for s in blocks:
-        wait("v", s, 16)
-    ts(f("NDF"), f("NDX"), 4.0, OP.mult)
-    tt(f("T5"), f("T1"), f("T3"), OP.add)
-    ts(f("T4"), f("T2"), 520.0, OP.mult)
-    call("v", lambda e: e.transpose(T.N4[:, :], T.NDF[:, :]), [f("N4")], [f("NDF")])
-    fill(f("SL", 0, 36, 18), 512)
-    fill(f("SL", 17, 18), 512)
-    fill(f("SL", 35, 36), 512)
+        aff(f("CB", 32 * h, 32 * h + 32), f("ISO", 0, 32), f("sI"), (12 - 8 * h) * U - 63488.0)
+        aff(f("CB", 64 + 32 * h, 96 + 32 * h), f("ISO", 0, 32), f("sO"), (4 + 8 * h) * U + 67584.0)
+    aff(f("T1", 0, 4), f("HE", 0, 4), 256.0, f("zb"))
+    tt(f("T1", 4, 8), f("T1", 0, 4), f("ISO", 0, 64, 16), OP.mult)
+    ts(f("ZWL"), f("T1", 4, 8), 512.0, OP.add)
+    aff(f("KT", 0, 33), f("N", 0, 33), 32 / 4096.0, f("kb0"))
+    ts(f("T2", 0, 33), f("N", 0, 33), f("e16"), OP.subtract, -1.0, OP.max)
+    ts(f("T3", 0, 33), f("T2", 0, 33), 16.0, OP.min, 32 / 4096.0, OP.mult)
     for h in range(2):
-        ts(f("SL", 18 * h + 1, 18 * h + 17), f("N4", 16 * h, 16 * h + 16), 0.25, OP.mult)
-    fill(f("PW", 512, 528), -BIG / 32)
-
-    def scores(t, src):
-        for a in range(2):
-            quant("XQ%d" % t, "XS%d" % t, 256 * a, 256 * a + 256, f(src, 1024 * a, 1024 * a + 1024))
-            mm(f("PS", 512 * a, 512 * a + 256), f("UQR"), f("USR"), f("XQ%d" % t, 256 * a, 256 * a + 256), f("XS%d" % t, 256 * a, 256 * a + 256))
-        for a in range(2):
-            tt(f("PW", 256 * a, 256 * a + 256), f("PS", 512 * a, 512 * a + 256), f("CM", 256 * a, 256 * a + 256), OP.mult)
-        act(f("SG", 0, 272), f("PW", 0, 528, ind=("SL", 0, 17)))
-        act(f("SG", 272, 544), f("PW", 0, 528, ind=("SL", 18, 35)))
-
-    def unpack(t):
-        for b in range(4):
-            mm(f("PS", 1024 + 512 * b, 1536 + 512 * b), f("EQ", 128 * b, 128 * b + 128), f("ES", 128 * b, 128 * b + 128), f("XQ%d" % t), f("XS%d" % t))
-        for b in range(4):
-            act(f("F%d" % t, b, 2048, 4), f("PS", 1024 + 512 * b, 1536 + 512 * b))
-
-    def differences(h):
-        scan(f("DM", BLK * h + 1, BLK * h + 289), f("TA", SQ3 * h + 2, SQ3 * h + 864, 3), f("TA", SQ3 * h + 8, SQ3 * h + 870, 3), 0.0, OP.subtract, OP.subtract)
-
-    scores(0, "XT")
-
-    ts(f("T1"), f("T5"), 512.0, OP.min)
-    ts(f("ARB", 0, 512), f("ARI"), -UNIT, OP.mult)
-    fill(f("ARB", 512, 520), 0.0)
-    tt(f("T3"), f("T1"), f("T4"), OP.max)
-    fill(f("ARB", 520, 528), UNIT / 64)
-    cp(f("NI"), f("N4"))
-    cp(f("AL"), f("T3"))
-    act(f("TA", 2, 1778, 3), f("ARB", ind=("AL", 0, 37)))
-    fill(f("HL"), 0.0)
+        aff(f("KT", 36 + 33 * h, 69 + 33 * h), f("T3", 0, 33), 1.0, f("kb%d" % h))
+    act(f("KT", 104, 137), f("N", 0, 33), AF.Copy, 1 / 4096.0)
+    act(f("KT", 140, 206), f("N", 0, 66), AF.Copy, 1 / 4096.0)
+    ts(f("JI"), f("K32", 0, 32, 2), f("s1"), OP.add, 1.0, OP.add)
+    ts(f("JJ"), f("JI"), 15, OP.bitwise_and)
+    for h in range(2):
+        ts(f("COLG", 8 * h, 8 * h + 8), f("JJ", 8 * h, 8 * h + 8), f("e16"), OP.add, 32.0 * h, OP.add)
+    aff(f("T2", 0, 16), f("N", 0, 16), 32.0, f("qh16"))
+    tt(f("T2", 16, 32), f("T2", 0, 16), f("JJ"), OP.add)
+    cp(f("CIRC"), f("T2", 16, 32))
+    ts(f("DDI"), f("K32"), -1.0, OP.mult, f("pm16"), OP.add)
+    ts(f("DI4"), f("DDI"), 15, OP.bitwise_and)
+    d = f("DI4")
+    ts(f("T1", 0, 32), d, 3.0, OP.mult)
+    tt(f("T2", 0, 32), f("T1", 0, 32), f("W1"), OP.add)
+    for h in range(2):
+        ts(f("T3", 16 * h, 16 * h + 16), f("DI4", 16 * h, 16 * h + 16), -1.0, OP.mult, f("sb"), OP.add)
+    aff(f("T3", 16, 32), f("T3", 16, 32), 1.0, 128.0)
+    ts(f("T4", 0, 32), d, 8.0, OP.is_gt)
+    tt(f("T1", 0, 32), f("T3", 0, 32), f("T4", 0, 32), OP.mult)
+    ts(f("T5", 0, 32), d, 0.0, OP.is_equal, 1024.0, OP.mult)
+    tt(f("T3", 0, 32), f("T1", 0, 32), f("T5", 0, 32), OP.max)
+    tt(f("T4", 0, 32), f("T3", 0, 32), f("T2", 0, 32), OP.max)
+    cp(f("OUT"), f("T4", 0, 32))
+    fill(f("T1", 0, 34, 33), 1024.0)
+    for h in range(2):
+        act(f("T1", 1 + h, 33, 2), f("T4", 16 * h, 16 * h + 16))
+    tt(f("T2", 0, 33), f("T1", 0, 33), f("T1", 1, 34), OP.subtract)
+    act(f("T3", 0, 33), f("T2", 0, 33), AF.Copy, e)
+    tt(f("T5", 0, 33), f("T3", 0, 33), f("T1", 1, 34), OP.add)
+    cp(f("EXP", 0, 33), f("T5", 0, 33))
     for b in range(4):
         quant("EQ", "ES", 128 * b, 128 * b + 128, f("ET", 3 - b, 515 - b))
-    unpack(0)
-    ts(f("NHI"), f("NI"), 1920, OP.bitwise_and)
-    ts(f("NLO"), f("NI"), 127, OP.bitwise_and)
+
+    quant("UQ", "US", 0, 128, f("UT"))
+    cp(f("UQR", cast=dt.uint32), f("UQ", cast=dt.uint32, ind=("UL",)))
+    act(f("USR"), f("US", ind=("UL",)))
+    ts(f("NDD"), f("NDI", ind=("NDL",)), 4.0, OP.mult)
+    tt(f("NDM"), f("NDD"), f("ISO"), OP.mult)
+    tt(f("NWI"), f("NDM"), f("DUM"), OP.add)
+    turn(f("NW"), f("NWI"))
+    cp(f("N4"), f("NW", ind=("SPG",)))
+    ts(f("SL"), f("N4"), 0.25, OP.mult)
+    for io in range(2):
+        tt(f("CC", 64 * io, 64 * io + 64), f("CB", 64 * io, 64 * io + 64), f("NDM"), OP.add)
+    act(f("NDD", 0, 32), f("N4"), AF.Copy, 2.0 ** -24)
+    act(f("NWI"), f("NW"), AF.Copy, 2.0 ** -24)
     for h in range(2):
-        fill(f("HL", 36 * h, 36 * h + 1), 2048.0)
-        ts(f("HL", 36 * h + 18, 36 * h + 19), pm, 4.0, OP.mult, 64.0 * h, OP.add)
-    for h in range(2):
-        cp(f("HL", 36 * h + 1, 36 * h + 17), f("NHI", 16 * h, 16 * h + 16))
-        cp(f("HL", 36 * h + 19, 36 * h + 35), f("NLO", 16 * h, 16 * h + 16))
-    for h in range(2):
-        fill(f("DM", BLK * h, BLK * h + 1), 0.0)
-    for h in range(2):
-        for j in range(2):
-            tt(f("DM", BLK * h + 289 + 17 * j, BLK * h + 306 + 17 * j), f("HL", 36 * h + 18 * j, 36 * h + 18 * j + 17), f("HL", 36 * h + 18 * j + 1, 36 * h + 18 * j + 18), OP.subtract)
-
-    def outer_list():
-        tt(f("T2"), f("YE"), f("H17"), OP.add)
-        cp(f("OUTL"), f("T2"))
-
-    def bases():
-        ts(f("CC"), f("SEG"), 1048576.0, OP.mult)
-        for j in range(2):
-            ts(f("ZK", 8 * j, 8 * j + 8), f("SEG", 0, 152, 19), 1048576.0, OP.mult, 71680.0, OP.add)
-
-    def priorities():
-        tt(f("CC"), f("CC"), f("PRI"), OP.add)
-        fill(f("RK", 0, 1), -BIG)
-
-    def member_columns(lo):
-        for s in range(lo, lo + 4):
-            a = 19 * s + 1
-            tt(f("CC", a, a + 16), f("CC", a, a + 16), f("N4", 16 * (s % 2), 16 * (s % 2) + 16), OP.add)
-
-    def output_list():
-        ts(f("T1", 0, 1), pm, 3.0, OP.mult)
-        ts(f("QD", 0, 32), f("OLX"), pm, OP.is_equal, 1736.0, OP.mult)
-        ts(f("EM", 0, 32), f("OLI"), f("T1", 0, 1), OP.add)
-        tt(f("EE", 0, 32), f("EM", 0, 32), f("QD", 0, 32), OP.max)
-        cp(f("OL"), f("EE", 0, 32))
-
-    def choose(s, j, slots):
-        def slot():
-            if slots:
-                slots.pop(0)()
-        for h in range(2):
-            scan(f("RX", ROW * h, ROW * h + ROW), f("RST", 0, ROW), s(h), 0.0, OP.min, OP.max)
-        slot()
-        for h in range(2):
-            ts(f("TT", ROW * h, ROW * h + ROW), f("RX", ROW * h, ROW * h + ROW), f("RX", ROW * h + 16, ROW * h + 17), OP.is_lt)
-        slot()
-        for h in range(2):
-            total(f("IX", 2 * j + h, 2 * j + h + 1), f("TT", ROW * h, ROW * h + ROW))
-        slot()
-        for h in range(2):
-            ts(f("KAP", BLK * h, BLK * h + BLK), f("YC"), f("IX", 2 * j + h, 2 * j + h + 1), OP.is_gt)
-        for h in range(2):
-            at = SEL * j + BLK * h
-            scan(f("RS", at, at + BLK), f("KAP", BLK * h, BLK * h + BLK), f("DM", BLK * h, BLK * h + BLK), 0.0, OP.mult, OP.add)
-
-    def key(j, io):
-        a = 76 * io + 38 * j
-        tt(f("KEY", a, a + 38), f("CC", a, a + 38), f("RS", SEL * j + 16, SEL * j + SEL, 17), OP.add if io else OP.subtract)
-
-    def member_row(j, h):
-        at = SEL * j + BLK * h
-        return f("RS", at + 16, at + 289, 17)
+        a, b = f("KT", 104 + 17 * h, 120 + 17 * h), f("KT", 140 + 33 * h, 172 + 33 * h)
+        tt(a, a, f("NDD", 16 * h, 16 * h + 16), OP.add)
+        tt(b, b, f("NWI", 32 * h, 32 * h + 32), OP.add)
+    ts(f("ARB"), f("ARI"), U, OP.mult)
+    act(f("TA", 2, 768, 3), f("ARB", ind=("CIRC",)))
 
     nxt = T.cores[(rank + 1) % len(T.cores)]
     rid, pid, _ = topo.addr(nxt)
-    mask = sum(1 << e for e in topo.engines(core, nxt)[:8])
-    engines = 8
+    engines = topo.engines(core, nxt)[:8]
+    mask = sum(1 << k for k in engines)
 
     def send(t):
         q, s = f("SQ%d" % t, 0, 64, cast=dt.uint8), f("SS%d" % t, 0, 64)
-        before("p", q[1] + s[1], [])
-        g.remote_dma(T["LQ%d" % t][:, 0:64].bitcast(dt.uint8), q[0], T.sem["arr%d" % t], T.sem["left"], pid, rid, mask)
-        g.remote_dma(T["LS%d" % t][:, 0:64], s[0], T.sem["arr%d" % t], T.sem["left"], pid, rid, mask)
-        after("in%d" % t, [], [("LQ%d" % t, 0, 64, 1), ("LS%d" % t, 0, 64, 1)], "arr%d" % t, 2 * engines)
-        count["arr%d" % t] = 2 * engines
-        count["left"] = count.get("left", 0) + 2 * engines
+        lq, ls = f("LQ%d" % t, 0, 64, cast=dt.uint8), f("LS%d" % t, 0, 64)
 
-    def clean(j):
+        def go(e):
+            e.remote_dma(lq[0], q[0], T.sem["arr%d" % t], T.sem["left"], pid, rid, mask)
+            e.remote_dma(ls[0], s[0], T.sem["arr%d" % t], T.sem["left"], pid, rid, mask)
+            return "arr%d" % t, 2 * len(engines)
+        note("p", go, [lq, ls], [q, s], 0.6 if t else 2.6, 2.2, "send")
+
+    def table():
+        act(f("TA", 768, 1024), f("TA", 2, 768, 3), AF.Copy, -1.0)
+        act(f("EX"), f("TA", ind=("EXP", 0, 33)))
         for h in range(2):
-            act(f("CLN", 34 * j + ROW * h, 34 * j + ROW * h + ROW), member_row(j, h), AF.Identity, 1.0 / UNIT, 192.0)
+            turn(f("TAB", 32 + 544 * h, 544 + 544 * h), f("EX", 16 * h, 16 * h + 512))
 
-    def scaled(j, out):
-        act(out, f("CLN", 34 * j, 34 * j + 34), AF.Identity, UNIT, -192.0 * UNIT)
-
-    def place_marks(j):
+    def choose(j, src):
+        n, at = (16, 0) if j == 0 else (32, 36)
         for h in range(2):
-            act(f("FG", 34 * j + ROW * h, 34 * j + ROW * h + ROW), f("YC", 0, ROW), AF.Abs, -1.0, f("IX", 2 * j + h, 2 * j + h + 1))
+            a = at + (n + 1) * h + 1
+            scan(f("RX", a, a + n), src(h), src(h), -2 * BIG, OP.max, OP.max)
+        w = 2 * n + 1
+        tt(f("FL", at, at + w), f("RX", at + 1, at + w + 1), f("RX", at, at + w), OP.is_gt)
+        scan(f("SE", at, at + w), f("FL", at, at + w), f("KT", at, at + w), 0.0, OP.max, OP.min)
+        for k, s in enumerate("AB"):
+            ts(f("L4", 4 * j + k, 4 * j + 4, 2), f("SE", at + n - 1, at + w, n + 1), f(s), OP.mult)
+        scan(f("SK", at, at + w), f("FL", at, at + w), f("KT", 104 + at, 104 + at + w), 0.0, OP.max, OP.min)
+        act(f("RK%d" % j, 4 * KS + 32, 4 * KS + 65, 32), f("SK", at + n - 1, at + w, n + 1), AF.Copy, 2.0 ** 24)
 
-    def rows(sp, out, lo, h):
-        scan(f(out, lo + SQ3 * h, SQ3 * h + SQ3, 3), f("KEEP", 0, 289), f(sp, 289 * h, 289 * h + 289), 0.0, OP.mult, OP.add)
+    def slots(j, ft):
+        gk, ky, rk = "GK%d" % j, "KY%d" % j, "RK%d" % j
+        l4 = ("L4", 4 * j, 4 * j + 4)
+        for io in range(2):
+            tt(f(gk, 64 * io, 64 * io + 64), f("TAB", ind=l4), f("CC", 64 * io, 64 * io + 64), OP.add)
+        for io in range(2):
+            turn(f(ky, 64 * io, 64 * io + 64), f(gk, 64 * io, 64 * io + 64))
+        for io, a, b, big in ((0, OP.min, OP.max, BIG), (1, OP.max, OP.min, -BIG)):
+            k = f(ky, 64 * io, 64 * io + 64)
+            scan(f(rk, KS * io + 1, KS * io + 65), k, k, big, a, a)
+            scan(f(rk, KS * (io + 2) + 1, KS * (io + 2) + 65), k, f(rk, KS * io, KS * io + 64), big, a, b)
+        lo = 48 * j
+        tt(f("DI", lo, lo + 48), f(rk, ind=("DL", 0, 3)), f("BP"), OP.add)
+        ts(f("DM", lo, lo + 48), f("DI", lo, lo + 48), 4095, OP.bitwise_and)
+        cp(f("LL", lo, lo + 48), f("DM", lo, lo + 48))
+        y = 384 * j
+        for io in range(2):
+            ab = f("AB", 256 * j + 128 * io, 256 * j + 128 * io + 128)
+            act(ab, f(ft, ind=("LL", lo + 8 * io, lo + 8 * io + 8)))
+            tt(f("D0Y", y + 1 + io, y + 384, 3), f(ft, ind=("LL", lo + 16 + 8 * io, lo + 24 + 8 * io)), ab, OP.add)
+        act(f("D1Y", y + 2, y + 384, 3), f(ft, ind=("LL", lo + 32, lo + 40)), AF.Copy, -2.0)
+        scan(f("YS", y, y + 384), f("D0Y", y, y + 384), f("D1Y", y, y + 384), 0.0, OP.max, OP.add)
+        for b in range(4):
+            o, i = f("YT", 128 * j + b, 128 * j + 128, 4), f("YS", y + 96 * b + 2, y + 96 * b + 96, 3)
+            if j == 1 and b % 2:
+                ts(o, i, 0.5, OP.mult)
+            else:
+                act(o, i, AF.Copy, 0.5)
 
-    def columns(rv, d0):
-        act(f(d0, 2, 1776, 3), f(rv, 0, 34, ind=("OUTL", 0, 37)), AF.Copy, -0.5 / UNIT)
+    def operands(j, d0, d1):
+        x = f("X2", 64 * j, 64 * j + 64)
+        act(f("XG", 64 * j, 64 * j + 64), f("TAB", ind=("L4", 4 * j, 4 * j + 4)))
+        turn(x, f("XG", 64 * j, 64 * j + 64))
+        act(f("SP%d" % j, 0, 256, 8), f("X2", 64 * j, 64 * j + 64, ind=("SPG",)))
+        act(f(d0, 2, 768, 3), f("X2", 64 * j, 64 * j + 64, ind=("COLG",)), AF.Copy, 0.5 / U)
+        act(f(d0, 1, 768, 3), f(d0, 2, 768, 3), AF.Sign, -1.0)
+        scan(f(d1, 0, 768, 3), f("KEEP"), f("SP%d" % j), 0.0, OP.mult, OP.add)
+        act(f(d1, 1, 768, 3), f(d1, 0, 768, 3), AF.Abs)
 
-    def column_signs(d0):
-        act(f(d0, 1, 1776, 3), f(d0, 2, 1776, 3), AF.Sign)
-
-    def steps(dst, d0, src, h):
-        lo, hi = SQ3 * h, SQ3 * h + SQ3
-        scan(f(dst, lo, hi), f(d0, lo, hi), f(src, lo, hi), 0.0, OP.mult, OP.add)
+    def steps(dst, d0, src):
+        for h in range(2):
+            lo, hi = 384 * h, 384 * h + 384
+            scan(f(dst, lo, hi), f(d0, lo, hi), f(src, lo, hi), 0.0, OP.mult, OP.add)
 
     for t in range(R):
-        ft = "F%d" % t
-        if t:
-            scores(t, "F%d" % (t - 1))
-            for h in range(2):
-                steps("TA", "D0X", "TD", h)
-            unpack(t)
+        ft, xq, xs = "F%d" % t, "XQ%d" % t, "XS%d" % t
+        src = "F%d" % (t - 1) if t else "XT"
+        table()
+        for a in range(2):
+            quant(xq, xs, 256 * a, 256 * a + 256, f(src, 1024 * a, 1024 * a + 1024))
+            mm(f("PS", 512 * a, 512 * a + 256), f("UQR"), f("USR"), f(xq, 256 * a, 256 * a + 256), f(xs, 256 * a, 256 * a + 256))
+        for a in range(2):
+            if t:
+                tt(f("PW", 256 * a, 256 * a + 256), f("PS", 512 * a, 512 * a + 256), f("CM", 256 * a, 256 * a + 256), OP.mult)
+            else:
+                act(f("PW", 256 * a, 256 * a + 256), f("PS", 512 * a, 512 * a + 256))
         for h in range(2):
-            scan(f("Z", 272 * h, 272 * h + 272), f("FOLD", 0, 272), f("SG", 272 * h, 272 * h + 272), 0.0, OP.mult, OP.add)
-        choose(lambda h: f("Z", 272 * h + 15, 272 * h + 272, 16), 0, [lambda: differences(0), lambda: differences(1)] + ([outer_list] if t == 0 else []))
-        for h in range(2):
-            ts(f("GT", ROW * h, ROW * h + ROW), member_row(0, h), 0.0, OP.not_equal, -BIG, OP.mult)
-        clean(0)
-        scaled(0, f("RVF", 0, 34))
-        scaled(0, f("SPF", 0, 578, 17))
-        columns("RVF", "D0F")
-        column_signs("D0F")
-        if t == 0:
-            bases()
-        for h in range(2):
-            tt(f("S2", ROW * h, ROW * h + ROW), f("Z", 272 * h + 15, 272 * h + 272, 16), f("GT", ROW * h, ROW * h + ROW), OP.add)
-        if t == 0:
-            choose(lambda h: f("S2", ROW * h, ROW * h + ROW), 1, [priorities, lambda: member_columns(0), lambda: member_columns(4)])
-            key(0, 0)
-            key(0, 1)
-        else:
-            choose(lambda h: f("S2", ROW * h, ROW * h + ROW), 1, [lambda: key(0, 0), lambda: key(0, 1)])
-        rows("SPF", "TA", 0, 0)
-        tt(f("KC"), f("RS", 305, 2 * SEL, BLK), f("RS", 322, 2 * SEL, BLK), OP.add)
-        key(1, 0)
-        key(1, 1)
+            o, i = f("SG", 256 * h, 256 * h + 256), f("PW", ind=("SL", 16 * h, 16 * h + 16))
+            if t:
+                act(o, i)
+            else:
+                tt(o, i, f("OWN", 0, 256), OP.mult)
+            scan(f("Z", 256 * h, 256 * h + 256), f("FOLD"), o, 0.0, OP.mult, OP.add)
         for b in range(4):
-            ts(f("KL", 4 * b, 4 * b + 4), f("KC"), float(b), OP.add)
-        act(f("KF"), f(ft, ind=("KL", 0, 16)))
-        for io in range(2):
-            scan(f("RK", 76 * io + 1, 76 * io + 77), f("KEY", 76 * io, 76 * io + 76), f("KEY", 76 * io, 76 * io + 76), -BIG, OP.max, OP.max)
-        scan(f("RK", 153, 229), f("KEY", 0, 76), f("RK", 0, 76), -BIG, OP.max, OP.min)
-        tt(f("DEC", 0, 8), f("RK", 19, 153, 19), f("ZK", 0, 8), OP.max)
-        scan(f("RK", 229, 305), f("KEY", 76, 152), f("RK", 76, 152), -BIG, OP.max, OP.min)
-        ts(f("DCM", 0, 8), f("DEC", 0, 8), 4095, OP.bitwise_and)
-        tt(f("DEC", 8, 16), f("RK", 171, 305, 19), f("ZK", 8, 16), OP.max)
-        for b in range(4):
-            ts(f("LL", 8 * b, 8 * b + 8), f("DCM", 0, 8), float(b), OP.add)
-            act(f("AB", 128 * b, 128 * b + 128), f(ft, ind=("LL", 8 * b, 8 * b + 8)))
-            if b == 1:
-                ts(f("DCM", 8, 16), f("DEC", 8, 16), 4095, OP.bitwise_and)
-        for b in range(4):
-            ts(f("LL", 32 + 8 * b, 40 + 8 * b), f("DCM", 8, 16), float(b), OP.add)
-        rows("SPF", "TA", 0, 1)
-        clean(1)
-        place_marks(0)
-        scaled(1, f("RVS", 0, 34))
-        scaled(1, f("SPS", 0, 578, 17))
-        place_marks(1)
-        act(f("SPA", 0, 578, 17), f("RVS", 0, 34), AF.Abs)
-        act(f("TA", 1, 1734, 3), f("TA", 0, 1734, 3), AF.Abs)
-        act(f("FS"), f("FG"), AF.Sign)
-        columns("RVS", "D0S")
-        column_signs("D0S")
-        for b in range(4):
-            tt(f("IO2", 128 * b, 128 * b + 128), f(ft, ind=("LL", 32 + 8 * b, 40 + 8 * b)), f("AB", 128 * b, 128 * b + 128), OP.add)
-
-        def larger(b):
-            tt(f("M2", 64 * b, 64 * b + 64), f("IO2", 128 * b, 128 * b + 64), f("IO2", 128 * b + 64, 128 * b + 128), OP.max)
-
-        def half(a):
-            ts(f("MH", 128 * a, 128 * a + 128), f("M2", 128 * a, 128 * a + 128), 0.5, OP.mult)
-
-        def less(b):
-            tt(f("YT", b, 256, 4), f("MH", 64 * b, 64 * b + 64), f("KF", 64 * b, 64 * b + 64), OP.subtract)
-
-        for fn, b in ((larger, 0), (larger, 1), (larger, 2), (half, 0), (larger, 3), (less, 0), (half, 1), (less, 1), (less, 2), (less, 3)):
-            fn(b)
+            mm(f("PS", 1024 + 512 * b, 1536 + 512 * b), f("EQ", 128 * b, 128 * b + 128), f("ES", 128 * b, 128 * b + 128), f(xq), f(xs))
+            for a in range(2):
+                act(f(ft, 1024 * a + b, 1024 * a + 1024, 4), f("PS", 1024 + 512 * b + 256 * a, 1280 + 512 * b + 256 * a))
+        choose(0, lambda h: f("Z", 256 * h + 15, 256 * h + 256, 16))
+        ts(f("GM"), f("TAB", ind=("L4", 0, 4)), 0.0, OP.not_equal, -BIG, OP.mult)
+        turn(f("GMT"), f("GM"))
+        act(f("ZW"), f("Z", ind=("ZWL",)))
+        tt(f("S2"), f("ZW"), f("GMT"), OP.add)
+        choose(1, lambda h: f("S2", 32 * h, 32 * h + 32))
+        slots(0, ft)
+        slots(1, ft)
         quant("SQ%d" % t, "SS%d" % t, 0, 128, f("YT"))
         send(t)
         if t == 0:
             for i in range(R):
                 dma("y", f("LQ%d" % i, 64, 128, cast=dt.uint8), f("SQ0", 64, 128, cast=dt.uint8))
                 dma("y", f("LS%d" % i, 64, 128), f("SS0", 64, 128))
-        for h in range(2):
-            steps("TB", "D0F", "TA", h)
-        tt(f("FH"), f("FS", 0, 34), f("FS", 34, 68), OP.add)
-        act(f("FV", 0, 34), f("FH"), AF.Identity, 2.0, -3.0)
-        act(f("SPX", 0, 578, 17), f("FH"), AF.Identity, 2.0, -3.0)
-        act(f("D0X", 1, 1776, 3), f("FV", 0, 34, ind=("OUTL", 0, 37)))
-        act(f("YW"), f("YT", 0, 256), AF.Copy, 32.0)
-        for h in range(2):
-            rows("SPS", "TB", 0, h)
-        for h in range(2):
-            rows("SPA", "TB", 1, h)
-        for h in range(2):
-            steps("TC", "D0S", "TB", h)
-        rows("SPX", "D0X", 2, 0)
-        for h in range(2):
-            ts(f("TD", SQ3 * h, SQ3 * h + SQ3, 3), f("TC", SQ3 * h + 2, SQ3 * h + SQ3, 3), 3.0 * UNIT, OP.min, -3.0 * UNIT, OP.max)
-        if t == 1:
-            output_list()
+            cp(f("CM", ind=("SL",)), f("OWN"))
+        operands(0, "D0F", "TA")
+        steps("TB", "D0F", "TA")
+        operands(1, "D0S", "TB")
+        steps("TC", "D0S", "TB")
+        ts(f("TD", 0, 768, 3), f("TC", 2, 768, 3), 3.0 * U, OP.min, -3.0 * U, OP.max)
+        ts(f("DD"), f("X2"), MARK, OP.is_equal, -2.0, OP.mult)
+        tt(f("SN"), f("DD", 0, 64), f("DD", 64, 128), OP.add)
+        aff(f("SPX", 0, 256, 8), f("SN", ind=("SPG",)), 1.0, 1.0)
+        aff(f("D0X", 1, 768, 3), f("SN", ind=("COLG",)), 1.0, 1.0)
+        scan(f("D0X", 2, 768, 3), f("KEEP"), f("SPX"), 0.0, OP.mult, OP.add)
+        steps("TA", "D0X", "TD")
         if t == R - 1:
-            rows("SPX", "D0X", 2, 1)
-            quant("VQ", "VS", 0, 128, f("VT"))
-            for h in range(2):
-                steps("TA", "D0X", "TD", h)
-            act(f("OAO"), f("TA", ind=("OL", 0, 32)), AF.Copy, -1.0 / UNIT)
-            dma("y", (T.oa[:, :], []), f("OAO"))
+            fill(f("TA", 1024, 1040), 0.0)
+            act(f("TA", 768, 1024), f("TA", 2, 768, 3), AF.Copy, -1.0)
+            act(f("OAO"), f("TA", ind=("OUT",)), AF.Copy, 1.0 / U)
+            dma("y", hbm(T.oa[:, :]), f("OAO"))
+        cp(f("KL"), f("DM", ind=("KLL", 0, 1)))
+        act(f("YW"), f("YT", 0, 256), AF.Copy, 32.0)
         for b in range(4):
-            mm(f("PS", 1024 + 512 * b, 1152 + 512 * b), f("WQ", 128 * b, 128 * b + 128), f("WS", 128 * b, 128 * b + 128), f("LQ%d" % t), f("LS%d" % t))
-        for b in range(4):
-            tt(f("V32", 64 * b, 64 * b + 64), f("PS", 1024 + 512 * b, 1088 + 512 * b), f("YW", b, 256, 4), OP.add)
+            at = (0, 512, 3072, 3584)[b]
+            mm(f("PS", at, at + 128), f("WQ", 128 * b, 128 * b + 128), f("WS", 128 * b, 128 * b + 128), f("LQ%d" % t), f("LS%d" % t))
+            tt(f("V32", 64 * b, 64 * b + 64), f("PS", at, at + 64), f("YW", b, 256, 4), OP.add)
         ts(f("VV"), f("V32"), 0.03125, OP.mult)
-        if t < R - 1:
-            rows("SPX", "D0X", 2, 1)
-        cp(f(ft, ind=("KL", 0, 16)), f("VV"))
+        cp(f(ft, ind=("KL",)), f("VV"))
 
+    quant("VQ", "VS", 0, 128, f("VT"))
     for a in range(2):
         lo, hi = 256 * a, 256 * a + 256
         quant("XQ3", "XS3", lo, hi, f("F2", 1024 * a, 1024 * a + 1024))
         mm(f("PS", 512 * a, 512 * a + 256), f("VQ"), f("VS"), f("XQ3", lo, hi), f("XS3", lo, hi))
-        dma("y", (T.oc[:, 4 * lo:4 * hi], []), f("XQ3", lo, hi, cast=dt.uint8))
+        dma("y", hbm(T.oc[:, 4 * lo:4 * hi]), f("XQ3", lo, hi, cast=dt.uint8))
     act(f("YO", 0, 256), f("PS", 0, 256))
-    dma("s", (T.y[:, 0:256], []), f("YO", 0, 256))
+    dma("s", hbm(T.y[:, 0:256]), f("YO", 0, 256))
     cp(f("YO", 256, 512), f("PS", 512, 768))
-    dma("y", (T.y[:, 256:512], []), f("YO", 256, 512))
+    dma("y", hbm(T.y[:, 256:512]), f("YO", 256, 512))
     for k in range(4):
-        dma("s" if k % 2 else "y", (T.osc[4 * k:4 * k + 4, :], []), (T.XS3[32 * k:32 * k + 4, 0:512], [("XS3", 0, 512, 1)]))
-    for sem in count:
-        if sem != "dma":
-            wait("p", sem, count[sem])
+        dma("s" if k % 2 else "y", hbm(T.osc[4 * k:4 * k + 4, :]), (T.XS3[32 * k:32 * k + 4, 0:512], [("XS3", 0, 512, 1)]))
+    issue()

@@ -1,4 +1,4 @@
-from concourse.mybir import dt, AluOpType, AxisListType, ActivationFunctionType
+from concourse.mybir import dt, AluOpType, ActivationFunctionType
 
 OP = AluOpType
 AF = ActivationFunctionType
@@ -15,39 +15,92 @@ for _n, _w, _d in (
     ("XT", 2048, BF), ("UT", 512, BF), ("VT", 512, BF), ("ET", 528, BF), ("ONE", 528, BF),
     ("UQ", 128, CODES), ("US", 128, PLANE), ("UQR", 128, CODES), ("USR", 128, PLANE), ("VQ", 128, CODES), ("VS", 128, PLANE),
     ("WQ", 512, CODES), ("WS", 512, PLANE), ("EQ", 512, CODES), ("ES", 512, PLANE),
-    ("NDI", 32, I32), ("ARI", 512, I32), ("ARB", 512, BF), ("IA", 160, I32), ("FA", 1280, F32), ("SC", 32, F32),
+    ("NDI", 32, I32), ("ARI", 512, I32), ("ARB", 512, BF), ("IA", 160, I32), ("FA", 1280, F32), ("SC", 32, F32), ("KT", 208, F32),
     ("KI", 256, BF), ("OWN", 512, BF), ("CM", 512, BF), ("FOLD", 256, BF), ("KEEP", 256, BF),
     ("UL", 8, U16), ("SL", 32, U16), ("SM", 32, U16), ("CIRC", 16, U16), ("COLG", 16, U16), ("EXP", 34, U16), ("OUT", 32, U16),
-    ("PW", 512, F32), ("SG", 512, F32), ("Z", 528, F32), ("ZW", 64, F32), ("RX", 104, F32), ("FL", 104, F32), ("SE", 104, F32), ("SK", 104, F32),
-    ("L4", 8, U16), ("GM", 64, BF), ("GMT", 64, BF), ("S2", 64, F32), ("TAB", 1120, BF), ("EX", 528, BF),
-    ("GK0", 128, F32), ("GK1", 128, F32), ("KY0", 128, F32), ("KY1", 128, F32), ("RK0", 400, F32), ("RK1", 400, F32),
-    ("DI", 96, I32), ("DM", 96, I32), ("LL", 96, U16), ("KL", 16, U16),
-    ("AB", 512, BF), ("D0Y", 768, BF), ("D1Y", 768, BF), ("YS", 768, BF), ("YT", 512, BF), ("YW", 256, BF), ("V32", 256, BF), ("VV", 256, BF),
+    ("PW", 512, F32), ("SG", 512, F32), ("Z", 528, F32), ("ZW", 64, F32), ("ZL", 64, F32), ("RB", 544, F32), ("RX", 72, F32),
+    ("FL", 104, F32), ("SE", 104, F32), ("SK", 104, F32),
+    ("L4", 8, U16), ("GM", 64, F32), ("S2", 64, F32), ("TAB", 1120, BF), ("TAM", 1120, BF), ("EX", 528, BF),
+    ("GK0", 128, F32), ("GK1", 128, F32), ("KY0", 128, F32), ("KY1", 128, F32),
+    ("RA0", 4 * KS, F32), ("RA1", 4 * KS, F32), ("RC0", 2 * KS, F32), ("RC1", 2 * KS, F32),
+    ("DI", 96, I32), ("DM", 96, I32), ("LL", 96, U16),
+    ("AB", 512, BF), ("D0Y", 768, BF), ("D1Y", 768, BF), ("YS", 768, BF), ("YT", 640, BF), ("YW", 256, BF), ("V32", 256, BF), ("VV", 256, BF),
     ("XG", 128, BF), ("X2", 128, BF), ("DD", 128, BF), ("SN", 64, BF), ("SP0", 256, BF), ("SP1", 256, BF), ("SPX", 256, BF),
     ("D0F", 768, BF), ("D0S", 768, BF), ("D0X", 768, BF), ("TA", 1040, BF), ("TB", 768, BF), ("TC", 768, BF), ("TD", 768, BF),
     ("OAO", 512, F32), ("YO", 512, F32),
-) + tuple(("F%d" % t, W, BF) for t in range(R)) + tuple((n + "%d" % t, 128, d) for t in range(R) for n, d in (("SQ", CODES), ("SS", PLANE), ("LQ", CODES), ("LS", PLANE))) \
+) + tuple(("F%d" % t, W, BF) for t in range(R)) \
+  + tuple((n + "%d" % t, w, d) for t in range(R) for n, w, d in (("SQ", 256, CODES), ("SS", 256, PLANE), ("LQ", 160, CODES), ("LS", 160, PLANE))) \
   + tuple((n + "%d" % t, 512, d) for t in range(R + 1) for n, d in (("XQ", CODES), ("XS", PLANE))):
     SCRATCH[_n] = ("sbuf", [128, _w], _d)
 
-SEMAPHORES = ["cv", "cs", "ct", "cp", "left"] + ["arr%d" % t for t in range(R)] + ["dm%d" % i for i in range(32)]
+SEMAPHORES = ["cv", "cs", "ct", "cp", "left"] + ["arr%d" % t for t in range(2 * R)] + ["dm%d" % i for i in range(40)]
 COUNTER = {"v": "cv", "s": "cs", "t": "ct", "p": "cp"}
 PART = {}
 for _b, _names in (
     ("IA", (("PI", 8), ("BITS", 8), ("DDI", 32), ("DI4", 32), ("JI", 16), ("JJ", 16))),
-    ("FA", (("N", 72), ("E64", 64), ("K32", 32), ("DU", 64), ("HE", 8), ("W1", 32), ("BP", 48), ("ISO", 64), ("NIS", 64), ("DUM", 64), ("CB", 128), ("CC", 128),
+    ("FA", (("N", 72), ("E64", 64), ("K32", 32), ("DU", 64), ("HE", 8), ("W1", 32), ("BP", 32), ("ISO", 64), ("NIS", 64), ("DUM", 64), ("CB", 128), ("CC", 128),
             ("NDD", 64), ("NDM", 64), ("NWI", 64), ("NW", 64), ("N4", 32), ("T1", 40), ("T2", 40), ("T3", 40), ("T4", 40), ("T5", 40))),
-    ("SC", tuple((n, 1) for n in ("pm", "e", "p31", "qh", "ql", "h1", "a1", "n1", "A", "B", "e16", "kb0", "kb1", "sO", "sI", "pm16", "sb", "s1", "qh16", "t66",
-                                  "dl", "kl", "zb"))),
-    ("SM", (("SPG", 2), ("DL", 4), ("NDL", 4), ("ZWL", 4), ("KLL", 2))),
+    ("SC", tuple((n, 1) for n in ("pm", "e", "p31", "qh", "ql", "h1", "A", "B", "e16", "kb0", "kb1", "sO", "sI", "pm16", "sb", "s1", "qh16", "t66",
+                                  "dl", "zb"))),
+    ("SM", (("SPG", 2), ("DL", 2), ("NDL", 4), ("ZWL", 4))),
 ):
     _a = 0
     for _n, _w in _names:
         PART[_n] = (_b, _a, _w)
         _a += _w
-SCRATCH["KT"] = ("sbuf", [128, 208], F32)
-CYC = 0.00104
-WAKE = 0.11
+CYC = 0.00083
+WAKE = 0.2
+PLAN = {"seed": 217, "noise": 0.8, "hold": 2.0}
+
+
+def order(ops, seed, noise, hold):
+    n = len(ops)
+    tail = [0.0] * n
+    users = [[] for _ in ops]
+    for i, o in enumerate(ops):
+        for k in o["need"]:
+            users[k].append(i)
+    for i in range(n - 1, -1, -1):
+        tail[i] = min(a[1] for a in ops[i]["alt"].values()) + ops[i]["lat"] + max([tail[u] + WAKE for u in users[i]] + [0.0])
+    x = seed
+    rank = []
+    for i in range(n):
+        x = (x * 1103515245 + 12345) % 2147483648
+        rank.append(tail[i] + noise * x / 2147483648.0)
+    free = {q: 0.0 for q in "vstpy"}
+    done = [0.0] * n
+    after = [0.0] * n
+    left = [len(o["need"]) for o in ops]
+    ready = [i for i in range(n) if not left[i]]
+    seq = []
+    while ready:
+        t0, q = min((max(free[k], after[i]), k) for i in ready for k in ops[i]["alt"])
+        mine = []
+        for i in ready:
+            alt = ops[i]["alt"]
+            if q in alt:
+                end = max(t0, after[i]) + alt[q][1]
+                if all(end <= max(free[k], after[i]) + alt[k][1] + 0.1 for k in alt):
+                    mine.append(i)
+        can = [i for i in mine if after[i] <= t0 + 0.01]
+        if not can:
+            free[q] = t0 + 0.05
+            continue
+        now = max(can, key=lambda i: rank[i])
+        d = ops[now]["alt"][q][1]
+        soon = [i for i in mine if rank[i] > rank[now] + d and hold * (after[i] - t0) < d]
+        if soon:
+            now = max(soon, key=lambda i: rank[i])
+        free[q] = max(t0, after[now]) + ops[now]["alt"][q][1]
+        done[now] = free[q] + ops[now]["lat"]
+        ready.remove(now)
+        seq.append((now, q))
+        for u in users[now]:
+            left[u] -= 1
+            after[u] = max(after[u], done[now] + WAKE)
+            if not left[u]:
+                ready.append(u)
+    return seq, max(done)
 
 
 def make_plan(g, T):
@@ -76,7 +129,7 @@ def make_plan(g, T):
     def bank(d):
         return (d[0], d[1] // 512 * 512, (d[2] + 511) // 512 * 512, 1) if d[0] == "PS" else d
 
-    def note(q, fn, outs, ins, dur, lat=0.0, kind="call"):
+    def note(alt, outs, ins, lat=0.0, kind="call"):
         reads = [d for v in ins for d in v[1] if d[0] != "PS"] + [d for v in outs for d in v[1][1:]]
         writes = [bank(v[1][0]) for v in outs if v[1]] + [bank(d) for v in ins for d in v[1] if d[0] == "PS"]
         me = len(ops)
@@ -90,50 +143,12 @@ def make_plan(g, T):
             hist[name] = [h for h in hist.get(name, []) if not (lo <= h[0] and h[1] <= hi and (st == 1 or st == h[2] and (lo - h[0]) % st == 0))] + [(lo, hi, st, True, me)]
         for name, lo, hi, st in reads:
             hist.setdefault(name, []).append((lo, hi, st, False, me))
-        ops.append({"q": q, "fn": fn, "need": need, "dur": dur, "lat": lat, "kind": kind})
-
-    def cost(q, out, ins, per):
-        if out[2] < 0:
-            return 0.05 - out[2] * 0.0032
-        for v in ins:
-            if v[2] < 0:
-                return 0.06 - v[2] * 0.0013
-        return max(64, max(v[2] for v in [out] + ins) * per) * CYC
-
-    def order():
-        n = len(ops)
-        tail = [0.0] * n
-        users = [[] for _ in ops]
-        for i, o in enumerate(ops):
-            for k in o["need"]:
-                users[k].append(i)
-        for i in range(n - 1, -1, -1):
-            tail[i] = ops[i]["dur"] + ops[i]["lat"] + max([tail[u] + WAKE for u in users[i]] + [0.0])
-        free = {q: 0.0 for q in eng}
-        done = [None] * n
-        left = [len(o["need"]) for o in ops]
-        ready = [i for i in range(n) if not left[i]]
-        seq = []
-        while ready:
-            start = {i: max([free[ops[i]["q"]]] + [done[k] + WAKE for k in ops[i]["need"]]) for i in ready}
-            first = min(ready, key=lambda i: (start[i], -tail[i]))
-            q, t0 = ops[first]["q"], start[first]
-            mine = [i for i in ready if ops[i]["q"] == q]
-            now = max((i for i in mine if start[i] <= t0 + 0.01), key=lambda i: tail[i])
-            soon = [i for i in mine if tail[i] > tail[now] + ops[now]["dur"] and 2 * (start[i] - t0) < ops[now]["dur"]]
-            if soon:
-                now = max(soon, key=lambda i: tail[i])
-            free[q] = start[now] + ops[now]["dur"]
-            done[now] = free[q] + ops[now]["lat"]
-            ready.remove(now)
-            seq.append(now)
-            for u in users[now]:
-                left[u] -= 1
-                if not left[u]:
-                    ready.append(u)
-        return seq
+        ops.append({"alt": alt, "need": sorted(need), "lat": lat, "kind": kind})
 
     def issue():
+        if "seq" not in PLAN:
+            PLAN["ops"] = ops
+            PLAN["seq"] = order(ops, PLAN["seed"], PLAN["noise"], PLAN["hold"])[0]
         count = {}
         known = {q: {} for q in eng}
         mark = {}
@@ -144,9 +159,9 @@ def make_plan(g, T):
                 eng[q].wait_ge(T.sem[sem], val)
 
         ndma = 0
-        for i in order():
+        for i, q in PLAN["seq"]:
             o = ops[i]
-            q = o["q"]
+            fn = o["alt"][q][0]
             need = {}
             for k in o["need"]:
                 sem, val = mark[k]
@@ -156,102 +171,127 @@ def make_plan(g, T):
             if o["kind"] == "call":
                 sem = COUNTER[q]
                 count[sem] = count.get(sem, 0) + 1
-                o["fn"](eng[q]).then_inc(T.sem[sem], 1)
+                fn(eng[q]).then_inc(T.sem[sem], 1)
             elif o["kind"] == "dma":
                 sem = "dm%d" % ndma
                 ndma += 1
                 count[sem] = 16
-                o["fn"](eng[q]).then_inc(T.sem[sem], 16)
+                fn(eng[q]).then_inc(T.sem[sem], 16)
             else:
-                sem, n = o["fn"](eng[q])
+                sem, n = fn(eng[q])
                 count[sem] = n
                 count["left"] = count.get("left", 0) + n
             mark[i] = (sem, count[sem])
         for sem in count:
             wait("p", sem, count[sem])
 
-    return view, note, cost, issue
+    return view, note, issue
 
 
 def rank_program(g, core, T, topo):
     rank = T.rank_of(core)
     if rank is None:
         return
-    f, note, cost, issue = make_plan(g, T)
+    f, note, issue = make_plan(g, T)
+
+    def cost(q, out, ins, per):
+        if out[2] < 0:
+            return 0.05 - out[2] * 0.0032
+        for v in ins:
+            if v[2] < 0:
+                return (0.05 if q == "v" else 0.065) - v[2] * 0.0013
+        return max(64, max(v[2] for v in [out] + ins) * per) * CYC + (0.05 if q == "s" else 0.0)
 
     def rate(*vs):
         return 0.5 if all(v[3] for v in vs) else 1.0
 
-    def tt(out, a, b, op):
-        note("v", lambda e: e.tensor_tensor(out[0], a[0], b[0], op), [out], [a, b], cost("v", out, [a, b], 1.0 if a[4] or b[4] else 2.0))
+    def num(s):
+        return s[0] if isinstance(s, tuple) else s
 
-    def ts(out, a, s1, op0, s2=None, op1=None):
-        ins = [a] + [s for s in (s1, s2) if isinstance(s, tuple)]
-        x1 = s1[0] if isinstance(s1, tuple) else s1
-        x2 = s2[0] if isinstance(s2, tuple) else s2
+    def cols(*ss):
+        return [s for s in ss if isinstance(s, tuple)]
+
+    def tt(out, a, b, op):
+        note({"v": (lambda e: e.tensor_tensor(out[0], a[0], b[0], op), cost("v", out, [a, b], 1.0 if a[4] or b[4] else 2.0))}, [out], [a, b])
+
+    def v_ts(out, a, s1, op0, s2=None, op1=None):
         c = cost("v", out, [a], rate(out, a))
         if op1 is None:
-            note("v", lambda e: e.tensor_scalar(out[0], a[0], x1, None, op0), [out], ins, c)
-        else:
-            note("v", lambda e: e.tensor_scalar(out[0], a[0], x1, x2, op0, op1), [out], ins, c)
+            return (lambda e: e.tensor_scalar(out[0], a[0], num(s1), None, op0), c)
+        return (lambda e: e.tensor_scalar(out[0], a[0], num(s1), num(s2), op0, op1), c)
+
+    def v_cp(out, a):
+        return (lambda e: e.tensor_copy(out[0], a[0]), cost("v", out, [a], rate(out, a)))
+
+    def s_act(out, a, func, scale=1.0, bias=None):
+        c = cost("s", out, [a], 1.0)
+        if bias is not None:
+            return (lambda e: e.activation(out[0], a[0], func, bias=num(bias), scale=num(scale)), c)
+        if isinstance(scale, tuple) or scale != 1.0:
+            return (lambda e: e.activation(out[0], a[0], func, scale=num(scale)), c)
+        return (lambda e: e.activation(out[0], a[0], func), c)
+
+    def ts(out, a, s1, op0, s2=None, op1=None):
+        note({"v": v_ts(out, a, s1, op0, s2, op1)}, [out], [a] + cols(s1, s2))
 
     def cp(out, a):
-        note("v", lambda e: e.tensor_copy(out[0], a[0]), [out], [a], cost("v", out, [a], rate(out, a)))
+        note({"v": v_cp(out, a)}, [out], [a])
+
+    def act(out, a, func, scale=1.0):
+        note({"s": s_act(out, a, func, scale)}, [out], [a] + cols(scale))
+
+    def move(out, a, scale=1.0, bias=None):
+        if bias is not None:
+            alt = {"v": v_ts(out, a, scale, OP.mult, bias, OP.add), "s": s_act(out, a, AF.Identity, scale, bias)}
+        elif isinstance(scale, tuple) or scale != 1.0:
+            alt = {"v": v_ts(out, a, scale, OP.mult), "s": s_act(out, a, AF.Copy, scale)}
+        else:
+            alt = {"v": v_cp(out, a), "s": s_act(out, a, AF.Copy)}
+        note(alt, [out], [a] + cols(scale, bias))
 
     def fill(out, c):
-        note("v", lambda e: e.memset(out[0], c), [out], [], cost("v", out, [], rate(out)))
+        note({"v": (lambda e: e.memset(out[0], c), cost("v", out, [], rate(out)))}, [out], [])
+
+    def const(out, c):
+        one = f("ONE", 0, out[2])
+        alt = {"v": (lambda e: e.memset(out[0], c), cost("v", out, [], rate(out))), "s": s_act(out, one, AF.Copy, c)}
+        if c == 0.0:
+            alt["p"] = (lambda e: e.iota(out[0], [[0, out[2]]], 0, 0, allow_small_or_imprecise_dtypes=True), 0.13 + 2 * CYC * out[2])
+        note(alt, [out], [one])
 
     def scan(out, d0, d1, init, op0, op1):
-        note("v", lambda e: e.tensor_tensor_scan(out[0], d0[0], d1[0], init, op0, op1), [out], [d0, d1], cost("v", out, [d0, d1], rate(out, d0, d1)))
+        note({"v": (lambda e: e.tensor_tensor_scan(out[0], d0[0], d1[0], init, op0, op1), cost("v", out, [d0, d1], rate(out, d0, d1)))}, [out], [d0, d1])
 
     def turn(out, a):
-        note("v", lambda e: e.transpose(out[0], a[0]), [out], [a], cost("v", out, [a], rate(out, a)))
+        note({"v": (lambda e: e.transpose(out[0], a[0]), cost("v", out, [a], rate(out, a)))}, [out], [a])
 
     def quant(qn, sn, lo, hi, a):
         q, s = f(qn, lo, hi), f(sn, lo, hi)
-        note("v", lambda e: e.quantize_mx(q[0], s[0], a[0]), [q, s], [a], 0.015 + 0.000275 * a[2])
-
-    def act(out, a, func=AF.Copy, scale=1.0, bias=None):
-        ins = [a] + [s for s in (scale, bias) if isinstance(s, tuple)]
-        sc = scale[0] if isinstance(scale, tuple) else scale
-        c = cost("s", out, [a], 1.0)
-        if bias is None and not isinstance(scale, tuple) and scale == 1.0:
-            note("s", lambda e: e.activation(out[0], a[0], func), [out], ins, c)
-        elif bias is None:
-            note("s", lambda e: e.activation(out[0], a[0], func, scale=sc), [out], ins, c)
-        else:
-            bi = bias[0] if isinstance(bias, tuple) else bias
-            note("s", lambda e: e.activation(out[0], a[0], func, bias=bi, scale=sc), [out], ins, c)
-
-    def aff(out, a, scale, bias):
-        act(out, a, AF.Identity, scale, bias)
+        note({"v": (lambda e: e.quantize_mx(q[0], s[0], a[0]), 0.012 + 0.00022 * a[2])}, [q, s], [a])
 
     def mm(out, l, ls, r, rs):
-        note("t", lambda e: e.matmul_mx(out[0], l[0], ls[0], r[0], rs[0], True, True), [out], [l, ls, r, rs], (r[2] + 16) * 0.0005)
+        note({"t": (lambda e: e.matmul_mx(out[0], l[0], ls[0], r[0], rs[0], True, True), (r[2] + 16) * 0.0005)}, [out], [l, ls, r, rs])
 
     def iota(out, pattern, base=0, cm=0, small=True):
         if small:
-            note("p", lambda e: e.iota(out[0], pattern, base, cm, allow_small_or_imprecise_dtypes=True), [out], [], 0.16 + 2 * CYC * out[2])
+            note({"p": (lambda e: e.iota(out[0], pattern, base, cm, allow_small_or_imprecise_dtypes=True), 0.13 + 2 * CYC * out[2])}, [out], [])
         else:
-            note("p", lambda e: e.iota(out[0], pattern, base, cm), [out], [], 0.16 + 2 * CYC * out[2])
+            note({"p": (lambda e: e.iota(out[0], pattern, base, cm), 0.13 + 2 * CYC * out[2])}, [out], [])
 
-    def zero(out):
-        iota(out, [[0, out[2]]])
-
-    def dma(q, out, in_, lat=2.2):
-        note(q, lambda e: e.dma_start(out[0], in_[0]), [out], [in_], 0.05, lat, "dma")
+    def dma(q, out, in_, lat=1.3):
+        note({k: (lambda e: e.dma_start(out[0], in_[0]), 0.05) for k in q}, [out], [in_], lat, "dma")
 
     def hbm(ap):
         return (ap, [])
 
     dma("y", f("NDI"), hbm(T.nd[:, :]))
-    dma("s", f("UT"), hbm(T.u[:, :]))
-    dma("y", f("XT", 0, 1024), hbm(T.x[:, 0:1024]), 3.0)
-    dma("s", f("XT", 1024, 2048), hbm(T.x[:, 1024:2048]), 3.0)
-    dma("y", f("ARI"), hbm(T.ar[:, :]), 3.5)
-    dma("s", f("WQ", cast=dt.uint8), hbm(T.wc[:, :]), 4.0)
-    dma("y", f("WS"), hbm(T.ws[:, :]), 4.0)
-    dma("s", f("VT"), hbm(T.v[:, :]), 4.0)
+    dma("s", f("UT"), hbm(T.u[:, :]), 1.6)
+    dma("y", f("XT", 0, 1024), hbm(T.x[:, 0:1024]), 2.0)
+    dma("s", f("XT", 1024, 2048), hbm(T.x[:, 1024:2048]), 2.0)
+    dma("y", f("ARI"), hbm(T.ar[:, :]), 2.2)
+    dma("y", f("WQ", cast=dt.uint8), hbm(T.wc[:, :]), 2.5)
+    dma("y", f("WS"), hbm(T.ws[:, :]), 2.5)
+    dma("y", f("VT"), hbm(T.v[:, :]), 2.5)
 
     iota(f("PI", 0, 1), [[0, 1]], 0, 1, small=False)
     iota(f("N"), [[1, 72]])
@@ -261,70 +301,72 @@ def rank_program(g, core, T, topo):
     iota(f("K32"), [[0, 2], [1, 16]])
     iota(f("DU"), [[64, 2], [0, 2], [4, 16]], 2048)
     iota(f("W1"), [[384, 2], [24, 16]], -1)
-    iota(f("BP"), [[0, 6], [1, 4], [0, 2]])
+    iota(f("BP"), [[0, 4], [1, 4], [0, 2]])
     fill(f("ONE"), 1.0)
     et, one = f("ET"), f("ONE")
-    note("p", lambda e: e.affine_select(et[0], one[0], [[-1, 528]], OP.is_equal, 0.0, 3, 4), [et], [one], 1.3)
-    for n, k in (("FOLD", 16), ("KEEP", 8)):
-        act(f(n), f("ONE", 0, 256))
-        fill(f(n, 0, 256, k), 0.0)
+    note({"p": (lambda e: e.affine_select(et[0], one[0], [[-1, 528]], OP.is_equal, 0.0, 3, 4), 1.05)}, [et], [one])
+    const(f("FOLD"), 2 * BIG)
+    fill(f("FOLD", 0, 256, 16), -2 * BIG)
+    const(f("KEEP"), 1.0)
+    fill(f("KEEP", 0, 256, 8), 0.0)
     for t in range(R):
-        zero(f("F%d" % t, 2048, W))
-    zero(f("YT", 256, 512))
+        const(f("F%d" % t, 2048, W), 0.0)
+    const(f("YT", 128, 512), 0.0)
     for a in (0, 544, 1088):
-        zero(f("TAB", a, a + 32))
+        const(f("TAB", a, a + 32), 0.0)
+        const(f("TAM", a, a + 32), 0.0)
     for n in ("SP0", "SP1", "SPX"):
-        act(f(n), f("ONE", 0, 256), AF.Copy, 0.0)
+        const(f(n), 0.0)
     for n, j in (("D0F", 0), ("D0S", 0), ("D0X", 0), ("TD", 1), ("TD", 2), ("TA", 0), ("TA", 1), ("D0Y", 0), ("D1Y", 1)):
-        act(f(n, j, 768, 3), f("ONE", 0, 256), AF.Copy, 0.0)
-    act(f("D1Y", 0, 768, 3), f("ONE", 0, 256), AF.Copy, -BIG)
+        const(f(n, j, 768, 3), 0.0)
+    const(f("D1Y", 0, 768, 3), -BIG)
     fill(f("TA", 1024, 1040), MARK)
     fill(f("Z", 512, 528), -BIG / 32)
-    fill(f("RX", 0, 34, 17), -2 * BIG)
-    fill(f("RX", 36, 102, 33), -2 * BIG)
-    for n in ("RK0", "RK1"):
-        zero(f(n))
-        fill(f(n, 0, 1), BIG)
-        fill(f(n, KS, KS + 1), -BIG)
+    fill(f("RB", 15, 288, 272), -2 * BIG)
+    fill(f("RX", 0, 34, 33), 2 * BIG)
+    for j in range(2):
+        const(f("RA%d" % j), 0.0)
+        const(f("RC%d" % j), 0.0)
+        fill(f("RA%d" % j, 0, 1), BIG)
+        fill(f("RA%d" % j, KS, KS + 1), -BIG)
 
     pi = f("PI", 0, 1)
-    for j, (sh, m) in enumerate(((0, 15), (4, 1), (0, 31), (3, 1), (0, 7), (0, 1), (1, 7), (1, 1))):
+    for j, (sh, m) in enumerate(((0, 15), (4, 1), (0, 31), (3, 1), (0, 7), (0, 1))):
         ts(f("BITS", j, j + 1), pi, sh, OP.logical_shift_right, m, OP.bitwise_and)
-    cp(f("SC", 0, 8), f("BITS"))
+    cp(f("SC", 0, 6), f("BITS", 0, 6))
     pm, e = f("pm"), f("e")
     for n, src, sc, bi in (("A", "e", -4096.0, 4096.0), ("B", "e", 4096.0, 0.0), ("e16", "e", 16.0, 0.0), ("kb0", "p31", 1 / 4096.0, 32 / 4096.0),
                            ("kb1", "p31", 1 / 4096.0, 576 / 4096.0), ("sO", "pm", -4096.0, 61440.0 - 67584.0), ("sI", "pm", 4096.0, 63488.0),
                            ("pm16", "pm", 1.0, 16.0), ("sb", "pm", 8.0, 783.0), ("s1", "qh", 1.0, f("ql")), ("qh16", "qh", 16.0, 0.0),
-                           ("t66", "qh", float(KS), 32.0), ("dl", "h1", 32.0, f("t66")), ("kl", "n1", 47.0, 32.0), ("zb", "pm", 16.0, -497.0)):
-        aff(f(n), f(src), sc, bi)
+                           ("t66", "qh", float(KS), 32.0), ("dl", "h1", 32.0, f("t66")), ("zb", "pm", 16.0, -497.0)):
+        move(f(n), f(src), sc, bi)
     ts(f("UL"), f("N", 0, 8), 16.0, OP.mult)
     ts(f("NDL"), f("HE", 0, 4), 16.0, OP.mult, pm, OP.add)
     ts(f("SPG"), f("N", 0, 64, 32), f("p31"), OP.add)
-    ts(f("DL", 0, 3), f("N", 0, 3), 2.0 * KS, OP.mult, f("dl"), OP.add)
-    ts(f("KLL", 0, 1), f("kl"), f("a1"), OP.add, f("h1"), OP.add)
+    ts(f("DL"), f("N", 0, 2), 2.0 * KS, OP.mult, f("dl"), OP.add)
     ts(f("ISO"), f("E64"), e, OP.is_equal)
-    aff(f("NIS"), f("ISO"), -1.0, 1.0)
+    move(f("NIS"), f("ISO"), -1.0, 1.0)
     tt(f("DUM"), f("DU"), f("NIS"), OP.mult)
-    ts(f("OWN", 0, 256), f("KI"), pm, OP.is_equal)
-    act(f("OWN", 256, 512), f("OWN", 0, 256))
+    ts(f("OWN", 0, 256), f("KI"), pm, OP.not_equal, -BIG, OP.mult)
+    move(f("OWN", 256, 512), f("OWN", 0, 256))
     for h in range(2):
-        aff(f("CB", 32 * h, 32 * h + 32), f("ISO", 0, 32), f("sI"), (12 - 8 * h) * U - 63488.0)
-        aff(f("CB", 64 + 32 * h, 96 + 32 * h), f("ISO", 0, 32), f("sO"), (4 + 8 * h) * U + 67584.0)
-    aff(f("T1", 0, 4), f("HE", 0, 4), 256.0, f("zb"))
+        move(f("CB", 32 * h, 32 * h + 32), f("ISO", 0, 32), f("sI"), (12 - 8 * h) * U - 63488.0)
+        move(f("CB", 64 + 32 * h, 96 + 32 * h), f("ISO", 0, 32), f("sO"), (4 + 8 * h) * U + 67584.0)
+    move(f("T1", 0, 4), f("HE", 0, 4), 256.0, f("zb"))
     tt(f("T1", 4, 8), f("T1", 0, 4), f("ISO", 0, 64, 16), OP.mult)
     ts(f("ZWL"), f("T1", 4, 8), 512.0, OP.add)
-    aff(f("KT", 0, 33), f("N", 0, 33), 32 / 4096.0, f("kb0"))
+    move(f("KT", 0, 33), f("N", 0, 33), 32 / 4096.0, f("kb0"))
     ts(f("T2", 0, 33), f("N", 0, 33), f("e16"), OP.subtract, -1.0, OP.max)
     ts(f("T3", 0, 33), f("T2", 0, 33), 16.0, OP.min, 32 / 4096.0, OP.mult)
     for h in range(2):
-        aff(f("KT", 36 + 33 * h, 69 + 33 * h), f("T3", 0, 33), 1.0, f("kb%d" % h))
-    act(f("KT", 104, 137), f("N", 0, 33), AF.Copy, 1 / 4096.0)
-    act(f("KT", 140, 206), f("N", 0, 66), AF.Copy, 1 / 4096.0)
+        move(f("KT", 36 + 33 * h, 69 + 33 * h), f("T3", 0, 33), 1.0, f("kb%d" % h))
+    move(f("KT", 104, 137), f("N", 0, 33), 1 / 4096.0)
+    move(f("KT", 140, 206), f("N", 0, 66), 1 / 4096.0)
     ts(f("JI"), f("K32", 0, 32, 2), f("s1"), OP.add, 1.0, OP.add)
     ts(f("JJ"), f("JI"), 15, OP.bitwise_and)
     for h in range(2):
         ts(f("COLG", 8 * h, 8 * h + 8), f("JJ", 8 * h, 8 * h + 8), f("e16"), OP.add, 32.0 * h, OP.add)
-    aff(f("T2", 0, 16), f("N", 0, 16), 32.0, f("qh16"))
+    move(f("T2", 0, 16), f("N", 0, 16), 32.0, f("qh16"))
     tt(f("T2", 16, 32), f("T2", 0, 16), f("JJ"), OP.add)
     cp(f("CIRC"), f("T2", 16, 32))
     ts(f("DDI"), f("K32"), -1.0, OP.mult, f("pm16"), OP.add)
@@ -334,7 +376,7 @@ def rank_program(g, core, T, topo):
     tt(f("T2", 0, 32), f("T1", 0, 32), f("W1"), OP.add)
     for h in range(2):
         ts(f("T3", 16 * h, 16 * h + 16), f("DI4", 16 * h, 16 * h + 16), -1.0, OP.mult, f("sb"), OP.add)
-    aff(f("T3", 16, 32), f("T3", 16, 32), 1.0, 128.0)
+    move(f("T3", 16, 32), f("T3", 16, 32), 1.0, 128.0)
     ts(f("T4", 0, 32), d, 8.0, OP.is_gt)
     tt(f("T1", 0, 32), f("T3", 0, 32), f("T4", 0, 32), OP.mult)
     ts(f("T5", 0, 32), d, 0.0, OP.is_equal, 1024.0, OP.mult)
@@ -343,9 +385,9 @@ def rank_program(g, core, T, topo):
     cp(f("OUT"), f("T4", 0, 32))
     fill(f("T1", 0, 34, 33), 1024.0)
     for h in range(2):
-        act(f("T1", 1 + h, 33, 2), f("T4", 16 * h, 16 * h + 16))
+        move(f("T1", 1 + h, 33, 2), f("T4", 16 * h, 16 * h + 16))
     tt(f("T2", 0, 33), f("T1", 0, 33), f("T1", 1, 34), OP.subtract)
-    act(f("T3", 0, 33), f("T2", 0, 33), AF.Copy, e)
+    move(f("T3", 0, 33), f("T2", 0, 33), e)
     tt(f("T5", 0, 33), f("T3", 0, 33), f("T1", 1, 34), OP.add)
     cp(f("EXP", 0, 33), f("T5", 0, 33))
     for b in range(4):
@@ -353,94 +395,112 @@ def rank_program(g, core, T, topo):
 
     quant("UQ", "US", 0, 128, f("UT"))
     cp(f("UQR", cast=dt.uint32), f("UQ", cast=dt.uint32, ind=("UL",)))
-    act(f("USR"), f("US", ind=("UL",)))
+    move(f("USR"), f("US", ind=("UL",)))
     ts(f("NDD"), f("NDI", ind=("NDL",)), 4.0, OP.mult)
     tt(f("NDM"), f("NDD"), f("ISO"), OP.mult)
     tt(f("NWI"), f("NDM"), f("DUM"), OP.add)
     turn(f("NW"), f("NWI"))
-    cp(f("N4"), f("NW", ind=("SPG",)))
+    move(f("N4"), f("NW", ind=("SPG",)))
     ts(f("SL"), f("N4"), 0.25, OP.mult)
     for io in range(2):
         tt(f("CC", 64 * io, 64 * io + 64), f("CB", 64 * io, 64 * io + 64), f("NDM"), OP.add)
-    act(f("NDD", 0, 32), f("N4"), AF.Copy, 2.0 ** -24)
-    act(f("NWI"), f("NW"), AF.Copy, 2.0 ** -24)
+    move(f("NDD", 0, 32), f("N4"), 2.0 ** -24)
+    move(f("NWI"), f("NW"), 2.0 ** -24)
     for h in range(2):
         a, b = f("KT", 104 + 17 * h, 120 + 17 * h), f("KT", 140 + 33 * h, 172 + 33 * h)
         tt(a, a, f("NDD", 16 * h, 16 * h + 16), OP.add)
         tt(b, b, f("NWI", 32 * h, 32 * h + 32), OP.add)
-    ts(f("ARB"), f("ARI"), U, OP.mult)
-    act(f("TA", 2, 768, 3), f("ARB", ind=("CIRC",)))
+    for h in range(2):
+        ts(f("ARB", 256 * h, 256 * h + 256), f("ARI", 256 * h, 256 * h + 256), U, OP.mult)
+    move(f("TA", 2, 768, 3), f("ARB", ind=("CIRC",)))
 
     nxt = T.cores[(rank + 1) % len(T.cores)]
     rid, pid, _ = topo.addr(nxt)
     engines = topo.engines(core, nxt)[:8]
     mask = sum(1 << k for k in engines)
 
-    def send(t):
-        q, s = f("SQ%d" % t, 0, 64, cast=dt.uint8), f("SS%d" % t, 0, 64)
-        lq, ls = f("LQ%d" % t, 0, 64, cast=dt.uint8), f("LS%d" % t, 0, 64)
+    def send(t, j):
+        a, b = 224 * j, 128 * j
+        q, s = f("SQ%d" % t, a, a + 32, cast=dt.uint8), f("SS%d" % t, a, a + 32)
+        lq, ls = f("LQ%d" % t, b, b + 32, cast=dt.uint8), f("LS%d" % t, b, b + 32)
+        sem = "arr%d" % (2 * t + j)
 
         def go(e):
-            e.remote_dma(lq[0], q[0], T.sem["arr%d" % t], T.sem["left"], pid, rid, mask)
-            e.remote_dma(ls[0], s[0], T.sem["arr%d" % t], T.sem["left"], pid, rid, mask)
-            return "arr%d" % t, 2 * len(engines)
-        note("p", go, [lq, ls], [q, s], 0.6 if t else 2.6, 2.2, "send")
+            e.remote_dma(lq[0], q[0], T.sem[sem], T.sem["left"], pid, rid, mask)
+            e.remote_dma(ls[0], s[0], T.sem[sem], T.sem["left"], pid, rid, mask)
+            return sem, 2 * len(engines)
+        note({"p": (go, 0.6 if t or j else 2.1)}, [lq, ls], [q, s], 1.5, "send")
 
     def table():
-        act(f("TA", 768, 1024), f("TA", 2, 768, 3), AF.Copy, -1.0)
-        act(f("EX"), f("TA", ind=("EXP", 0, 33)))
+        move(f("TA", 768, 1024), f("TA", 2, 768, 3), -1.0)
+        for a, b in ((0, 16), (16, 33)):
+            move(f("EX", 16 * a, 16 * b), f("TA", ind=("EXP", a, b)))
         for h in range(2):
-            turn(f("TAB", 32 + 544 * h, 544 + 544 * h), f("EX", 16 * h, 16 * h + 512))
+            lo = 32 + 544 * h
+            for a in range(2):
+                turn(f("TAB", lo + 256 * a, lo + 256 * a + 256), f("EX", 16 * h + 256 * a, 16 * h + 256 * a + 256))
+            for a in range(2):
+                o, i = f("TAM", lo + 256 * a, lo + 256 * a + 256), f("TAB", lo + 256 * a, lo + 256 * a + 256)
+                note({"v": v_ts(o, i, 0.0, OP.not_equal, BIG, OP.mult), "s": s_act(o, i, AF.Abs, 8 * BIG)}, [o], [i])
 
-    def choose(j, src):
+    def choose(j, flags):
         n, at = (16, 0) if j == 0 else (32, 36)
-        for h in range(2):
-            a = at + (n + 1) * h + 1
-            scan(f("RX", a, a + n), src(h), src(h), -2 * BIG, OP.max, OP.max)
         w = 2 * n + 1
-        tt(f("FL", at, at + w), f("RX", at + 1, at + w + 1), f("RX", at, at + w), OP.is_gt)
+        flags(f("FL", at, at + w))
         scan(f("SE", at, at + w), f("FL", at, at + w), f("KT", at, at + w), 0.0, OP.max, OP.min)
         for k, s in enumerate("AB"):
             ts(f("L4", 4 * j + k, 4 * j + 4, 2), f("SE", at + n - 1, at + w, n + 1), f(s), OP.mult)
         scan(f("SK", at, at + w), f("FL", at, at + w), f("KT", 104 + at, 104 + at + w), 0.0, OP.max, OP.min)
-        act(f("RK%d" % j, 4 * KS + 32, 4 * KS + 65, 32), f("SK", at + n - 1, at + w, n + 1), AF.Copy, 2.0 ** 24)
+        move(f("RA%d" % j, 2 * KS + 32, 2 * KS + 65, 32), f("SK", at + n - 1, at + w, n + 1), 2.0 ** 24)
 
-    def slots(j, ft):
-        gk, ky, rk = "GK%d" % j, "KY%d" % j, "RK%d" % j
+    def slots(j, t):
+        ft, gk, ky, ra, rc = "F%d" % t, "GK%d" % j, "KY%d" % j, "RA%d" % j, "RC%d" % j
         l4 = ("L4", 4 * j, 4 * j + 4)
+        sides = ((0, OP.min, OP.max, BIG), (1, OP.max, OP.min, -BIG))
         for io in range(2):
             tt(f(gk, 64 * io, 64 * io + 64), f("TAB", ind=l4), f("CC", 64 * io, 64 * io + 64), OP.add)
         for io in range(2):
             turn(f(ky, 64 * io, 64 * io + 64), f(gk, 64 * io, 64 * io + 64))
-        for io, a, b, big in ((0, OP.min, OP.max, BIG), (1, OP.max, OP.min, -BIG)):
+        for io, a, b, big in sides:
             k = f(ky, 64 * io, 64 * io + 64)
-            scan(f(rk, KS * io + 1, KS * io + 65), k, k, big, a, a)
-            scan(f(rk, KS * (io + 2) + 1, KS * (io + 2) + 65), k, f(rk, KS * io, KS * io + 64), big, a, b)
-        lo = 48 * j
-        tt(f("DI", lo, lo + 48), f(rk, ind=("DL", 0, 3)), f("BP"), OP.add)
-        ts(f("DM", lo, lo + 48), f("DI", lo, lo + 48), 4095, OP.bitwise_and)
-        cp(f("LL", lo, lo + 48), f("DM", lo, lo + 48))
-        y = 384 * j
+            scan(f(ra, KS * io + 1, KS * io + 65), k, k, big, a, a)
+        for io, a, b, big in sides:
+            scan(f(rc, KS * io + 1, KS * io + 65), f(ky, 64 * io, 64 * io + 64), f(ra, KS * io, KS * io + 64), big, a, b)
+        for src, lo, n in ((ra, 48 * j, 32), (rc, 48 * j + 32, 16)):
+            tt(f("DI", lo, lo + n), f(src, ind=("DL", 0, n // 16)), f("BP", 0, n), OP.add)
+            ts(f("DM", lo, lo + n), f("DI", lo, lo + n), 4095, OP.bitwise_and)
+            cp(f("LL", lo, lo + n), f("DM", lo, lo + n))
+        lo, y = 48 * j, 384 * j
         for io in range(2):
             ab = f("AB", 256 * j + 128 * io, 256 * j + 128 * io + 128)
-            act(ab, f(ft, ind=("LL", lo + 8 * io, lo + 8 * io + 8)))
-            tt(f("D0Y", y + 1 + io, y + 384, 3), f(ft, ind=("LL", lo + 16 + 8 * io, lo + 24 + 8 * io)), ab, OP.add)
-        act(f("D1Y", y + 2, y + 384, 3), f(ft, ind=("LL", lo + 32, lo + 40)), AF.Copy, -2.0)
+            move(ab, f(ft, ind=("LL", lo + 8 * io, lo + 8 * io + 8)))
+            tt(f("D0Y", y + 1 + io, y + 384, 3), f(ft, ind=("LL", lo + 32 + 8 * io, lo + 40 + 8 * io)), ab, OP.add)
+        move(f("D1Y", y + 2, y + 384, 3), f(ft, ind=("LL", lo + 16, lo + 24)), -2.0)
         scan(f("YS", y, y + 384), f("D0Y", y, y + 384), f("D1Y", y, y + 384), 0.0, OP.max, OP.add)
         for b in range(4):
-            o, i = f("YT", 128 * j + b, 128 * j + 128, 4), f("YS", y + 96 * b + 2, y + 96 * b + 96, 3)
-            if j == 1 and b % 2:
-                ts(o, i, 0.5, OP.mult)
-            else:
-                act(o, i, AF.Copy, 0.5)
+            move(f("YT", 512 * j + b, 512 * j + 128, 4), f("YS", y + 96 * b + 2, y + 96 * b + 96, 3), 0.5)
+        quant("SQ%d" % t, "SS%d" % t, 128 * j, 128 * j + 128, f("YT", 128 * j, 128 * j + 512))
+        send(t, j)
+        move(f("YW", 128 * j, 128 * j + 128), f("YS", y + 2, y + 384, 3), 16.0)
+
+    def anew(j, t):
+        lq, ls = "LQ%d" % t, "LS%d" % t
+        for b in range(4):
+            at = (0, 512, 3072, 3584)[b]
+            lo = 128 * j + 32 * b
+            mm(f("PS", at, at + 128), f("WQ", 128 * b, 128 * b + 128), f("WS", 128 * b, 128 * b + 128), f(lq, 32 * j, 32 * j + 128), f(ls, 32 * j, 32 * j + 128))
+            tt(f("V32", lo, lo + 32), f("PS", at + 96 * j, at + 96 * j + 32), f("YW", lo, lo + 32), OP.add)
+        move(f("VV", 128 * j, 128 * j + 128), f("V32", 128 * j, 128 * j + 128), 0.03125)
+        cp(f("F%d" % t, ind=("LL", 48 * j + 16, 48 * j + 24)), f("VV", 128 * j, 128 * j + 128))
 
     def operands(j, d0, d1):
         x = f("X2", 64 * j, 64 * j + 64)
-        act(f("XG", 64 * j, 64 * j + 64), f("TAB", ind=("L4", 4 * j, 4 * j + 4)))
+        move(f("XG", 64 * j, 64 * j + 64), f("TAB", ind=("L4", 4 * j, 4 * j + 4)))
         turn(x, f("XG", 64 * j, 64 * j + 64))
-        act(f("SP%d" % j, 0, 256, 8), f("X2", 64 * j, 64 * j + 64, ind=("SPG",)))
-        act(f(d0, 2, 768, 3), f("X2", 64 * j, 64 * j + 64, ind=("COLG",)), AF.Copy, 0.5 / U)
-        act(f(d0, 1, 768, 3), f(d0, 2, 768, 3), AF.Sign, -1.0)
+        move(f("SP%d" % j, 0, 256, 8), f("X2", 64 * j, 64 * j + 64, ind=("SPG",)), -0.5)
+        move(f(d0, 2, 768, 3), f("X2", 64 * j, 64 * j + 64, ind=("COLG",)), 1.0 / U)
+        o, i = f(d0, 1, 768, 3), f(d0, 2, 768, 3)
+        note({"v": v_ts(o, i, 1.0, OP.min, -1.0, OP.max), "s": s_act(o, i, AF.Sign)}, [o], [i])
         scan(f(d1, 0, 768, 3), f("KEEP"), f("SP%d" % j), 0.0, OP.mult, OP.add)
         act(f(d1, 1, 768, 3), f(d1, 0, 768, 3), AF.Abs)
 
@@ -448,6 +508,12 @@ def rank_program(g, core, T, topo):
         for h in range(2):
             lo, hi = 384 * h, 384 * h + 384
             scan(f(dst, lo, hi), f(d0, lo, hi), f(src, lo, hi), 0.0, OP.mult, OP.add)
+
+    def rise_of_second(out):
+        for h in range(2):
+            s = f("S2", 32 * h, 32 * h + 32)
+            scan(f("RX", 33 * h + 1, 33 * h + 33), s, s, 2 * BIG, OP.min, OP.min)
+        tt(out, f("RX", 1, 66), f("RX", 0, 65), OP.is_lt)
 
     for t in range(R):
         ft, xq, xs = "F%d" % t, "XQ%d" % t, "XS%d" % t
@@ -458,34 +524,34 @@ def rank_program(g, core, T, topo):
             mm(f("PS", 512 * a, 512 * a + 256), f("UQR"), f("USR"), f(xq, 256 * a, 256 * a + 256), f(xs, 256 * a, 256 * a + 256))
         for a in range(2):
             if t:
-                tt(f("PW", 256 * a, 256 * a + 256), f("PS", 512 * a, 512 * a + 256), f("CM", 256 * a, 256 * a + 256), OP.mult)
+                tt(f("PW", 256 * a, 256 * a + 256), f("PS", 512 * a, 512 * a + 256), f("CM", 256 * a, 256 * a + 256), OP.add)
             else:
-                act(f("PW", 256 * a, 256 * a + 256), f("PS", 512 * a, 512 * a + 256))
+                move(f("PW", 256 * a, 256 * a + 256), f("PS", 512 * a, 512 * a + 256))
         for h in range(2):
             o, i = f("SG", 256 * h, 256 * h + 256), f("PW", ind=("SL", 16 * h, 16 * h + 16))
             if t:
-                act(o, i)
+                move(o, i)
             else:
-                tt(o, i, f("OWN", 0, 256), OP.mult)
-            scan(f("Z", 256 * h, 256 * h + 256), f("FOLD"), o, 0.0, OP.mult, OP.add)
+                tt(o, i, f("OWN", 0, 256), OP.add)
+            scan(f("RB", 272 * h + 16, 272 * h + 272), o, o, -2 * BIG, OP.max, OP.max)
+        for h in range(2):
+            scan(f("Z", 256 * h, 256 * h + 256), f("FOLD"), f("SG", 256 * h, 256 * h + 256), 0.0, OP.min, OP.max)
         for b in range(4):
             mm(f("PS", 1024 + 512 * b, 1536 + 512 * b), f("EQ", 128 * b, 128 * b + 128), f("ES", 128 * b, 128 * b + 128), f(xq), f(xs))
             for a in range(2):
-                act(f(ft, 1024 * a + b, 1024 * a + 1024, 4), f("PS", 1024 + 512 * b + 256 * a, 1280 + 512 * b + 256 * a))
-        choose(0, lambda h: f("Z", 256 * h + 15, 256 * h + 256, 16))
-        ts(f("GM"), f("TAB", ind=("L4", 0, 4)), 0.0, OP.not_equal, -BIG, OP.mult)
-        turn(f("GMT"), f("GM"))
-        act(f("ZW"), f("Z", ind=("ZWL",)))
-        tt(f("S2"), f("ZW"), f("GMT"), OP.add)
-        choose(1, lambda h: f("S2", 32 * h, 32 * h + 32))
-        slots(0, ft)
-        slots(1, ft)
-        quant("SQ%d" % t, "SS%d" % t, 0, 128, f("YT"))
-        send(t)
+                move(f(ft, 1024 * a + b, 1024 * a + 1024, 4), f("PS", 1024 + 512 * b + 256 * a, 1280 + 512 * b + 256 * a))
+        choose(0, lambda o: tt(o, f("RB", 31, 544, 16), f("RB", 15, 528, 16), OP.is_gt))
+        move(f("ZW"), f("Z", ind=("ZWL",)))
+        turn(f("ZL"), f("ZW"))
+        tt(f("GM"), f("TAM", ind=("L4", 0, 4)), f("ZL"), OP.subtract)
+        turn(f("S2"), f("GM"))
+        choose(1, rise_of_second)
+        slots(0, t)
+        slots(1, t)
         if t == 0:
             for i in range(R):
-                dma("y", f("LQ%d" % i, 64, 128, cast=dt.uint8), f("SQ0", 64, 128, cast=dt.uint8))
-                dma("y", f("LS%d" % i, 64, 128), f("SS0", 64, 128))
+                dma("y", f("LQ%d" % i, 32, 128, cast=dt.uint8), f("SQ0", 32, 128, cast=dt.uint8))
+                dma("y", f("LS%d" % i, 32, 128), f("SS0", 32, 128))
             cp(f("CM", ind=("SL",)), f("OWN"))
         operands(0, "D0F", "TA")
         steps("TB", "D0F", "TA")
@@ -494,23 +560,18 @@ def rank_program(g, core, T, topo):
         ts(f("TD", 0, 768, 3), f("TC", 2, 768, 3), 3.0 * U, OP.min, -3.0 * U, OP.max)
         ts(f("DD"), f("X2"), MARK, OP.is_equal, -2.0, OP.mult)
         tt(f("SN"), f("DD", 0, 64), f("DD", 64, 128), OP.add)
-        aff(f("SPX", 0, 256, 8), f("SN", ind=("SPG",)), 1.0, 1.0)
-        aff(f("D0X", 1, 768, 3), f("SN", ind=("COLG",)), 1.0, 1.0)
+        move(f("SPX", 0, 256, 8), f("SN", ind=("SPG",)), 1.0, 1.0)
+        move(f("D0X", 1, 768, 3), f("SN", ind=("COLG",)), 1.0, 1.0)
         scan(f("D0X", 2, 768, 3), f("KEEP"), f("SPX"), 0.0, OP.mult, OP.add)
         steps("TA", "D0X", "TD")
         if t == R - 1:
             fill(f("TA", 1024, 1040), 0.0)
-            act(f("TA", 768, 1024), f("TA", 2, 768, 3), AF.Copy, -1.0)
-            act(f("OAO"), f("TA", ind=("OUT",)), AF.Copy, 1.0 / U)
-            dma("y", hbm(T.oa[:, :]), f("OAO"))
-        cp(f("KL"), f("DM", ind=("KLL", 0, 1)))
-        act(f("YW"), f("YT", 0, 256), AF.Copy, 32.0)
-        for b in range(4):
-            at = (0, 512, 3072, 3584)[b]
-            mm(f("PS", at, at + 128), f("WQ", 128 * b, 128 * b + 128), f("WS", 128 * b, 128 * b + 128), f("LQ%d" % t), f("LS%d" % t))
-            tt(f("V32", 64 * b, 64 * b + 64), f("PS", at, at + 64), f("YW", b, 256, 4), OP.add)
-        ts(f("VV"), f("V32"), 0.03125, OP.mult)
-        cp(f(ft, ind=("KL",)), f("VV"))
+            move(f("TA", 768, 1024), f("TA", 2, 768, 3), -1.0)
+            for a in range(2):
+                move(f("OAO", 256 * a, 256 * a + 256), f("TA", ind=("OUT", 16 * a, 16 * a + 16)), 1.0 / U)
+            dma("y", hbm(T.oa[:, :]), f("OAO"), 2.0)
+        anew(0, t)
+        anew(1, t)
 
     quant("VQ", "VS", 0, 128, f("VT"))
     for a in range(2):
@@ -518,10 +579,8 @@ def rank_program(g, core, T, topo):
         quant("XQ3", "XS3", lo, hi, f("F2", 1024 * a, 1024 * a + 1024))
         mm(f("PS", 512 * a, 512 * a + 256), f("VQ"), f("VS"), f("XQ3", lo, hi), f("XS3", lo, hi))
         dma("y", hbm(T.oc[:, 4 * lo:4 * hi]), f("XQ3", lo, hi, cast=dt.uint8))
-    act(f("YO", 0, 256), f("PS", 0, 256))
-    dma("s", hbm(T.y[:, 0:256]), f("YO", 0, 256))
-    cp(f("YO", 256, 512), f("PS", 512, 768))
-    dma("y", hbm(T.y[:, 256:512]), f("YO", 256, 512))
+        move(f("YO", lo, hi), f("PS", 2 * lo, 2 * lo + 256))
+        dma("ys", hbm(T.y[:, lo:hi]), f("YO", lo, hi), 1.6)
     for k in range(4):
-        dma("s" if k % 2 else "y", hbm(T.osc[4 * k:4 * k + 4, :]), (T.XS3[32 * k:32 * k + 4, 0:512], [("XS3", 0, 512, 1)]))
+        dma("ys", hbm(T.osc[4 * k:4 * k + 4, :]), (T.XS3[32 * k:32 * k + 4, 0:512], [("XS3", 0, 512, 1)]))
     issue()

@@ -12,15 +12,14 @@ KS = 66
 CODES, PLANE, BF, F32, I32, U16 = "float8_e4m3fn_x4", "uint8", "bfloat16", "float32", "int32", "uint16"
 SCRATCH = {"PS": ("psum", [128, 4096], F32)}
 for _n, _w, _d in (
-    ("XT", 2048, BF), ("UT", 512, BF), ("VT", 512, BF), ("ET", 528, BF), ("ONE", 528, BF),
+    ("XT", 2048, BF), ("UT", 512, BF), ("VT", 512, BF), ("ET", 528, BF), ("ONE", 528, BF), ("ID", 128, BF),
     ("UQ", 128, CODES), ("US", 128, PLANE), ("UQR", 128, CODES), ("USR", 128, PLANE), ("VQ", 128, CODES), ("VS", 128, PLANE),
-    ("WQ", 512, CODES), ("WS", 512, PLANE), ("EQ", 512, CODES), ("ES", 512, PLANE),
-    ("NDI", 32, I32), ("ARI", 512, I32), ("ARB", 512, BF), ("IA", 160, I32), ("FA", 1280, F32), ("SC", 32, F32), ("KT", 208, F32),
-    ("KI", 256, BF), ("OWN", 512, BF), ("CM", 512, BF), ("FOLD", 256, BF), ("KEEP", 256, BF),
+    ("WQ", 512, CODES), ("WS", 512, PLANE), ("EQ", 512, CODES), ("ES", 512, PLANE), ("LQ", 320, CODES), ("LS", 320, PLANE),
+    ("NDI", 32, I32), ("ARI", 512, I32), ("IA", 160, I32), ("FA", 1600, F32), ("SC", 32, F32), ("KT", 136, F32),
+    ("OWN", 512, BF), ("CM", 512, BF), ("FOLD", 256, BF), ("KEEP", 256, BF),
     ("UL", 8, U16), ("SL", 32, U16), ("SM", 32, U16), ("CIRC", 16, U16), ("COLG", 16, U16), ("EXP", 34, U16), ("OUT", 32, U16),
-    ("PW", 512, F32), ("SG", 512, F32), ("Z", 528, F32), ("ZW", 64, F32), ("ZL", 64, F32), ("RB", 544, F32), ("RX", 72, F32),
-    ("FL", 104, F32), ("SE", 104, F32), ("SK", 104, F32),
-    ("L4", 8, U16), ("GM", 64, F32), ("S2", 64, F32), ("TAB", 1120, BF), ("TAM", 1120, BF), ("EX", 528, BF),
+    ("PW", 512, F32), ("SG", 512, F32), ("Z", 528, F32), ("ZW", 64, F32), ("RX", 136, F32), ("FL", 136, F32), ("SK", 136, F32),
+    ("IX", 4, F32), ("JK", 208, BF), ("L4", 8, U16), ("GM", 64, BF), ("GT", 64, BF), ("S2", 64, F32), ("TAB", 1120, BF), ("EX", 528, BF),
     ("GK0", 128, F32), ("GK1", 128, F32), ("KY0", 128, F32), ("KY1", 128, F32),
     ("RA0", 4 * KS, F32), ("RA1", 4 * KS, F32), ("RC0", 2 * KS, F32), ("RC1", 2 * KS, F32),
     ("DI", 96, I32), ("DM", 96, I32), ("LL", 96, U16),
@@ -28,20 +27,19 @@ for _n, _w, _d in (
     ("XG", 128, BF), ("X2", 128, BF), ("DD", 128, BF), ("SN", 64, BF), ("SP0", 256, BF), ("SP1", 256, BF), ("SPX", 256, BF),
     ("D0F", 768, BF), ("D0S", 768, BF), ("D0X", 768, BF), ("TA", 1040, BF), ("TB", 768, BF), ("TC", 768, BF), ("TD", 768, BF),
     ("OAO", 512, F32), ("YO", 512, F32),
-) + tuple(("F%d" % t, W, BF) for t in range(R)) \
-  + tuple((n + "%d" % t, w, d) for t in range(R) for n, w, d in (("SQ", 256, CODES), ("SS", 256, PLANE), ("LQ", 160, CODES), ("LS", 160, PLANE))) \
+) + tuple(("F%d" % t, W, BF) for t in range(R)) + tuple((n + "%d" % t, 256, d) for t in range(R) for n, d in (("SQ", CODES), ("SS", PLANE))) \
   + tuple((n + "%d" % t, 512, d) for t in range(R + 1) for n, d in (("XQ", CODES), ("XS", PLANE))):
     SCRATCH[_n] = ("sbuf", [128, _w], _d)
 
-SEMAPHORES = ["cv", "cs", "ct", "cp", "left"] + ["arr%d" % t for t in range(2 * R)] + ["dm%d" % i for i in range(40)]
+SEMAPHORES = ["cv", "cs", "ct", "cp", "left"] + ["arr%d" % t for t in range(2 * R)] + ["dm%d" % i for i in range(32)]
 COUNTER = {"v": "cv", "s": "cs", "t": "ct", "p": "cp"}
 PART = {}
 for _b, _names in (
     ("IA", (("PI", 8), ("BITS", 8), ("DDI", 32), ("DI4", 32), ("JI", 16), ("JJ", 16))),
-    ("FA", (("N", 72), ("E64", 64), ("K32", 32), ("DU", 64), ("HE", 8), ("W1", 32), ("BP", 32), ("ISO", 64), ("NIS", 64), ("DUM", 64), ("CB", 128), ("CC", 128),
-            ("NDD", 64), ("NDM", 64), ("NWI", 64), ("NW", 64), ("N4", 32), ("T1", 40), ("T2", 40), ("T3", 40), ("T4", 40), ("T5", 40))),
-    ("SC", tuple((n, 1) for n in ("pm", "e", "p31", "qh", "ql", "h1", "A", "B", "e16", "kb0", "kb1", "sO", "sI", "pm16", "sb", "s1", "qh16", "t66",
-                                  "dl", "zb"))),
+    ("FA", (("N", 88), ("E64", 64), ("K32", 32), ("DU", 64), ("HE", 8), ("W1", 32), ("BP", 32), ("ISO", 64), ("NIS", 64), ("DUM", 64), ("CB", 128), ("CC", 128),
+            ("NDD", 64), ("NDM", 64), ("NWI", 64), ("NW", 64), ("N4", 32), ("NS", 32), ("NT", 64)) + tuple(("T%d" % i, 40) for i in range(10))),
+    ("SC", tuple((n, 1) for n in ("pm", "e", "p31", "qh", "ql", "h1", "A", "B", "nA", "nB", "e1", "pA", "pB", "pS", "zg", "e16", "sO", "sI", "pm16", "sb", "s1",
+                                  "qh16", "t66", "dl", "zb"))),
     ("SM", (("SPG", 2), ("DL", 2), ("NDL", 4), ("ZWL", 4))),
 ):
     _a = 0
@@ -50,57 +48,127 @@ for _b, _names in (
         _a += _w
 CYC = 0.00083
 WAKE = 0.2
-PLAN = {"seed": 217, "noise": 0.8, "hold": 2.0}
+PLAN = {"seed": 1, "passes": 120, "moves": 16000}
 
 
-def order(ops, seed, noise, hold):
+def order(ops, seed, passes, moves):
     n = len(ops)
-    tail = [0.0] * n
+    need = [o["need"] for o in ops]
     users = [[] for _ in ops]
-    for i, o in enumerate(ops):
-        for k in o["need"]:
-            users[k].append(i)
-    for i in range(n - 1, -1, -1):
-        tail[i] = min(a[1] for a in ops[i]["alt"].values()) + ops[i]["lat"] + max([tail[u] + WAKE for u in users[i]] + [0.0])
-    x = seed
-    rank = []
     for i in range(n):
-        x = (x * 1103515245 + 12345) % 2147483648
-        rank.append(tail[i] + noise * x / 2147483648.0)
-    free = {q: 0.0 for q in "vstpy"}
-    done = [0.0] * n
-    after = [0.0] * n
-    left = [len(o["need"]) for o in ops]
-    ready = [i for i in range(n) if not left[i]]
-    seq = []
-    while ready:
-        t0, q = min((max(free[k], after[i]), k) for i in ready for k in ops[i]["alt"])
-        mine = []
-        for i in ready:
-            alt = ops[i]["alt"]
-            if q in alt:
-                end = max(t0, after[i]) + alt[q][1]
-                if all(end <= max(free[k], after[i]) + alt[k][1] + 0.1 for k in alt):
-                    mine.append(i)
-        can = [i for i in mine if after[i] <= t0 + 0.01]
-        if not can:
-            free[q] = t0 + 0.05
-            continue
-        now = max(can, key=lambda i: rank[i])
-        d = ops[now]["alt"][q][1]
-        soon = [i for i in mine if rank[i] > rank[now] + d and hold * (after[i] - t0) < d]
-        if soon:
-            now = max(soon, key=lambda i: rank[i])
-        free[q] = max(t0, after[now]) + ops[now]["alt"][q][1]
-        done[now] = free[q] + ops[now]["lat"]
-        ready.remove(now)
-        seq.append((now, q))
-        for u in users[now]:
-            left[u] -= 1
-            after[u] = max(after[u], done[now] + WAKE)
-            if not left[u]:
-                ready.append(u)
-    return seq, max(done)
+        for k in need[i]:
+            users[k].append(i)
+    lat = [o["lat"] for o in ops]
+    dur = [{q: a[1] for q, a in o["alt"].items()} for o in ops]
+    state = [seed]
+
+    def rnd():
+        state[0] = (state[0] * 1103515245 + 12345) % 2147483648
+        return state[0] / 2147483648.0
+
+    def pick(xs):
+        return xs[int(rnd() * len(xs))]
+
+    def lay(rank, before, back, toll):
+        busy = {q: [] for q in "vstpy"}
+        start, end, on = [0.0] * n, [0.0] * n, [""] * n
+        for i in sorted(range(n), key=lambda k: rank[k]):
+            r = max([end[k] + WAKE + 0.03 for k in before[i]] + [0.0]) + (lat[i] if back else 0.0)
+            best = None
+            for q, d in dur[i].items():
+                b, t, lo, hi = busy[q], r, 0, len(busy[q])
+                while lo < hi:
+                    mid = (lo + hi) // 2
+                    if b[mid][1] <= t:
+                        lo = mid + 1
+                    else:
+                        hi = mid
+                while lo < len(b) and b[lo][0] < t + d - 1e-9:
+                    t = b[lo][1]
+                    lo += 1
+                e = t + d + (toll if q == "v" and len(dur[i]) > 1 else 0.0)
+                if best is None or e < best[0]:
+                    best = (e, t, q, d, lo)
+            busy[best[2]].insert(best[4], (best[1], best[1] + best[3]))
+            start[i], end[i], on[i] = best[1], best[1] + best[3] + (0.0 if back else lat[i]), best[2]
+        return start, end, on
+
+    def run(seq, on, wake, slow, trace=False):
+        free = {q: 0.0 for q in "vstpy"}
+        last = {q: -1 for q in "vstpy"}
+        done, why = [0.0] * n, [None] * n
+        for i in seq:
+            q = on[i]
+            s, w = free[q], (last[q], True)
+            for k in need[i]:
+                if done[k] + wake > s:
+                    s, w = done[k] + wake, (k, False)
+            why[i], last[q] = w, i
+            free[q] = s + dur[i][q] * slow
+            done[i] = free[q] + lat[i]
+        m = max(done)
+        if not trace:
+            return m
+        i, arcs = done.index(m), []
+        while i >= 0:
+            k, queued = why[i]
+            if queued and k >= 0:
+                arcs.append((k, i))
+            i = k
+        return arcs
+
+    def value(seq, on):
+        return run(seq, on, WAKE, 1.0) + 0.5 * run(seq, on, 1.4 * WAKE, 1.3)
+
+    def sound(p, before, ids):
+        for i in ids:
+            for k in before[i]:
+                if p[i] <= p[k]:
+                    p[i] = p[k] + 1e-6
+        return p
+
+    tail = [0.0] * n
+    for i in range(n - 1, -1, -1):
+        tail[i] = min(dur[i].values()) + lat[i] + max([tail[u] + WAKE for u in users[i]] + [0.0])
+    best, base = None, [-x for x in tail]
+    for it in range(passes):
+        toll, amp = pick((0.0, 0.1, 0.2, 0.4)), pick((0.05, 0.15, 0.3))
+        p = sound([x + amp * rnd() for x in base], need, range(n))
+        for rep in range(2):
+            start, end, on = lay(p, need, False, toll)
+            seq = sorted(range(n), key=lambda i: (start[i], i))
+            v = value(seq, on)
+            if best is None or v < best[0]:
+                best, base = (v, seq, on), start
+            end = lay(sound([-x for x in end], users, range(n - 1, -1, -1)), users, True, toll)[1]
+            p = sound([-x for x in end], need, range(n))
+    now, seq, on = best
+    arcs = run(seq, on, WAKE, 1.0, True)
+    for it in range(moves):
+        a, b = pick(arcs)
+        r = rnd()
+        seq2, on2 = seq, on
+        if r < 0.2 and len(dur[a]) + len(dur[b]) > 2:
+            x = a if len(dur[a]) > 1 and (len(dur[b]) == 1 or rnd() < 0.5) else b
+            on2 = list(on)
+            on2[x] = pick([q for q in dur[x] if q != on[x]])
+        else:
+            p = {x: y for y, x in enumerate(seq)}
+            early = r < 0.6
+            todo = [(b, p[a] - pick((0, 0, 2, 6, 15)) - 0.5)] if early else [(a, p[b] + pick((0, 0, 2, 6, 15, 40)) + 0.5)]
+            while todo:
+                x, v = todo.pop()
+                if p[x] > v if early else p[x] < v:
+                    p[x] = v
+                    todo += [(k, v - 1e-4) for k in need[x]] if early else [(k, v + 1e-4) for k in users[x]]
+            seq2 = sorted(seq, key=p.get)
+        v = value(seq2, on2)
+        if v <= now + 0.01 * rnd():
+            now, seq, on = v, seq2, on2
+            arcs = run(seq, on, WAKE, 1.0, True) if rnd() < 0.7 else run(seq, on, 1.4 * WAKE, 1.3, True)
+            if v < best[0]:
+                best = (v, seq, on)
+    return [(i, best[2][i]) for i in best[1]]
 
 
 def make_plan(g, T):
@@ -143,12 +211,12 @@ def make_plan(g, T):
             hist[name] = [h for h in hist.get(name, []) if not (lo <= h[0] and h[1] <= hi and (st == 1 or st == h[2] and (lo - h[0]) % st == 0))] + [(lo, hi, st, True, me)]
         for name, lo, hi, st in reads:
             hist.setdefault(name, []).append((lo, hi, st, False, me))
-        ops.append({"alt": alt, "need": sorted(need), "lat": lat, "kind": kind})
+        ops.append({"alt": alt, "need": sorted(need), "lat": lat, "kind": kind, "name": "%s%d" % outs[0][1][0][:2] if outs[0][1] else "out"})
 
     def issue():
         if "seq" not in PLAN:
             PLAN["ops"] = ops
-            PLAN["seq"] = order(ops, PLAN["seed"], PLAN["noise"], PLAN["hold"])[0]
+            PLAN["seq"] = order(ops, PLAN["seed"], PLAN["passes"], PLAN["moves"])
         count = {}
         known = {q: {} for q in eng}
         mark = {}
@@ -159,7 +227,8 @@ def make_plan(g, T):
                 eng[q].wait_ge(T.sem[sem], val)
 
         ndma = 0
-        for i, q in PLAN["seq"]:
+        loads = sorted(x for x in PLAN["seq"] if ops[x[0]]["kind"] == "load")
+        for i, q in loads + [x for x in PLAN["seq"] if ops[x[0]]["kind"] != "load"]:
             o = ops[i]
             fn = o["alt"][q][0]
             need = {}
@@ -172,15 +241,15 @@ def make_plan(g, T):
                 sem = COUNTER[q]
                 count[sem] = count.get(sem, 0) + 1
                 fn(eng[q]).then_inc(T.sem[sem], 1)
-            elif o["kind"] == "dma":
+            elif o["kind"] == "send":
+                sem, n = fn(eng[q])
+                count[sem] = n
+                count["left"] = count.get("left", 0) + n
+            else:
                 sem = "dm%d" % ndma
                 ndma += 1
                 count[sem] = 16
                 fn(eng[q]).then_inc(T.sem[sem], 16)
-            else:
-                sem, n = fn(eng[q])
-                count[sem] = n
-                count["left"] = count.get("left", 0) + n
             mark[i] = (sem, count[sem])
         for sem in count:
             wait("p", sem, count[sem])
@@ -249,6 +318,9 @@ def rank_program(g, core, T, topo):
             alt = {"v": v_cp(out, a), "s": s_act(out, a, AF.Copy)}
         note(alt, [out], [a] + cols(scale, bias))
 
+    def below(out, a, last, n):
+        note({"s": (lambda e: e.activation(out[0], a[0], AF.Sign, bias=last[0], scale=-1.0, accum_out=n[0]), cost("s", out, [a], 1.0) + 0.02)}, [out, n], [a, last])
+
     def fill(out, c):
         note({"v": (lambda e: e.memset(out[0], c), cost("v", out, [], rate(out)))}, [out], [])
 
@@ -278,55 +350,58 @@ def rank_program(g, core, T, topo):
         else:
             note({"p": (lambda e: e.iota(out[0], pattern, base, cm), 0.13 + 2 * CYC * out[2])}, [out], [])
 
-    def dma(q, out, in_, lat=1.3):
-        note({k: (lambda e: e.dma_start(out[0], in_[0]), 0.05) for k in q}, [out], [in_], lat, "dma")
+    def dma(q, out, in_, lat=1.3, kind="dma"):
+        note({k: (lambda e: e.dma_start(out[0], in_[0]), 0.05) for k in q}, [out], [in_], lat, kind)
 
     def hbm(ap):
         return (ap, [])
 
-    dma("y", f("NDI"), hbm(T.nd[:, :]))
-    dma("s", f("UT"), hbm(T.u[:, :]), 1.6)
-    dma("y", f("XT", 0, 1024), hbm(T.x[:, 0:1024]), 2.0)
-    dma("s", f("XT", 1024, 2048), hbm(T.x[:, 1024:2048]), 2.0)
-    dma("y", f("ARI"), hbm(T.ar[:, :]), 2.2)
-    dma("y", f("WQ", cast=dt.uint8), hbm(T.wc[:, :]), 2.5)
-    dma("y", f("WS"), hbm(T.ws[:, :]), 2.5)
-    dma("y", f("VT"), hbm(T.v[:, :]), 2.5)
+    dma("y", f("NDI"), hbm(T.nd[:, :]), 1.3, "load")
+    dma("s", f("UT"), hbm(T.u[:, :]), 1.7, "load")
+    dma("y", f("XT", 0, 1024), hbm(T.x[:, 0:1024]), 2.3, "load")
+    dma("s", f("XT", 1024, 2048), hbm(T.x[:, 1024:2048]), 2.8, "load")
+    dma("y", f("ARI"), hbm(T.ar[:, :]), 3.3, "load")
+    dma("y", f("WQ", cast=dt.uint8), hbm(T.wc[:, :]), 4.0, "load")
+    dma("y", f("WS"), hbm(T.ws[:, :]), 4.5, "load")
+    dma("y", f("VT"), hbm(T.v[:, :]), 5.0, "load")
 
     iota(f("PI", 0, 1), [[0, 1]], 0, 1, small=False)
-    iota(f("N"), [[1, 72]])
+    iota(f("N"), [[1, 88]])
     iota(f("E64"), [[0, 2], [1, 2], [0, 16]])
     iota(f("HE", 0, 4), [[1, 2], [0, 2]])
-    iota(f("KI"), [[0, 16], [1, 16]])
     iota(f("K32"), [[0, 2], [1, 16]])
     iota(f("DU"), [[64, 2], [0, 2], [4, 16]], 2048)
     iota(f("W1"), [[384, 2], [24, 16]], -1)
     iota(f("BP"), [[0, 4], [1, 4], [0, 2]])
     fill(f("ONE"), 1.0)
-    et, one = f("ET"), f("ONE")
-    note({"p": (lambda e: e.affine_select(et[0], one[0], [[-1, 528]], OP.is_equal, 0.0, 3, 4), 1.05)}, [et], [one])
+    ident, one = f("ID"), f("ONE", 0, 128)
+    note({"p": (lambda e: e.affine_select(ident[0], one[0], [[-1, 128]], OP.is_equal, 0.0, 0, 1), 0.38)}, [ident], [one])
+    const(f("ET"), 0.0)
+    move(f("ET", 3, 515, 4), ident)
     const(f("FOLD"), 2 * BIG)
     fill(f("FOLD", 0, 256, 16), -2 * BIG)
     const(f("KEEP"), 1.0)
     fill(f("KEEP", 0, 256, 8), 0.0)
     for t in range(R):
         const(f("F%d" % t, 2048, W), 0.0)
-    const(f("YT", 128, 512), 0.0)
+    const(f("YT", 0, 512), 0.0)
+    quant("LQ", "LS", 96, 224, f("YT", 0, 512))
     for a in (0, 544, 1088):
         const(f("TAB", a, a + 32), 0.0)
-        const(f("TAM", a, a + 32), 0.0)
     for n in ("SP0", "SP1", "SPX"):
         const(f(n), 0.0)
     for n, j in (("D0F", 0), ("D0S", 0), ("D0X", 0), ("TD", 1), ("TD", 2), ("TA", 0), ("TA", 1), ("D0Y", 0), ("D1Y", 1)):
         const(f(n, j, 768, 3), 0.0)
     const(f("D1Y", 0, 768, 3), -BIG)
     fill(f("TA", 1024, 1040), MARK)
-    fill(f("Z", 512, 528), -BIG / 32)
-    fill(f("RB", 15, 288, 272), -2 * BIG)
-    fill(f("RX", 0, 34, 33), 2 * BIG)
+    fill(f("Z", 512, 513), -BIG / 32)
+    fill(f("Z", 513, 528), -1.5 * BIG)
+    fill(f("RX", 0, 35), -2 * BIG)
+    fill(f("RX", 52, 103), 2 * BIG)
     for j in range(2):
         const(f("RA%d" % j), 0.0)
-        const(f("RC%d" % j), 0.0)
+        const(f("RC%d" % j, 0, 2 * KS, KS - 1), 0.0)
+        fill(f("RC%d" % j, KS, KS + 1), 0.0)
         fill(f("RA%d" % j, 0, 1), BIG)
         fill(f("RA%d" % j, KS, KS + 1), -BIG)
 
@@ -335,40 +410,40 @@ def rank_program(g, core, T, topo):
         ts(f("BITS", j, j + 1), pi, sh, OP.logical_shift_right, m, OP.bitwise_and)
     cp(f("SC", 0, 6), f("BITS", 0, 6))
     pm, e = f("pm"), f("e")
-    for n, src, sc, bi in (("A", "e", -4096.0, 4096.0), ("B", "e", 4096.0, 0.0), ("e16", "e", 16.0, 0.0), ("kb0", "p31", 1 / 4096.0, 32 / 4096.0),
-                           ("kb1", "p31", 1 / 4096.0, 576 / 4096.0), ("sO", "pm", -4096.0, 61440.0 - 67584.0), ("sI", "pm", 4096.0, 63488.0),
-                           ("pm16", "pm", 1.0, 16.0), ("sb", "pm", 8.0, 783.0), ("s1", "qh", 1.0, f("ql")), ("qh16", "qh", 16.0, 0.0),
-                           ("t66", "qh", float(KS), 32.0), ("dl", "h1", 32.0, f("t66")), ("zb", "pm", 16.0, -497.0)):
+    for n, src, sc, bi in (("A", "e", -32.0, 32.0), ("B", "e", 32.0, None), ("nA", "e", 32.0, -32.0), ("nB", "e", -32.0, None), ("e1", "e", -1.0, 1.0),
+                           ("pA", "p31", f("e1"), None), ("pB", "p31", e, None), ("pS", "e", -512.0, f("pB")), ("e16", "e", 16.0, None),
+                           ("sO", "pm", -4096.0, 61440.0 - 67584.0), ("sI", "pm", 4096.0, 63488.0), ("pm16", "pm", 1.0, 16.0), ("sb", "pm", 8.0, 783.0),
+                           ("s1", "qh", 1.0, f("ql")), ("qh16", "qh", 16.0, None), ("t66", "qh", float(KS), 32.0), ("dl", "h1", 32.0, f("t66")),
+                           ("zb", "pm", 16.0, -497.0)):
         move(f(n), f(src), sc, bi)
     ts(f("UL"), f("N", 0, 8), 16.0, OP.mult)
     ts(f("NDL"), f("HE", 0, 4), 16.0, OP.mult, pm, OP.add)
     ts(f("SPG"), f("N", 0, 64, 32), f("p31"), OP.add)
     ts(f("DL"), f("N", 0, 2), 2.0 * KS, OP.mult, f("dl"), OP.add)
     ts(f("ISO"), f("E64"), e, OP.is_equal)
-    move(f("NIS"), f("ISO"), -1.0, 1.0)
+    ts(f("NIS"), f("E64"), e, OP.not_equal)
     tt(f("DUM"), f("DU"), f("NIS"), OP.mult)
-    ts(f("OWN", 0, 256), f("KI"), pm, OP.not_equal, -BIG, OP.mult)
-    move(f("OWN", 256, 512), f("OWN", 0, 256))
+    ts(f("OWN", 0, 32), f("K32"), pm, OP.not_equal, -BIG, OP.mult)
+    for n in (32, 64, 128, 256):
+        move(f("OWN", n, 2 * n), f("OWN", 0, n))
     for h in range(2):
         move(f("CB", 32 * h, 32 * h + 32), f("ISO", 0, 32), f("sI"), (12 - 8 * h) * U - 63488.0)
         move(f("CB", 64 + 32 * h, 96 + 32 * h), f("ISO", 0, 32), f("sO"), (4 + 8 * h) * U + 67584.0)
-    move(f("T1", 0, 4), f("HE", 0, 4), 256.0, f("zb"))
-    tt(f("T1", 4, 8), f("T1", 0, 4), f("ISO", 0, 64, 16), OP.mult)
-    ts(f("ZWL"), f("T1", 4, 8), 512.0, OP.add)
-    move(f("KT", 0, 33), f("N", 0, 33), 32 / 4096.0, f("kb0"))
-    ts(f("T2", 0, 33), f("N", 0, 33), f("e16"), OP.subtract, -1.0, OP.max)
-    ts(f("T3", 0, 33), f("T2", 0, 33), 16.0, OP.min, 32 / 4096.0, OP.mult)
-    for h in range(2):
-        move(f("KT", 36 + 33 * h, 69 + 33 * h), f("T3", 0, 33), 1.0, f("kb%d" % h))
-    move(f("KT", 104, 137), f("N", 0, 33), 1 / 4096.0)
-    move(f("KT", 140, 206), f("N", 0, 66), 1 / 4096.0)
+    move(f("T6", 0, 4), f("HE", 0, 4), 256.0, f("zb"))
+    tt(f("T6", 4, 8), f("T6", 0, 4), f("ISO", 0, 64, 16), OP.mult)
+    ts(f("zg"), pm, 15.0, OP.not_equal, e, OP.mult)
+    move(f("T6", 8, 12), f("NIS", 0, 64, 16), f("zg"), 512.0)
+    tt(f("T6", 12, 16), f("T6", 4, 8), f("T6", 8, 12), OP.add)
+    cp(f("ZWL"), f("T6", 12, 16))
+    move(f("KT", 0, 50), f("N", 0, 50), 1 / 4096.0)
+    move(f("KT", 52, 134), f("N", 0, 82), 1 / 4096.0)
     ts(f("JI"), f("K32", 0, 32, 2), f("s1"), OP.add, 1.0, OP.add)
     ts(f("JJ"), f("JI"), 15, OP.bitwise_and)
     for h in range(2):
         ts(f("COLG", 8 * h, 8 * h + 8), f("JJ", 8 * h, 8 * h + 8), f("e16"), OP.add, 32.0 * h, OP.add)
-    move(f("T2", 0, 16), f("N", 0, 16), 32.0, f("qh16"))
-    tt(f("T2", 16, 32), f("T2", 0, 16), f("JJ"), OP.add)
-    cp(f("CIRC"), f("T2", 16, 32))
+    move(f("T7", 0, 16), f("N", 0, 16), 32.0, f("qh16"))
+    tt(f("T7", 16, 32), f("T7", 0, 16), f("JJ"), OP.add)
+    cp(f("CIRC"), f("T7", 16, 32))
     ts(f("DDI"), f("K32"), -1.0, OP.mult, f("pm16"), OP.add)
     ts(f("DI4"), f("DDI"), 15, OP.bitwise_and)
     d = f("DI4")
@@ -376,19 +451,19 @@ def rank_program(g, core, T, topo):
     tt(f("T2", 0, 32), f("T1", 0, 32), f("W1"), OP.add)
     for h in range(2):
         ts(f("T3", 16 * h, 16 * h + 16), f("DI4", 16 * h, 16 * h + 16), -1.0, OP.mult, f("sb"), OP.add)
-    move(f("T3", 16, 32), f("T3", 16, 32), 1.0, 128.0)
     ts(f("T4", 0, 32), d, 8.0, OP.is_gt)
-    tt(f("T1", 0, 32), f("T3", 0, 32), f("T4", 0, 32), OP.mult)
+    move(f("T3", 16, 32), f("T3", 16, 32), 1.0, 128.0)
+    tt(f("T8", 0, 32), f("T3", 0, 32), f("T4", 0, 32), OP.mult)
     ts(f("T5", 0, 32), d, 0.0, OP.is_equal, 1024.0, OP.mult)
-    tt(f("T3", 0, 32), f("T1", 0, 32), f("T5", 0, 32), OP.max)
-    tt(f("T4", 0, 32), f("T3", 0, 32), f("T2", 0, 32), OP.max)
-    cp(f("OUT"), f("T4", 0, 32))
-    fill(f("T1", 0, 34, 33), 1024.0)
+    tt(f("T0", 0, 32), f("T2", 0, 32), f("T5", 0, 32), OP.max)
+    tt(f("T1", 0, 32), f("T0", 0, 32), f("T8", 0, 32), OP.max)
+    cp(f("OUT"), f("T1", 0, 32))
+    fill(f("T9", 0, 34, 33), 1024.0)
     for h in range(2):
-        move(f("T1", 1 + h, 33, 2), f("T4", 16 * h, 16 * h + 16))
-    tt(f("T2", 0, 33), f("T1", 0, 33), f("T1", 1, 34), OP.subtract)
-    move(f("T3", 0, 33), f("T2", 0, 33), e)
-    tt(f("T5", 0, 33), f("T3", 0, 33), f("T1", 1, 34), OP.add)
+        move(f("T9", 1 + h, 33, 2), f("T1", 16 * h, 16 * h + 16))
+    move(f("T2", 0, 33), f("T9", 0, 33), e)
+    move(f("T3", 0, 33), f("T9", 1, 34), f("e1"))
+    tt(f("T5", 0, 33), f("T3", 0, 33), f("T2", 0, 33), OP.add)
     cp(f("EXP", 0, 33), f("T5", 0, 33))
     for b in range(4):
         quant("EQ", "ES", 128 * b, 128 * b + 128, f("ET", 3 - b, 515 - b))
@@ -404,25 +479,26 @@ def rank_program(g, core, T, topo):
     ts(f("SL"), f("N4"), 0.25, OP.mult)
     for io in range(2):
         tt(f("CC", 64 * io, 64 * io + 64), f("CB", 64 * io, 64 * io + 64), f("NDM"), OP.add)
-    move(f("NDD", 0, 32), f("N4"), 2.0 ** -24)
-    move(f("NWI"), f("NW"), 2.0 ** -24)
+    move(f("NS"), f("N4"), 2.0 ** -24)
+    move(f("NT"), f("NW"), 2.0 ** -24)
     for h in range(2):
-        a, b = f("KT", 104 + 17 * h, 120 + 17 * h), f("KT", 140 + 33 * h, 172 + 33 * h)
-        tt(a, a, f("NDD", 16 * h, 16 * h + 16), OP.add)
-        tt(b, b, f("NWI", 32 * h, 32 * h + 32), OP.add)
-    for h in range(2):
-        ts(f("ARB", 256 * h, 256 * h + 256), f("ARI", 256 * h, 256 * h + 256), U, OP.mult)
-    move(f("TA", 2, 768, 3), f("ARB", ind=("CIRC",)))
+        a, b = f("KT", 34 * h, 34 * h + 16), f("KT", 52 + 50 * h, 84 + 50 * h)
+        tt(a, a, f("NS", 16 * h, 16 * h + 16), OP.add)
+        tt(b, b, f("NT", 32 * h, 32 * h + 32), OP.add)
+    ts(f("TA", 2, 768, 3), f("ARI", ind=("CIRC",)), U, OP.mult)
 
     nxt = T.cores[(rank + 1) % len(T.cores)]
     rid, pid, _ = topo.addr(nxt)
     engines = topo.engines(core, nxt)[:8]
     mask = sum(1 << k for k in engines)
 
+    def landing(t, j):
+        return 224 + 32 * t if j else 64 - 32 * t
+
     def send(t, j):
-        a, b = 224 * j, 128 * j
+        a, b = 224 * j, landing(t, j)
         q, s = f("SQ%d" % t, a, a + 32, cast=dt.uint8), f("SS%d" % t, a, a + 32)
-        lq, ls = f("LQ%d" % t, b, b + 32, cast=dt.uint8), f("LS%d" % t, b, b + 32)
+        lq, ls = f("LQ", b, b + 32, cast=dt.uint8), f("LS", b, b + 32)
         sem = "arr%d" % (2 * t + j)
 
         def go(e):
@@ -439,19 +515,21 @@ def rank_program(g, core, T, topo):
             lo = 32 + 544 * h
             for a in range(2):
                 turn(f("TAB", lo + 256 * a, lo + 256 * a + 256), f("EX", 16 * h + 256 * a, 16 * h + 256 * a + 256))
-            for a in range(2):
-                o, i = f("TAM", lo + 256 * a, lo + 256 * a + 256), f("TAB", lo + 256 * a, lo + 256 * a + 256)
-                note({"v": v_ts(o, i, 0.0, OP.not_equal, BIG, OP.mult), "s": s_act(o, i, AF.Abs, 8 * BIG)}, [o], [i])
 
-    def choose(j, flags):
-        n, at = (16, 0) if j == 0 else (32, 36)
-        w = 2 * n + 1
-        flags(f("FL", at, at + w))
-        scan(f("SE", at, at + w), f("FL", at, at + w), f("KT", at, at + w), 0.0, OP.max, OP.min)
-        for k, s in enumerate("AB"):
-            ts(f("L4", 4 * j + k, 4 * j + 4, 2), f("SE", at + n - 1, at + w, n + 1), f(s), OP.mult)
-        scan(f("SK", at, at + w), f("FL", at, at + w), f("KT", 104 + at, 104 + at + w), 0.0, OP.max, OP.min)
-        move(f("RA%d" % j, 2 * KS + 32, 2 * KS + 65, 32), f("SK", at + n - 1, at + w, n + 1), 2.0 ** 24)
+    def choose(j, src):
+        n, at, op, big = (16, 0, OP.max, -2 * BIG) if j == 0 else (32, 52, OP.min, 2 * BIG)
+        for h in range(2):
+            a = at + 1 + (n + 18) * h
+            scan(f("RX", a, a + n), src(h), src(h), big, op, op)
+        for h in range(2):
+            lo, hi, junk = at + (n + 1) * h, at + n + 1 + (n + 18) * h, 52 * (2 * j + h)
+            below(f("JK", junk, junk + hi - lo), f("RX", lo, hi), f("RX", hi - 1, hi), f("IX", 2 * j + h, 2 * j + h + 1))
+        for k, (a, b) in enumerate(((("A", "pA"), ("B", "pB")), (("nA", "pA"), ("nB", "pS")))[j]):
+            ts(f("L4", 4 * j + k, 4 * j + 4, 2), f("IX", 2 * j, 2 * j + 2), f(a), OP.mult, f(b), OP.add)
+        w = 2 * n + 18
+        tt(f("FL", at, at + w), f("RX", at + 1, at + w + 1), f("RX", at, at + w), OP.is_lt if j else OP.is_gt)
+        scan(f("SK", at, at + w), f("FL", at, at + w), f("KT", at, at + w), 0.0, OP.max, OP.min)
+        move(f("RA%d" % j, 2 * KS + 32, 2 * KS + 65, 32), f("SK", at + n - 1, at + w, n + 18), 2.0 ** 24)
 
     def slots(j, t):
         ft, gk, ky, ra, rc = "F%d" % t, "GK%d" % j, "KY%d" % j, "RA%d" % j, "RC%d" % j
@@ -466,11 +544,12 @@ def rank_program(g, core, T, topo):
             scan(f(ra, KS * io + 1, KS * io + 65), k, k, big, a, a)
         for io, a, b, big in sides:
             scan(f(rc, KS * io + 1, KS * io + 65), f(ky, 64 * io, 64 * io + 64), f(ra, KS * io, KS * io + 64), big, a, b)
-        for src, lo, n in ((ra, 48 * j, 32), (rc, 48 * j + 32, 16)):
-            tt(f("DI", lo, lo + n), f(src, ind=("DL", 0, n // 16)), f("BP", 0, n), OP.add)
-            ts(f("DM", lo, lo + n), f("DI", lo, lo + n), 4095, OP.bitwise_and)
-            cp(f("LL", lo, lo + n), f("DM", lo, lo + n))
         lo, y = 48 * j, 384 * j
+        for src, a, n in ((ra, lo, 32), (rc, lo + 32, 16)):
+            tt(f("DI", a, a + n), f(src, ind=("DL", 0, n // 16)), f("BP", 0, n), OP.add)
+        for a, n in ((lo, 32), (lo + 32, 16)) if j else ((lo, 48),):
+            ts(f("DM", a, a + n), f("DI", a, a + n), 4095, OP.bitwise_and)
+            cp(f("LL", a, a + n), f("DM", a, a + n))
         for io in range(2):
             ab = f("AB", 256 * j + 128 * io, 256 * j + 128 * io + 128)
             move(ab, f(ft, ind=("LL", lo + 8 * io, lo + 8 * io + 8)))
@@ -484,11 +563,11 @@ def rank_program(g, core, T, topo):
         move(f("YW", 128 * j, 128 * j + 128), f("YS", y + 2, y + 384, 3), 16.0)
 
     def anew(j, t):
-        lq, ls = "LQ%d" % t, "LS%d" % t
+        c = landing(t, j) - 96 * j
         for b in range(4):
-            at = (0, 512, 3072, 3584)[b]
+            at = (0, 512, 3072, 3584)[b] if j == 0 else 1024 + 512 * b
             lo = 128 * j + 32 * b
-            mm(f("PS", at, at + 128), f("WQ", 128 * b, 128 * b + 128), f("WS", 128 * b, 128 * b + 128), f(lq, 32 * j, 32 * j + 128), f(ls, 32 * j, 32 * j + 128))
+            mm(f("PS", at, at + 128), f("WQ", 128 * b, 128 * b + 128), f("WS", 128 * b, 128 * b + 128), f("LQ", c, c + 128), f("LS", c, c + 128))
             tt(f("V32", lo, lo + 32), f("PS", at + 96 * j, at + 96 * j + 32), f("YW", lo, lo + 32), OP.add)
         move(f("VV", 128 * j, 128 * j + 128), f("V32", 128 * j, 128 * j + 128), 0.03125)
         cp(f("F%d" % t, ind=("LL", 48 * j + 16, 48 * j + 24)), f("VV", 128 * j, 128 * j + 128))
@@ -509,12 +588,6 @@ def rank_program(g, core, T, topo):
             lo, hi = 384 * h, 384 * h + 384
             scan(f(dst, lo, hi), f(d0, lo, hi), f(src, lo, hi), 0.0, OP.mult, OP.add)
 
-    def rise_of_second(out):
-        for h in range(2):
-            s = f("S2", 32 * h, 32 * h + 32)
-            scan(f("RX", 33 * h + 1, 33 * h + 33), s, s, 2 * BIG, OP.min, OP.min)
-        tt(out, f("RX", 1, 66), f("RX", 0, 65), OP.is_lt)
-
     for t in range(R):
         ft, xq, xs = "F%d" % t, "XQ%d" % t, "XS%d" % t
         src = "F%d" % (t - 1) if t else "XT"
@@ -533,25 +606,21 @@ def rank_program(g, core, T, topo):
                 move(o, i)
             else:
                 tt(o, i, f("OWN", 0, 256), OP.add)
-            scan(f("RB", 272 * h + 16, 272 * h + 272), o, o, -2 * BIG, OP.max, OP.max)
-        for h in range(2):
-            scan(f("Z", 256 * h, 256 * h + 256), f("FOLD"), f("SG", 256 * h, 256 * h + 256), 0.0, OP.min, OP.max)
-        for b in range(4):
-            mm(f("PS", 1024 + 512 * b, 1536 + 512 * b), f("EQ", 128 * b, 128 * b + 128), f("ES", 128 * b, 128 * b + 128), f(xq), f(xs))
-            for a in range(2):
-                move(f(ft, 1024 * a + b, 1024 * a + 1024, 4), f("PS", 1024 + 512 * b + 256 * a, 1280 + 512 * b + 256 * a))
-        choose(0, lambda o: tt(o, f("RB", 31, 544, 16), f("RB", 15, 528, 16), OP.is_gt))
+            scan(f("Z", 256 * h, 256 * h + 256), f("FOLD"), o, 0.0, OP.min, OP.max)
+        for a in range(2):
+            for b in range(4):
+                at = 1024 + 512 * b if a == 0 else (3072, 3584, 0, 512)[b]
+                mm(f("PS", at, at + 256), f("EQ", 128 * b, 128 * b + 128), f("ES", 128 * b, 128 * b + 128), f(xq, 256 * a, 256 * a + 256), f(xs, 256 * a, 256 * a + 256))
+                move(f(ft, 1024 * a + b, 1024 * a + 1024, 4), f("PS", at, at + 256))
+        choose(0, lambda h: f("Z", 256 * h + 15, 256 * h + 256, 16))
         move(f("ZW"), f("Z", ind=("ZWL",)))
-        turn(f("ZL"), f("ZW"))
-        tt(f("GM"), f("TAM", ind=("L4", 0, 4)), f("ZL"), OP.subtract)
-        turn(f("S2"), f("GM"))
-        choose(1, rise_of_second)
+        ts(f("GM"), f("TAB", ind=("L4", 0, 4)), 0.0, OP.not_equal, BIG, OP.mult)
+        turn(f("GT"), f("GM"))
+        tt(f("S2"), f("GT"), f("ZW"), OP.subtract)
+        choose(1, lambda h: f("S2", 32 * h, 32 * h + 32))
         slots(0, t)
         slots(1, t)
         if t == 0:
-            for i in range(R):
-                dma("y", f("LQ%d" % i, 32, 128, cast=dt.uint8), f("SQ0", 32, 128, cast=dt.uint8))
-                dma("y", f("LS%d" % i, 32, 128), f("SS0", 32, 128))
             cp(f("CM", ind=("SL",)), f("OWN"))
         operands(0, "D0F", "TA")
         steps("TB", "D0F", "TA")
@@ -574,13 +643,14 @@ def rank_program(g, core, T, topo):
         anew(1, t)
 
     quant("VQ", "VS", 0, 128, f("VT"))
-    for a in range(2):
-        lo, hi = 256 * a, 256 * a + 256
-        quant("XQ3", "XS3", lo, hi, f("F2", 1024 * a, 1024 * a + 1024))
-        mm(f("PS", 512 * a, 512 * a + 256), f("VQ"), f("VS"), f("XQ3", lo, hi), f("XS3", lo, hi))
-        dma("y", hbm(T.oc[:, 4 * lo:4 * hi]), f("XQ3", lo, hi, cast=dt.uint8))
-        move(f("YO", lo, hi), f("PS", 2 * lo, 2 * lo + 256))
-        dma("ys", hbm(T.y[:, lo:hi]), f("YO", lo, hi), 1.6)
+    for a in range(4):
+        lo, hi = 128 * a, 128 * a + 128
+        quant("XQ3", "XS3", lo, hi, f("F2", 512 * a, 512 * a + 512))
+        mm(f("PS", 512 * a, 512 * a + 128), f("VQ"), f("VS"), f("XQ3", lo, hi), f("XS3", lo, hi))
+        move(f("YO", lo, hi), f("PS", 4 * lo, 4 * lo + 128))
+        dma("ys", hbm(T.y[:, lo:hi]), f("YO", lo, hi))
+        if a % 2:
+            dma("ys", hbm(T.oc[:, 4 * lo - 512:4 * hi]), f("XQ3", lo - 128, hi, cast=dt.uint8))
     for k in range(4):
         dma("ys", hbm(T.osc[4 * k:4 * k + 4, :]), (T.XS3[32 * k:32 * k + 4, 0:512], [("XS3", 0, 512, 1)]))
     issue()

@@ -8,6 +8,7 @@ U = 131072.0
 MARK = 0.125
 BIG = 1.0e29
 KS = 66
+MID = W // 2
 
 CODES, PLANE, BF, F32, I32, U16 = "float8_e4m3fn_x4", "uint8", "bfloat16", "float32", "int32", "uint16"
 SCRATCH = {"PS": ("psum", [128, 4096], F32)}
@@ -15,13 +16,13 @@ for _n, _w, _d in (
     ("XT", 2048, BF), ("UT", 512, BF), ("VT", 512, BF), ("ET", 528, BF), ("ONE", 528, BF), ("ID", 128, BF),
     ("UQ", 128, CODES), ("US", 128, PLANE), ("UQR", 128, CODES), ("USR", 128, PLANE), ("VQ", 128, CODES), ("VS", 128, PLANE),
     ("WQ", 512, CODES), ("WS", 512, PLANE), ("EQ", 512, CODES), ("ES", 512, PLANE), ("LQ", 320, CODES), ("LS", 320, PLANE),
-    ("NDI", 32, I32), ("ARI", 512, I32), ("IA", 160, I32), ("FA", 1600, F32), ("SC", 32, F32), ("KT", 136, F32),
+    ("NDI", 32, I32), ("ARI", 512, I32), ("IA", 160, I32), ("FA", 1600, F32), ("SC", 32, F32), ("KT", 136, F32), ("KU", 136, F32), ("HI", 8, F32), ("B4", 4, F32),
     ("OWN", 512, BF), ("CM", 512, BF), ("FOLD", 256, BF), ("KEEP", 256, BF),
     ("UL", 8, U16), ("SL", 32, U16), ("SM", 32, U16), ("CIRC", 16, U16), ("COLG", 16, U16), ("EXP", 34, U16), ("OUT", 32, U16),
-    ("PW", 512, F32), ("SG", 512, F32), ("Z", 528, F32), ("ZW", 64, F32), ("RX", 136, F32), ("FL", 136, F32), ("SK", 136, F32),
+    ("PW", 512, F32), ("SG", 512, F32), ("Z", 528, F32), ("ZW", 64, F32), ("RX", 136, F32), ("RB", 816, F32), ("FL", 136, F32), ("SK", 136, F32),
     ("IX", 4, F32), ("JK", 208, BF), ("L4", 8, U16), ("GM", 64, BF), ("GT", 64, BF), ("S2", 64, F32), ("TAB", 1120, BF), ("EX", 528, BF),
     ("GK0", 128, F32), ("GK1", 128, F32), ("KY0", 128, F32), ("KY1", 128, F32),
-    ("RA0", 4 * KS, F32), ("RA1", 4 * KS, F32), ("RC0", 2 * KS, F32), ("RC1", 2 * KS, F32),
+    ("RA0", 6 * KS, F32), ("RA1", 4 * KS, F32), ("RC0", 2 * KS, F32), ("RC1", 2 * KS, F32),
     ("DI", 96, I32), ("DM", 96, I32), ("LL", 96, U16),
     ("AB", 512, BF), ("D0Y", 768, BF), ("D1Y", 768, BF), ("YS", 768, BF), ("YT", 640, BF), ("YW", 256, BF), ("V32", 256, BF), ("VV", 256, BF),
     ("XG", 128, BF), ("X2", 128, BF), ("DD", 128, BF), ("SN", 64, BF), ("SP0", 256, BF), ("SP1", 256, BF), ("SPX", 256, BF),
@@ -36,11 +37,11 @@ COUNTER = {"v": "cv", "s": "cs", "t": "ct", "p": "cp"}
 PART = {}
 for _b, _names in (
     ("IA", (("PI", 8), ("BITS", 8), ("DDI", 32), ("DI4", 32), ("JI", 16), ("JJ", 16))),
-    ("FA", (("N", 88), ("E64", 64), ("K32", 32), ("DU", 64), ("HE", 8), ("W1", 32), ("BP", 32), ("ISO", 64), ("NIS", 64), ("DUM", 64), ("CB", 128), ("CC", 128),
+    ("FA", (("N", 88), ("E64", 64), ("K32", 32), ("DU", 64), ("HE", 8), ("W1", 32), ("BP", 48), ("ISO", 64), ("NIS", 64), ("DUM", 64), ("CB", 128), ("CC", 128),
             ("NDD", 64), ("NDM", 64), ("NWI", 64), ("NW", 64), ("N4", 32), ("NS", 32), ("NT", 64)) + tuple(("T%d" % i, 40) for i in range(10))),
-    ("SC", tuple((n, 1) for n in ("pm", "e", "p31", "qh", "ql", "h1", "A", "B", "nA", "nB", "e1", "pA", "pB", "pS", "zg", "e16", "sO", "sI", "pm16", "sb", "s1",
+    ("SC", tuple((n, 1) for n in ("pm", "e", "p31", "qh", "ql", "h1", "A", "B", "e1", "p0", "p1", "zg", "e16", "sO", "sI", "sb", "s1",
                                   "qh16", "t66", "dl", "zb"))),
-    ("SM", (("SPG", 2), ("DL", 2), ("NDL", 4), ("ZWL", 4))),
+    ("SM", (("SPG", 2), ("DL", 4), ("DK", 2), ("NDL", 4), ("ZWL", 4))),
 ):
     _a = 0
     for _n, _w in _names:
@@ -48,6 +49,13 @@ for _b, _names in (
         _a += _w
 CYC = 0.00083
 WAKE = 0.2
+ORDER = "00y01s02y03s04y0hv3bv1ev1av08p1kv1nv1mv2yp0ap09p0bp1lv1ov0cp0ep1jv2zv0dp19v1cv18v1pv34v0ls0js1zs1ws20s1fv30v37v24v1yv29v1xs2js21s0up0ip2av26v25v2cv2rv2vs2hs32v33v31v0mv2sv2bv38v3pv35s23s2wv3mv2ds36v2is2gs3qv2xv2qp0wp3nv1dp0ks3rv39v2es2ks3os0vp1ts4bv3sv2fs0sp3ds3cs1rs4dv1ss3ts43v3xv3wv4ct3es3fs3uv3kv3gv3vv0fp4et3zv15p05y06y07y2mv2lv3hv4fs4gs1vs44s41s1us16p4hv4rt1gp0qp0xp4zt46s4kv4iv1qs2ns4lv3jv45s22s2ov0pp0gp0yp53s4av48v49v47v54s55v4ss4pt56v4qs4xt50s4ys27v3iv5lv11p5mv4nt0rp3lv2pv5nv4vt7ds4os4tt5ov57v5av58s0zp51t5pv13p5qv4jv5rv5sv4mv5tv3yv5bv52s4ws0ns59v10p5uv40v12p7ev1bv5vv5cv1hv1iv4us42s17v5dv7fs5ev5ws28v0ov5ys5fs5gs60s2uv0tv5xv5zv2tv7gs5iv5hv5jv61v69v5ks64s63s65s6av7iv6bv68s6cv62v7hs7js6dv6ev7ms66v6kv6fv6hv6nv6gv6lv6mv67p6qv6ov6pv6tv6iv6ws6rv6sv6uv6jv6vv6ys7nv85t6xv70s14p6zv7os7ps7wv7lv71v74s7kv75s73s72v79v7qs78s76v7rv77p7ss7avhnv7xv7ys7zs7tv7bv7uv86v87t88v89t8av83t84v7cv8bs8jt8kv8ft8gv8dt8ev8ht8iv8cv8ls80v7vv8mv81v8uv8wv82v8vt8xt8ns9gt8yv98t8zv9at9hs9it93s9kt9ct8os9js8pv90v99s9et8rv96t94v91v92v8tv8sv9ns8qv9ms9ov9pv95v9ds9bsbss9tva4v9ssa5v9uv9fsa6vbtv97sa7v9vv9qva8va9v9ls9wv9ys9xvbuvaav9rvabv9zs3avbxvacva1va0vbvsbysa2vadvc1sasvatvbwsa3vauvaevavvawvahsc2vaxvafsc4sayvb3vb6vazvb0vajsb9vaivb8vb4vb5vbcvb7vb1vagvbbvbdvbavb2vbfsbevbhsakvbgvbivbjscbvc0vamsalsansaosc5sc3sbkvapvbmsbnsaqpccvblvbovarscmtbzvcdscitcesbpvc6vcfvc7sbqpcktbrvc8vc9vcotcwtcutcavcnvcjvclvcpvcqschvcgvd2scxvcvvcytczvcstctvcrvd0vd1vd9vdbvdatdctd4sd6vd8vdrtd3sddvdttdvtdevdssd7vduvdntd5vdfvdisdztdltdxtdptdjvdosdgve0sdmse2sdkvdhve1se4ve3vdyse5vgxve8vekvejvg7se7se9vemvg8velveaveovg9ve6sdqsgasecveesenvebvedseqvgcvepvgbvervgdsegvefvehvesvf7vf8vetvdwsggsf9veisfavghvfbvfcvewseyseusgqvgjsfivfdvflvfevexvffvfnvfovfmvfjvfrvfgvfkvevvfqvftvfsvfpvfhvezvfwsfusfxvfvvgksfysf0sf2sf1vgfvf3sf6sfzvf4vf5ph3tgrvh9tg3vg0vgisg2sg1sh7tgevg6sgssgtsg4vglvguvgmsgnvgovg5ph5tgpvh4vhavh8vh6vgvvgwvhbshfthgvgyshhthivhdthevhjthkvhcvhlvhmvh1sgzsh2yhovhrvhuvhxvhpthsti0yhvti7shqvhyti1si6yi5yhtvh0yhwvhzvi2si3si8si4y"
+_OLD6 = "00y01s02y03s04y0hv08p19v2yp1fv1av1ds0ps1kv1ov1lv1mv1jv0cp09p1nv0ap0bp2zv0lv3bv1pv0js0ep30v1cv34v1ys0dp1zs37v0mv26v0wp2cv29v1xs0ip25v2av0up24v32v33v21s1ts31v2rv2ds3pv2bv3mv18v23s20s3qv2sv1ss35s36v2gs3nv2is2vs2es2qp0fp3rv4dv1rs1ws0ks3os2ks2fs2hs2js0sp05y4bv4et38v0vp3sv1ev2wv2mv1bv4gs06y39v2lv4ct3tv07y16p4fs2xv1gp3wv3vv15p0qp3ds3uv3cs17s3es3fs1vs2ns43v44s0ns4hv4kv3gv3jv0gp10p3xv0xp2ov11p3hv1qs22s1us3kv4jv4iv0yp4pt4xt0zp3zv46s14p45s53s4lv54s4mv4av48v49v47v55v4rt4zt56v2pv40v4ss3iv4ys13p5lv5mv5av3lv12p4qs41s4vt5nv4nt5ov5bv59s57v3yv50s7ds4ws0rp58s4tt51t5pv5qv4os4us5cv27v5rv5sv42v5ev5dv28v5tv2uv1iv0tv5uv5gs5fs0ov3av2tv52s7ev5vv1hv5hv5iv5jv7fs5wv5ys60s5ks69v6av5xv7gs5zv6cv7ms6bv7iv7hs61v6ev6dv65s64s62s7nv63v6nv6gv6kv6hv6fv7js6pv7ps6ov6tv66v6mv6lv6iv6qv6vv7wv6ys6uv67p6ws7os6jv6sv6rv7xv6zv70s6xv7ys7qs79v7zs71v74s72s80v73v75v7av78s76v68s7lv7kv7bv77p7rv7cv7ssh5v7tv7uv87t88v83t84v89t8av85t86v8bs7vv8dt8ev8ft8gv8jt8kv8ht8iv8cv8ls81v8mv82v8wv8ns8uv8xt9gt8ps8vt9ct8zv98t8os9et8yv9at8tv8rv9kt96t90v8qv93s9hs8sv9it99s91v9fs94v92v9ms9ns95v9dv9ov9pv9bs9qv9ss9js9tva5vbtsa4v9uva7vbuv97sa6v9vva9vbvva8vbws9xv9zs9wvabvaav9rvbyv9ysbxvacvbzsa1va0va2vadvasvarvc2sa3saevauvatvc3vawv9lsavvahsc4sc0vayvazvb2vaxvb5vccvbbvb0vc5sb4vb3vb8vb7vafsajsb6vbesbgsbdvaivbcvbavb9vb1vbisagvbfvc6sbhvakvcdvbjvansalscesc1vamvbnvblvbmsbksaovc7vbqvbovapvbsvaqvcgvbpvcfsc8sbrpcavc9vcbvchvcivcjtckvctscuscvscltcmvcntcovcptcqvcrvcsvcwvd2vd0vd3tdmtcyvcxvd1tdktd5vdetdnsdgtd4vditdlsczvdctdqtdfsd9vdotd6sdpsdhvdavd7vdtsdssdjsd8vdbvdvvduvdysdwvdzvfzseavdxsddse0vebvg0vecve1vedvg1veevg2se3ve5se2vefvegvg4ve4sg3sg5sehvgpveive7ve6ve8vejvexvg8se9seyvg6vezvf0vg9vekvdrsf1venselsepsf2vg7vf3vf8vgasfbvf5vf4vfevfavf9vfdvf6vfcvfhvemvffvfksfgvf7vfjvfmsfivgbsfoseovflvfnveqvfpvesvgiveuvgcsftversfqvetsfrsfsvgdvfwvgjvgesfuvewvgksfvvevvglsgfvggvgmvghvgnvgovfxpfysgqsgrsgtsgsyh1th2vguygzth0vgxtgyvgvtgwvh3vh4vh9vh6vhcvhfvhnshqshath7thiyhjyhdthgthoyhbvh8vhevhhvhkshlyhmshpy"
+_OLD5 = "04y02y00y03s08p2yp0dp0hv01s1cv3bv18v0ls0ap0bp1ov1kv1nv1lv1mv0js1jv1fv2zv19v1ev1pv1ys1av09p34v37v0mv1zv0cp25v29v0ep0up30v24v2av20s1ws23s0ip26v33v2cv2rv2vs1rs32v31v2qp2bv2dv2js35s1xs1ss2sv3pv38v3mv2wv36v2ks2es2gs2is0wp0vp3qv2fs21s0ks2hs1dp0fp3nv39v0sp3rv2xv4bv3os3cs1ts3sv3ts3dv4dv3vv3wv3es4ct2lv3fs22s43v4et3gv2mv27v15p1us4fs3zv3uv05y06y07y4gs2ns44s1vs16p3kv3xv3hv4hv4rt1gp41s0xp4zt0qp4kv4iv46s4lv45s0gp4av2ov48v10p0pp3jv49v1qs53s0rp47v54s55v56v4ss2pv3iv57v4xt0yp4pt50s5lv11p4ys4qs58s7ds5mv4vt1bv3lv4ws4nt5nv5ov0zp4tt5av40v5pv51t4os5qv4jv4us5rv13p5sv4mv5tv3yv5bv59v12p5uv7ev52s0ns42v5vv5cv28v1hv14p7fs17v5ev5ws5dv5ys5gs5fs0ov2uv0tv60s2tv5xv5zv1iv7gs5hv5iv5jv61v69v5ks63s64s65s6av7iv6bv68v6cv62v7hs7js6dv6ev7ms66v6kv6fv6nv6gv6hv67p6lv6mv6qv6pv6ov6tv6iv6ws6rv6sv6uv6jv6vv6ys7nv6xv70s85t6zv7os7lv7ps71v7wv72s75s87t7kv74v73v79v7qs78s76v7rv7av7xv77p7sshnv83t7ys7zs7bv7tv7uv86v88v84v89t8av8bs7cv80v8ft8gv8jt8kv8ht8iv8dt8ev8cv8lv7vv8mv3av81v8uv8wv82v8vt8xt8ns9gt8yv98t8zv9at9hs9it93s9kt9ct8pv90v9et96t8rv94v99s8os9js91v9ns8tv9ms8sv8qv9bs92v9pv9ov95v9ds9tvbssa4v9ssa5v9ls9uv9qv9fsa6vbtva7v9vv9rva8v97sa9vbus9xv9wvaavabv9zsbxv9ysacva0va1vbvsbysadva2vasvatva3vc1sauvaevavvbwsawvafsahsc2vaxvayvajscbvc4sc3sb3vb6vb0vazvagvb7vb4vb5vb8vb9vbfsbhsbcvb1vaivbavbbvb2vbevbdvakvbgvbivamvbjsaosalsansc5sc0varsbkvapvccvbnvblsbmsbovbzvaqpbrvcdscesbpvc6vcfvc7sbqpcktc8vc9vcitcmtclvcavcotcjvcnvcpvcqschvcgvd2scytcwtcxvczvcstctvcutcvvcrvd0vd1vd9vdbvdatdctdrtd4sd6vd3sd5vgxvddvdttdvtdevd8vdssduvdntdisd7vdztdltdxtdptdfvdjve0sdosdgvdkve2sdhve1se3ve4vdmse7se5ve8vg7sdysejvekvdqse6se9vg8vemveavelvg9veovgasebvedsenvecveqvepvgcveesgbvervgdsegvefvehvesvf7vf8vetvdwseivggsf9vfavghvfbveysfcvewseusgqvgjsfdvfivflvfevffvfovfjvfkvfmvfrvfgvfnvevvexvftvfhvfsvfusfqvfwsfpvezvfxvgksfysfvvf3sf2sf0sf1vgfvf6sfzvf4vf5ph3tgrvg3vg0vgish7tgevg1sg2sg6vgssgtsg4vglvguvgmsgnvgovg5ph9th5thfthdth4vgpvhavh8vh6vgwvgvvhhthgvhevhivhbsgyshjthkvhcvhlvhmvh1vgzsh0yh2yhovhrvhuvhxvhpthsti0shvti7shqvhyti5yhtvi1yhwvhzvi2si3si4yi6yi8s"
+_OLD4 = "01s03s0hv08p2zp3cv0bp1lv1pv1nv1qv1mv0js0ls04y1dv1ov0ap02y1kv1hv30v1bv1rv09p1jv00y1gv1ev0cp31v38v2bv27v26v1yv2av20s1zs21s0dp1fp0ep1vs1us25s2ks22v1cv0ip34v2cv35v36s2sv33v2iv3qv32v1ts3nv2dv2ls2ws3rv2tv37v39v2es2js0ks28v3ov3ps2nv3sv2xv3av2fv3ds2hs4cv2yv13p3ev3tv2rp4ev2gs3gs4dt3lv3us3fv06y05y4ft44v1ip4gs3hv07y0pp2os4hs45s0yp3wv3xv10p0gp3iv3vv0sp3kv23s1ws47s46s0mv2mv4kv4wt4ot4qt4iv4yt24s4lv4jv4xs1sv53v40v3yv52v48v55s49v4bv54s4av0zp4rs57v42s0fp0xp56v4zs3mv2pv4ps50t5nv78s5mv41v4st5pv58v59s5ov29v0tp2qv5rv18p5qv3jv5tv5sv5bv4mt4ts5as3zv79v5uv5cv0vv4ut51s4ns1as5vv5dv4vv5wv14p5ev0wv5fv19p0uv5zv5xs5gs5hs0ns5yv43s61s1xs5iv5jv7as7hs60v6av6bv0ov5kv62v6cv6dv7dv64v6ev6fv65v2vv2uv17p5ls66s0qp63s6iv67v69s6gv7es15p11p68p6jv6hv7iv6lv6kv0rp6ov7rv6nv6mv7bs6vv6qv6pv6rs6ts7cs6sv7ks82t6uv7js84t7gv6wv6ys70s7fv3bv6zv6xv7ls7mv7sv71v7ns73s74v72p7us7pv12p7ts75v7ov76v80t7qv16p83v85v81v7yt7zv77v88t89v8ct8dv8et8fv86s8at8bv87v8gs7vv8hv7wv8rv8pv8st7xv8qt8uv97t93t8is8tv95t98v9dt99t8vs8zt9bt91t8xv8js8wv8ks8yv9fv8lv9gv9nv8nv9hs8mv8ov9is96s9lv9kv9jvh6v9mv9cs9as9es9ova0v9zv9pva2v94sa1v9qva4va3v9sv9rva6va5vbhv9us9ts92s90sa7v9wv9vva8v9xvaova9vanvaqvbqsacs9yvbivapvbrvasvarvadvatvauvaasavvbjsbksabvawvayvbmvaesblsb1vaxvb4safvb0vb3vazvajvagvb2vb6vc0vaisahsakvalpb7vbnsb8sb5vc7tamsbtsbssbovb9vbpvc9tcbtbcvbbvc1vbasbdsbgsbvvbevc2vbuvbwsc4vbyvbxvbfpc3sc8vbzvcavccvcdtcevc5vc6vcfscgvcrsctscjtckvchtcivcsscltcmvcntcovcpvcqvcvvd0vcyvcwvcxvd1tcztd3vdctdetd2vditddvdgtd6sdktdhsdatdmtdjsd4vd8td7vd5vdpvdovcuvdrsdqsdbvdsvdtvggvduvd9sdxve9vdlsdyvdwsfqsdnsdvse8vebvdzveavfrvedve0vecve1vfsse2sefveeve3sfvvftsdfsegve4ve5ve6vehvexvewvfwseivezveyvejse7vf1vf0velsf3vf2vf4vensekvfzsfusf5vemvf6vffsf7vfavfdseovf9versfbvfcvessf8vepveqvg0vfgvfevetvfhsfivfyvg9vg2seupfmsfjsfkvg1sgotflvfxvg3sfpsfnvg4vgavgcvfopgqtg5sg7vgmtg6vevsgbsgdvg8vgpvgstgwtgrvgevgytgtvgnvgfvghsguvgxvgzvh2th3vh0th1vgvvh4sh5vhavh7vhgvhbthdvgksglyh8tgisgjyhjyhhthryhkyhcshethpsh9vhivhfvhoyhlshnshqshmy"
+_OLD3 = "00y03s08p02y0hv1dv01s04y0bp39v1iv1lv09p1jv1kv1mv1nv1av18v0ls0vs0ap0dp19v1ov23v1bv0ws2wp0mv1cp24v28v1xv1ys1ws1vs0cp27v22s25v2xv0ep2gs2hs29v1ev3nv31v2av2yv2es2pv30v32v35v0up0jp1zs33s2fs2bs2ts2zv2qv3kv1rs3ms3ov36v34v0ip3lv37v3pv2uv1ss2op3as3bs49v3qv4bv2cs3uv2kv3cv0fp3tv2vv0kv2dv2is3ds3ev3rs3sv2jv4at41v0sp4ct4ds05y4es06y3fv07y0pp1qs2ls20s4fv42s16p4hv21s15p4gv4iv2mv4zv0xp3iv50v3vv1ps44s46v43s51s3xv48v4nt52s45v47v54v53v4vt3jv26v2nv1fp1us3zs0gp10p5jv5kv4xt55v1ts3hv4os4ws4pt4tt5lv57s75s0yp5mv58v5nv11p5ov3gv59v56v5pv5qv4lt0zp4ys4qs4us4jt1hv1gv4ks4rt4ss5av5rv4mv5bv5sv3wv5cv76v3yv13p5tv5ds5es40s0tv17v5uv5ws0ns5ys5fv2rv5gv5hv14s77s5vv0rp7es0qp5xv12p67v68v5is5zv69v6av0ov2sv63v6bv6cv61v62v7av6fv60s64v6dv78s7bs6ev79s66s6gv7fv6iv6lv6hv7gv65p6jv6kv6ov7dv6nv6qs6mv6ss6pv6rv7cv7ov7hs7is6tv7jv7pv6uv6vs6wv6xv70v7ksh3v7qs6yv7mv7rs71v7lv6zp7sv7xt7zt7vt72v7nv81t87t7yv80v7wv82v73v83s8bt84v8cv85t89t88v86v8av74v8ds8ev7uv8ov8mv8pt7tv38v8nt8rv8wt8fs90t8qv96t8xs9at8us98t8yt94t91v8sv8hs92t8vv8gs8tv9dv8lv9cv8jv9fs9es9bs8iv8kv9gv9hv9ks97s9iv9lv9js9wv9mv9xv8zs9yv9nv95s9zva0v9pva1v9ova2v9rsa3v9qsbeva4v99s9sv9tv93sbfv9uva5vakvalvbnsa6vbgs9vsamvanva7sbovaovapva9sbxvaqvabsbhsarvasva8vatvaavbpsauvayvavvacvb3sb0vazvb1sagsafsaxvawvaevadvb4vb5sb2vbisahvajsbyvb6vaipbjvb8vb7vbavb9vbdvbksbzvbbvbqsc1vbmvbcpblvc0sbrvbsvbtsbvvbuvc8tc9vc6tc7vcatcbvc4tc5vccvbwvcdvcitcgtcetcjvchvcfvcktclvc2vcmvc3vcnvcoscqscvvcxvcpscwtcytczvddtd5tdbtd0vdescuvd7td6vd3vd9td1sdftdhtdjtdcsd2vd8sd4vdasdlvgdvdmvctvcsvcrvdnsdosdqvdpvdgsdisdtsdrvduvfnse6vdssdvve5ve8vdwvfove7veavdxvdyvdkse9vfpsecvdzse0sfsvebvfqse2ve1vftsedve3veuvetvfrse4seevewvevvfwsefveyvexvegveiseksf1vezvf0vejvf2vehvf3vf4vf7vfxvelvfasf5vf6vf8vfcsf9vensepvemveosfbvfesfdvfyseqvfzsg6vffverpfuvessfhvfgvfjvfivfvvg0sfkvg7vg1vfmvg8sg9vflpg2sgavg3vg4vg5vgjtgkvgltgmvgntgovgptgqvgbvgrvgcvgsvgesghsgztgvtgfsh0vgwvgiygttggygxtguvgyvh1vh2vh7vh4vhavhdvh8th5thgyhbthethoyhlyhhyhnyhmsh9vh6vhcvhfvhishjyhks"
+_OLD2 = "03s08p0hv02y04s01s00y0ap39v18v1iv09p0ls1jv1mv1nv1lv1kv0bp2wp0us1ev1bv1av0ws1ov0vs23v0dp0mv1cs19v1dv2kv2xv24v25v0cp28v1xs27v2yv30v1ws1ys35v0ep20s1zs1rs22s2es2gs3nv1vs0ip2av0jp2pv2op29v31v3ov2ts33s3kv32v2zv1qs2bs3ms3pv2qv3lv2is3qv36v2hs2cs34v2ls49v3tv2uv2fs0fp4at3rs1ss2ds2jv0kv37v4bv15p4ds3hv3xv2vv4ct3uv3sv3bs3as2mv0sp4es1ps06y05y07y3vv3jv3cs3ds41v0pp4lt4tt4ms3zs4fv16p4hv21s1ts3ev4gv42s0xp4iv1us4xt4pt17s3fv26v2nv4zv50v1fp43v4us44s0gp52s51s4ys4qs57s10p0yp3iv4vt3gv4jt45v4ws46v48v47v54v53v55v56s4ks75s4rt4nt3yv3wv11p5kv5jv40v5mv1gv5lv0zp58v5ov4ss0ns5nv2sv59v5qv5pv14p4os2rv5av5rv0qv5bv5cv12p5sv76v0tv5ds5es5tv0ov38v77s1hv13p5us5wv5fv5hv5ys5gv5xv0rs5vv5is78s68v67v7es5zv6av69v63v6cv62s6bv60v61v7fv79s6ev6fv7hs64v6dv6gv6lv7gs65p7av7bs6iv6hv6nv6mv7ov6kv6jv6ov6qs6ss7cv7is6pv7vt7xt6rv7dv6tv7jv7pv6vv6wv6xs6uv70v7ks7qsh3v6yv7rs71v7lv6zp7mv7sv72v7zt66s7wv7yv80v81t87t8bt82v73v7nv83s84v89t8av85t86v88v8cv74v8ds8ev7uv8mv8ov8nt7tv8pt8qv96t8fs8wt8rv94t97s92t8sv8us9at8yt90t8xv8hs98t8vv8gs8tv9dv8jv9cv8lv9fs8kv9es8iv9bs9hv9gv9ks95s9iv9lv9js9xv9mv9wv9zv9nv93s91s9yva1v99s9ova0v9pva3v9qsa2v9rsbeva4v9sv9tvbfv9uva5v8zsbnsakv9vsalvbgsa6vamvanva7saovbovapva9saqvbxvabsasvarva8vbhsatvaavbpsauvavvayvacvb1sawvaxvazvb3sb0vagvaesafsadvb2vb5sb4vbisahvb6vbjvajsaipbyvb8vb9vb7sbavbksbzvbdvbbvbqsbmvblvbcpc0sbrvbsvbtsc1vbuvc6tc7vc4tc5vcatcbvc8tc9vbvvcgtccvbwvcdvcetcitchvcfvcktcjvclvc2vcmvc3vcnvcoscpscvvcxvcqscwtcrvcytczvdbtddtd0vd7tdcsdhtcuvcsvd1sd3vdjtd9td5tctvdisdftgdvd2vd8sd4vdesdlvdmvdtvdkvdnsdosdpvdqvd6sdasdgsdrvduvfnse5vdssdvve6ve7vdwvfove8ve9vdyvdxveavebvfpse0secvdzsfsvfqsedve1ve2ve3vftseevetve4seuvfrsefvevvewvegsexveyveisezveksf1vf0vehvf2vfwsejvf3vf4vf7vfuvfasf6vf5velvfcsf9vf8vfbvfesfdvepsemseosenvfxvessffvfyseqvg6vfivfhvfjvfgsfvvfkvg7verpfzsfmsg1vg8vflpg0vg2sg9vg3vg4vgavg5vgbvgptgltgcvgntgjtgqvgesgmvgovgkvgxtgrvgyvghsgttguvgzth0vgvtgwvgsvh1sgiygfsh2vggyhevhhyh9vhjvhmyh4vhcyhathbvhfthgvhkthlvhoshqshdyhpsh5thiyh6shrsh8yh7yhny"
+_OLD = "1dv39v0hv1ev08p1iv0bp1lv1jv2wp03s1mv0ap01s1kv1nv18v00y2xv0ep1bv19v1ov1av32v04y0ls0mv02y06y35v2yv24v2kv05y0cp28v2av09p07y2zv0dp27v0us23v0ws1xs1ys31v3nv30v2pv29v25v3ov1zs3kv2qv0jp36v3pv1vs2op1ws22s2bs2ts2is33s34v3lv3qv2uv49v0ip4bv2vv2es2gs2fs20s2jv37v0kv2cs2hs3uv3tv3iv3ms3rs3sv3vv0vs1cp4at4ct1rs1ps3xv2ds41v4ds4es2ls3bs3as0fp4fv4hv0sp3zs1ss0pp3ds3cs1ts16p3ev15p4gv1fp3fv4iv42s3jv4zv2mv1us50v0xp43v17s44s46v51s52s48v1qs45v47v54v0qp21s53v0rp10p0yp55v4nt4pt3hv4xt5mv4vt5lv56v2nv5ov0gp26v4os11p5nv4qs0ns59v4ys57s0zp58s4tt4us4ws4lt5qv5pv12p3gv5av5sv5rv5tv4jt5bv5uv0tv5cv5dv5vv4ms13p4rt4ks4sv14p5wv2rv5iv5fs5es1hv1gv3wv3yv5hv2sv5gv5zs60v5xs5yv6bv6av40s61s7hs78s62v5jv79v66s6dv6cv63s65v64v5kv6fv7as6ev7bs7iv0ov67v6iv68p80t6hv7dv6jv6gv7js69s7es6ov7rv6kv6lv7cv6qv6ts82t7sv6nv6pv6mv6rs6vs84t6uv7ks6sv7ts7fv6wv6xs7ls7gv6zv6yv70v7yt7mv7vv71v72p7ns74v7pv7ov8at88t8et8ct75v81v83v85v7zv76v7qv73s7us86s87v8bv89v8fv8dv77v8gs38v8hv7xv8pv8rv8qt7wv8st8tv93t8is95t8uv8zt94s99t9bthcv8vs8xv9dt97t91t96v8ks8wv8js8yv9fv8ov9gv8mv9hs8lv8nv9is9cs9lv9kv9jv9os90s9mv9pv9nva2v9qva1v9esa4v9rva3va6v9sv92s98s9tva5va8vbkva9v9us9vsa7v9as9yvblv9wv9xvaav9zvbmsaqvarva0sbnsabvasvatvacvbtsauvavvbpvadsawvayvafsaxvb1vahsbuvazvaevbqsb0vb4vagvb7sb3vb2vb5vb6vb9saivb8vbbsbavalsamsajvaksapsbovbcvanvbsvbgvbdvbvsbesbfsaopbwsbrvbhvc3vbjvbyvbipbxvc4vbzsc1vc5sc6sc0vc7vc2vcgtchvc8vcetcctcatcfvcdvcbvc9vcivcuscktclvcqtcrvcmtcnvcotcpvcjvcsscwsctvd0vd1vd3vcvscxvd2tcyvgmvd4td5vdhtdbtd6vdltczvdisddtdftd7sd9vdntdptdjtdmvdcsd8vdesdavdgsdrvdsve0vdtsdusdxvdqvdosdvvdwvdksdyvdzseeve1vfwsedvegve2vfxvefveive3vehvfysfzsekve4ve6se5ve7sejvelvg1vemveavg2senve9ve8vebveovf3vg5sf2vepsecvf5versg6vf4vetsf7vgfvf6veqvg0sfavggvf8vf9vg7sfbvg8sesvghsfcvfgvfdveuvfjsfevffvfivfhvflsewvexseysevvfkvfnsfmvezvf0pgutgstgytg9sfovf1sfrsfssfqsgwtg4vg3vfvsgjvfpvgavftvfupgbsgisgcvgdvgevgvvgtvgzvgxvglvh0vgkvh1vh2th3vh4th8th9vgnsgqsgosgrygpyh5vh6th7vhavhbvhqvhhvhdvhmvhrthithethlyhnthuyhwyhxyhyyhvshjvhsshfvhovhgyhtyhkyhps"
 PLAN = {"seed": 1, "passes": 120, "moves": 16000}
 
 
@@ -216,7 +224,10 @@ def make_plan(g, T):
     def issue():
         if "seq" not in PLAN:
             PLAN["ops"] = ops
-            PLAN["seq"] = order(ops, PLAN["seed"], PLAN["passes"], PLAN["moves"])
+            if len(ORDER) == 3 * len(ops):
+                PLAN["seq"] = [(int(ORDER[k:k + 2], 36), ORDER[k + 2]) for k in range(0, len(ORDER), 3)]
+            else:
+                PLAN["seq"] = order(ops, PLAN["seed"], PLAN["passes"], PLAN["moves"])
         count = {}
         known = {q: {} for q in eng}
         mark = {}
@@ -242,9 +253,9 @@ def make_plan(g, T):
                 count[sem] = count.get(sem, 0) + 1
                 fn(eng[q]).then_inc(T.sem[sem], 1)
             elif o["kind"] == "send":
-                sem, n = fn(eng[q])
-                count[sem] = n
-                count["left"] = count.get("left", 0) + n
+                sem, come, gone = fn(eng[q])
+                count[sem] = come
+                count["left"] = count.get("left", 0) + gone
             else:
                 sem = "dm%d" % ndma
                 ndma += 1
@@ -350,20 +361,19 @@ def rank_program(g, core, T, topo):
         else:
             note({"p": (lambda e: e.iota(out[0], pattern, base, cm), 0.13 + 2 * CYC * out[2])}, [out], [])
 
-    def dma(q, out, in_, lat=1.3, kind="dma"):
-        note({k: (lambda e: e.dma_start(out[0], in_[0]), 0.05) for k in q}, [out], [in_], lat, kind)
+    def dma(q, out, in_, lat=1.2, kind="dma", busy=0.15):
+        note({k: (lambda e: e.dma_start(out[0], in_[0]), busy) for k in q}, [out], [in_], lat, kind)
 
     def hbm(ap):
         return (ap, [])
 
     dma("y", f("NDI"), hbm(T.nd[:, :]), 1.3, "load")
     dma("s", f("UT"), hbm(T.u[:, :]), 1.7, "load")
-    dma("y", f("XT", 0, 1024), hbm(T.x[:, 0:1024]), 2.3, "load")
-    dma("s", f("XT", 1024, 2048), hbm(T.x[:, 1024:2048]), 2.8, "load")
-    dma("y", f("ARI"), hbm(T.ar[:, :]), 3.3, "load")
-    dma("y", f("WQ", cast=dt.uint8), hbm(T.wc[:, :]), 4.0, "load")
-    dma("y", f("WS"), hbm(T.ws[:, :]), 4.5, "load")
-    dma("y", f("VT"), hbm(T.v[:, :]), 5.0, "load")
+    dma("y", f("XT", 0, 1024), hbm(T.x[:, 0:1024]), 2.5, "load")
+    dma("s", f("XT", 1024, 2048), hbm(T.x[:, 1024:2048]), 3.0, "load")
+    dma("y", f("ARI"), hbm(T.ar[:, :]), 3.5, "load")
+    for out, src in ((f("WQ", cast=dt.uint8), T.wc), (f("WS"), T.ws), (f("VT"), T.v)):
+        dma("y", out, (src[:, :], f("ARI")[1]), 2.5)
 
     iota(f("PI", 0, 1), [[0, 1]], 0, 1, small=False)
     iota(f("N"), [[1, 88]])
@@ -372,7 +382,8 @@ def rank_program(g, core, T, topo):
     iota(f("K32"), [[0, 2], [1, 16]])
     iota(f("DU"), [[64, 2], [0, 2], [4, 16]], 2048)
     iota(f("W1"), [[384, 2], [24, 16]], -1)
-    iota(f("BP"), [[0, 4], [1, 4], [0, 2]])
+    iota(f("BP"), [[0, 6], [1, 4], [0, 2]], MID)
+    iota(f("B4"), [[1, 4]], MID)
     fill(f("ONE"), 1.0)
     ident, one = f("ID"), f("ONE", 0, 128)
     note({"p": (lambda e: e.affine_select(ident[0], one[0], [[-1, 128]], OP.is_equal, 0.0, 0, 1), 0.38)}, [ident], [one])
@@ -390,18 +401,16 @@ def rank_program(g, core, T, topo):
         const(f("TAB", a, a + 32), 0.0)
     for n in ("SP0", "SP1", "SPX"):
         const(f(n), 0.0)
-    for n, j in (("D0F", 0), ("D0S", 0), ("D0X", 0), ("TD", 1), ("TD", 2), ("TA", 0), ("TA", 1), ("D0Y", 0), ("D1Y", 1)):
+    for n, j in (("D0F", 0), ("D0S", 0), ("D0X", 0), ("TD", 1), ("TD", 2), ("D0Y", 0), ("D1Y", 1)):
         const(f(n, j, 768, 3), 0.0)
     const(f("D1Y", 0, 768, 3), -BIG)
     fill(f("TA", 1024, 1040), MARK)
     fill(f("Z", 512, 513), -BIG / 32)
     fill(f("Z", 513, 528), -1.5 * BIG)
-    fill(f("RX", 0, 35), -2 * BIG)
-    fill(f("RX", 52, 103), 2 * BIG)
+    fill(f("RX", 52, 103), -2 * BIG)
+    fill(f("RB", 15, 560, 16), -2 * BIG)
     for j in range(2):
-        const(f("RA%d" % j), 0.0)
-        const(f("RC%d" % j, 0, 2 * KS, KS - 1), 0.0)
-        fill(f("RC%d" % j, KS, KS + 1), 0.0)
+        const(f("RA%d" % j, 3 * KS + 32, 4 * KS, 32), 0.0)
         fill(f("RA%d" % j, 0, 1), BIG)
         fill(f("RA%d" % j, KS, KS + 1), -BIG)
 
@@ -410,33 +419,33 @@ def rank_program(g, core, T, topo):
         ts(f("BITS", j, j + 1), pi, sh, OP.logical_shift_right, m, OP.bitwise_and)
     cp(f("SC", 0, 6), f("BITS", 0, 6))
     pm, e = f("pm"), f("e")
-    for n, src, sc, bi in (("A", "e", -32.0, 32.0), ("B", "e", 32.0, None), ("nA", "e", 32.0, -32.0), ("nB", "e", -32.0, None), ("e1", "e", -1.0, 1.0),
-                           ("pA", "p31", f("e1"), None), ("pB", "p31", e, None), ("pS", "e", -512.0, f("pB")), ("e16", "e", 16.0, None),
-                           ("sO", "pm", -4096.0, 61440.0 - 67584.0), ("sI", "pm", 4096.0, 63488.0), ("pm16", "pm", 1.0, 16.0), ("sb", "pm", 8.0, 783.0),
+    for n, src, sc, bi in (("A", "e", -32.0, 32.0), ("B", "e", 32.0, None), ("e1", "e", -1.0, 1.0),
+                           ("p0", "p31", 1 / 32.0, None), ("p1", "e", -16.0, f("p0")), ("e16", "e", 16.0, None),
+                           ("sO", "pm", -4096.0, 61440.0 - 67584.0), ("sI", "pm", 4096.0, 63488.0), ("sb", "pm", 8.0, 783.0),
                            ("s1", "qh", 1.0, f("ql")), ("qh16", "qh", 16.0, None), ("t66", "qh", float(KS), 32.0), ("dl", "h1", 32.0, f("t66")),
                            ("zb", "pm", 16.0, -497.0)):
         move(f(n), f(src), sc, bi)
     ts(f("UL"), f("N", 0, 8), 16.0, OP.mult)
     ts(f("NDL"), f("HE", 0, 4), 16.0, OP.mult, pm, OP.add)
     ts(f("SPG"), f("N", 0, 64, 32), f("p31"), OP.add)
-    ts(f("DL"), f("N", 0, 2), 2.0 * KS, OP.mult, f("dl"), OP.add)
+    ts(f("DL", 0, 3), f("N", 0, 3), 2.0 * KS, OP.mult, f("dl"), OP.add)
+    ts(f("DK", 0, 1), f("dl"), 4.0, OP.add)
     ts(f("ISO"), f("E64"), e, OP.is_equal)
     ts(f("NIS"), f("E64"), e, OP.not_equal)
     tt(f("DUM"), f("DU"), f("NIS"), OP.mult)
     ts(f("OWN", 0, 32), f("K32"), pm, OP.not_equal, -BIG, OP.mult)
-    for n in (32, 64, 128, 256):
+    for n in (32, 64, 128):
         move(f("OWN", n, 2 * n), f("OWN", 0, n))
     for h in range(2):
-        move(f("CB", 32 * h, 32 * h + 32), f("ISO", 0, 32), f("sI"), (12 - 8 * h) * U - 63488.0)
-        move(f("CB", 64 + 32 * h, 96 + 32 * h), f("ISO", 0, 32), f("sO"), (4 + 8 * h) * U + 67584.0)
+        move(f("CB", 32 * h, 32 * h + 32), f("ISO", 0, 32), f("sI"), (12 - 8 * h) * U - 63488.0 - MID)
+        move(f("CB", 64 + 32 * h, 96 + 32 * h), f("ISO", 0, 32), f("sO"), (4 + 8 * h) * U + 67584.0 - MID)
     move(f("T6", 0, 4), f("HE", 0, 4), 256.0, f("zb"))
     tt(f("T6", 4, 8), f("T6", 0, 4), f("ISO", 0, 64, 16), OP.mult)
     ts(f("zg"), pm, 15.0, OP.not_equal, e, OP.mult)
     move(f("T6", 8, 12), f("NIS", 0, 64, 16), f("zg"), 512.0)
     tt(f("T6", 12, 16), f("T6", 4, 8), f("T6", 8, 12), OP.add)
     cp(f("ZWL"), f("T6", 12, 16))
-    move(f("KT", 0, 50), f("N", 0, 50), 1 / 4096.0)
-    move(f("KT", 52, 134), f("N", 0, 82), 1 / 4096.0)
+    iota(f("KU"), [[4096, 136]])
     ts(f("JI"), f("K32", 0, 32, 2), f("s1"), OP.add, 1.0, OP.add)
     ts(f("JJ"), f("JI"), 15, OP.bitwise_and)
     for h in range(2):
@@ -444,7 +453,7 @@ def rank_program(g, core, T, topo):
     move(f("T7", 0, 16), f("N", 0, 16), 32.0, f("qh16"))
     tt(f("T7", 16, 32), f("T7", 0, 16), f("JJ"), OP.add)
     cp(f("CIRC"), f("T7", 16, 32))
-    ts(f("DDI"), f("K32"), -1.0, OP.mult, f("pm16"), OP.add)
+    iota(f("DDI"), [[0, 2], [-1, 16]], 16, 1, small=False)
     ts(f("DI4"), f("DDI"), 15, OP.bitwise_and)
     d = f("DI4")
     ts(f("T1", 0, 32), d, 3.0, OP.mult)
@@ -479,12 +488,12 @@ def rank_program(g, core, T, topo):
     ts(f("SL"), f("N4"), 0.25, OP.mult)
     for io in range(2):
         tt(f("CC", 64 * io, 64 * io + 64), f("CB", 64 * io, 64 * io + 64), f("NDM"), OP.add)
-    move(f("NS"), f("N4"), 2.0 ** -24)
-    move(f("NT"), f("NW"), 2.0 ** -24)
     for h in range(2):
-        a, b = f("KT", 34 * h, 34 * h + 16), f("KT", 52 + 50 * h, 84 + 50 * h)
-        tt(a, a, f("NS", 16 * h, 16 * h + 16), OP.add)
-        tt(b, b, f("NT", 32 * h, 32 * h + 32), OP.add)
+        a, b = f("KU", 34 * h, 34 * h + 16), f("KU", 52 + 50 * h, 84 + 50 * h)
+        tt(a, a, f("N4", 16 * h, 16 * h + 16), OP.add)
+        tt(b, b, f("NW", 32 * h, 32 * h + 32), OP.add)
+    move(f("KT", 0, 52), f("KU", 0, 52), 2.0 ** -24)
+    move(f("KT", 52, 136), f("KU", 52, 136), 2.0 ** -24)
     ts(f("TA", 2, 768, 3), f("ARI", ind=("CIRC",)), U, OP.mult)
 
     nxt = T.cores[(rank + 1) % len(T.cores)]
@@ -504,7 +513,7 @@ def rank_program(g, core, T, topo):
         def go(e):
             e.remote_dma(lq[0], q[0], T.sem[sem], T.sem["left"], pid, rid, mask)
             e.remote_dma(ls[0], s[0], T.sem[sem], T.sem["left"], pid, rid, mask)
-            return sem, 2 * len(engines)
+            return sem, 2 * len(engines), 2 * len(engines)
         note({"p": (go, 0.6 if t or j else 2.1)}, [lq, ls], [q, s], 1.5, "send")
 
     def table():
@@ -517,19 +526,19 @@ def rank_program(g, core, T, topo):
                 turn(f("TAB", lo + 256 * a, lo + 256 * a + 256), f("EX", 16 * h + 256 * a, 16 * h + 256 * a + 256))
 
     def choose(j, src):
-        n, at, op, big = (16, 0, OP.max, -2 * BIG) if j == 0 else (32, 52, OP.min, 2 * BIG)
-        for h in range(2):
+        n, at = 16 + 16 * j, 52 * j
+        buf, st = ("RX", 1) if j else ("RB", 16)
+        for h in range(2 * j):
             a = at + 1 + (n + 18) * h
-            scan(f("RX", a, a + n), src(h), src(h), big, op, op)
+            scan(f("RX", a, a + n), src(h), src(h), -2 * BIG, OP.max, OP.max)
         for h in range(2):
-            lo, hi, junk = at + (n + 1) * h, at + n + 1 + (n + 18) * h, 52 * (2 * j + h)
-            below(f("JK", junk, junk + hi - lo), f("RX", lo, hi), f("RX", hi - 1, hi), f("IX", 2 * j + h, 2 * j + h + 1))
-        for k, (a, b) in enumerate(((("A", "pA"), ("B", "pB")), (("nA", "pA"), ("nB", "pS")))[j]):
-            ts(f("L4", 4 * j + k, 4 * j + 4, 2), f("IX", 2 * j, 2 * j + 2), f(a), OP.mult, f(b), OP.add)
+            lo, hi = at + (n + 1) * h, at + n + 1 + (n + 18) * h
+            below(f("JK", lo, hi), f(buf, st * lo + st - 1, st * hi, st), f(buf, st * hi - 1, st * hi), f("IX", 2 * j + h, 2 * j + h + 1))
+        for k, a in enumerate("AB"):
+            ts(f("L4", 4 * j + k, 4 * j + 4, 2), f("IX", 2 * j, 2 * j + 2), f("p%d" % j), OP.add, f(a), OP.mult)
         w = 2 * n + 18
-        tt(f("FL", at, at + w), f("RX", at + 1, at + w + 1), f("RX", at, at + w), OP.is_lt if j else OP.is_gt)
-        scan(f("SK", at, at + w), f("FL", at, at + w), f("KT", at, at + w), 0.0, OP.max, OP.min)
-        move(f("RA%d" % j, 2 * KS + 32, 2 * KS + 65, 32), f("SK", at + n - 1, at + w, n + 18), 2.0 ** 24)
+        scan(f("SK", at, at + w), f("JK", at, at + w), f("KT", at, at + w), 0.0, OP.max, OP.min)
+        move(f("RA%d" % j, 2 * KS + 32, 2 * KS + 65, 32), f("SK", at + n - 1, at + w, n + 18), 2.0 ** 24, -float(MID))
 
     def slots(j, t):
         ft, gk, ky, ra, rc = "F%d" % t, "GK%d" % j, "KY%d" % j, "RA%d" % j, "RC%d" % j
@@ -543,13 +552,25 @@ def rank_program(g, core, T, topo):
             k = f(ky, 64 * io, 64 * io + 64)
             scan(f(ra, KS * io + 1, KS * io + 65), k, k, big, a, a)
         for io, a, b, big in sides:
-            scan(f(rc, KS * io + 1, KS * io + 65), f(ky, 64 * io, 64 * io + 64), f(ra, KS * io, KS * io + 64), big, a, b)
+            scan(f(rc, KS * io + 1, KS * io + 65) if j else f(ra, KS * (4 + io) + 1, KS * (4 + io) + 65), f(ky, 64 * io, 64 * io + 64), f(ra, KS * io, KS * io + 64), big, a, b)
         lo, y = 48 * j, 384 * j
-        for src, a, n in ((ra, lo, 32), (rc, lo + 32, 16)):
-            tt(f("DI", a, a + n), f(src, ind=("DL", 0, n // 16)), f("BP", 0, n), OP.add)
-        for a, n in ((lo, 32), (lo + 32, 16)) if j else ((lo, 48),):
-            ts(f("DM", a, a + n), f("DI", a, a + n), 4095, OP.bitwise_and)
-            cp(f("LL", a, a + n), f("DM", a, a + n))
+        if j:
+            tt(f("DI", 64, 80), f(ra, 128, 4 * KS, ind=("DK", 0, 1)), f("BP", 0, 16), OP.add)
+        else:
+            tt(f("DI", 0, 48), f(ra, ind=("DL", 0, 3)), f("BP", 0, 48), OP.add)
+        a, n = (64, 8) if j else (0, 48)
+        ts(f("DM", a, a + n), f("DI", a, a + n), 4095, OP.bitwise_and)
+        cp(f("LL", a, a + n), f("DM", a, a + n))
+        for io in range(2 * j):
+            ts(f("HI", 4 + 2 * io, 6 + 2 * io), f(ra, KS * io + 32, KS * io + 65, 32), 1.5 * 2.0 ** 35, OP.add, -1.5 * 2.0 ** 35, OP.add)
+            for h in range(2):
+                c = KS * io + 32 * h + 32
+                ts(f("LL", lo + 8 * io + h, lo + 8 + 8 * io, 2), f("B4"), f(ra, c, c + 1), OP.add, f("HI", 4 + 2 * io + h, 5 + 2 * io + h), OP.subtract)
+        for io in range(2 * j):
+            ts(f("HI", 2 * io, 2 * io + 2), f(rc, KS * io + 32, KS * io + 65, 32), 1.5 * 2.0 ** 35, OP.add, -1.5 * 2.0 ** 35, OP.add)
+            for h in range(2):
+                c = KS * io + 32 * h + 32
+                ts(f("LL", lo + 32 + 8 * io + h, lo + 40 + 8 * io, 2), f("B4"), f(rc, c, c + 1), OP.add, f("HI", 2 * io + h, 2 * io + h + 1), OP.subtract)
         for io in range(2):
             ab = f("AB", 256 * j + 128 * io, 256 * j + 128 * io + 128)
             move(ab, f(ft, ind=("LL", lo + 8 * io, lo + 8 * io + 8)))
@@ -606,6 +627,7 @@ def rank_program(g, core, T, topo):
                 move(o, i)
             else:
                 tt(o, i, f("OWN", 0, 256), OP.add)
+            scan(f("RB", 544 * h + 16, 544 * h + 272), o, o, -2 * BIG, OP.max, OP.max)
             scan(f("Z", 256 * h, 256 * h + 256), f("FOLD"), o, 0.0, OP.min, OP.max)
         for a in range(2):
             for b in range(4):
@@ -616,12 +638,13 @@ def rank_program(g, core, T, topo):
         move(f("ZW"), f("Z", ind=("ZWL",)))
         ts(f("GM"), f("TAB", ind=("L4", 0, 4)), 0.0, OP.not_equal, BIG, OP.mult)
         turn(f("GT"), f("GM"))
-        tt(f("S2"), f("GT"), f("ZW"), OP.subtract)
+        tt(f("S2"), f("ZW"), f("GT"), OP.subtract)
         choose(1, lambda h: f("S2", 32 * h, 32 * h + 32))
         slots(0, t)
         slots(1, t)
         if t == 0:
-            cp(f("CM", ind=("SL",)), f("OWN"))
+            for a in range(4):
+                cp(f("CM", ind=("SL", 8 * a, 8 * a + 8)), f("OWN", 0, 128))
         operands(0, "D0F", "TA")
         steps("TB", "D0F", "TA")
         operands(1, "D0S", "TB")
@@ -638,7 +661,7 @@ def rank_program(g, core, T, topo):
             move(f("TA", 768, 1024), f("TA", 2, 768, 3), -1.0)
             for a in range(2):
                 move(f("OAO", 256 * a, 256 * a + 256), f("TA", ind=("OUT", 16 * a, 16 * a + 16)), 1.0 / U)
-            dma("y", hbm(T.oa[:, :]), f("OAO"), 2.0)
+                dma("y", hbm(T.oa[:, 256 * a:256 * a + 256]), f("OAO", 256 * a, 256 * a + 256), 2.2)
         anew(0, t)
         anew(1, t)
 
@@ -648,9 +671,10 @@ def rank_program(g, core, T, topo):
         quant("XQ3", "XS3", lo, hi, f("F2", 512 * a, 512 * a + 512))
         mm(f("PS", 512 * a, 512 * a + 128), f("VQ"), f("VS"), f("XQ3", lo, hi), f("XS3", lo, hi))
         move(f("YO", lo, hi), f("PS", 4 * lo, 4 * lo + 128))
-        dma("ys", hbm(T.y[:, lo:hi]), f("YO", lo, hi))
-        if a % 2:
-            dma("ys", hbm(T.oc[:, 4 * lo - 512:4 * hi]), f("XQ3", lo - 128, hi, cast=dt.uint8))
+    for lo, hi in ((0, 256), (256, 512)):
+        dma("ys", hbm(T.oc[:, 4 * lo:4 * hi]), f("XQ3", lo, hi, cast=dt.uint8), 1.6)
+    for lo, hi in ((0, 256), (256, 384), (384, 512)):
+        dma("ys", hbm(T.y[:, lo:hi]), f("YO", lo, hi), 1.0 + (hi - lo) / 400.0)
     for k in range(4):
         dma("ys", hbm(T.osc[4 * k:4 * k + 4, :]), (T.XS3[32 * k:32 * k + 4, 0:512], [("XS3", 0, 512, 1)]))
     issue()

@@ -1,14 +1,16 @@
+import math
 from concourse.mybir import dt, AluOpType, ActivationFunctionType
 
 OP = AluOpType
 AF = ActivationFunctionType
 R = 3
 W = 2176
-U = 131072.0
+U = 65536.0
+STEP = U / 16
 MARK = 0.125
 BIG = 1.0e29
-KS = 66
-MID = W // 2
+NONE = 12 * U + 15 * STEP + 2048
+EMPTY = 528
 
 CODES, PLANE, BF, F32, I32, U16 = "float8_e4m3fn_x4", "uint8", "bfloat16", "float32", "int32", "uint16"
 SCRATCH = {"PS": ("psum", [128, 4096], F32)}
@@ -16,18 +18,15 @@ for _n, _w, _d in (
     ("XT", 2048, BF), ("UT", 512, BF), ("VT", 512, BF), ("ET", 528, BF), ("ONE", 528, BF), ("ID", 128, BF),
     ("UQ", 128, CODES), ("US", 128, PLANE), ("UQR", 128, CODES), ("USR", 128, PLANE), ("VQ", 128, CODES), ("VS", 128, PLANE),
     ("WQ", 512, CODES), ("WS", 512, PLANE), ("EQ", 512, CODES), ("ES", 512, PLANE), ("LQ", 320, CODES), ("LS", 320, PLANE),
-    ("NDI", 32, I32), ("ARI", 512, I32), ("IA", 160, I32), ("FA", 1600, F32), ("SC", 32, F32), ("KT", 136, F32), ("KU", 136, F32), ("HI", 8, F32), ("B4", 4, F32),
-    ("OWN", 512, BF), ("CM", 512, BF), ("FOLD", 256, BF), ("KEEP", 256, BF),
-    ("UL", 8, U16), ("SL", 32, U16), ("SM", 32, U16), ("CIRC", 16, U16), ("COLG", 16, U16), ("EXP", 34, U16), ("OUT", 32, U16),
-    ("PW", 512, F32), ("SG", 512, F32), ("Z", 528, F32), ("ZW", 64, F32), ("RX", 136, F32), ("RB", 816, F32), ("FL", 136, F32), ("SK", 136, F32),
-    ("IX", 4, F32), ("JK", 208, BF), ("L4", 8, U16), ("GM", 64, BF), ("GT", 64, BF), ("S2", 64, F32), ("TAB", 1120, BF), ("EX", 528, BF),
-    ("GK0", 128, F32), ("GK1", 128, F32), ("KY0", 128, F32), ("KY1", 128, F32),
-    ("RA0", 6 * KS, F32), ("RA1", 4 * KS, F32), ("RC0", 2 * KS, F32), ("RC1", 2 * KS, F32),
-    ("DI", 96, I32), ("DM", 96, I32), ("LL", 96, U16),
+    ("NDI", 32, I32), ("ARI", 512, I32), ("IA", 16, I32), ("FA", 864, F32), ("SC", 32, F32), ("SM", 32, U16),
+    ("UL", 8, U16), ("SL", 32, U16), ("NL", 32, U16), ("PA", 32, U16), ("PB", 32, U16), ("PD", 32, U16), ("LA", 64, U16), ("L1", 8, U16), ("L2", 2, U16), ("LL", 96, U16),
+    ("NW", 64, F32), ("IOT", 512, F32), ("COL", 544, F32), ("ARB", 512, BF),
+    ("PW", 512, F32), ("SG", 512, F32), ("TS", 528, F32), ("RX", 96, F32), ("JK", 96, BF), ("IX", 8, F32),
+    ("ZW", 64, F32), ("ZM", 64, F32), ("GM", 64, F32), ("GT", 64, F32),
+    ("TAB", 544, BF), ("TZ", 512, BF), ("T1", 1536, BF), ("T2", 1536, BF), ("KEEP", 768, BF), ("TBL", 512, BF), ("XG", 64, BF), ("XW", 256, BF), ("XI", 128, F32),
+    ("GK0", 160, F32), ("GK1", 160, F32), ("KY0", 648, F32), ("KY1", 648, F32), ("TN", 544, BF), ("DI", 96, I32), ("DM", 96, I32),
     ("AB", 512, BF), ("D0Y", 768, BF), ("D1Y", 768, BF), ("YS", 768, BF), ("YT", 640, BF), ("YW", 256, BF), ("V32", 256, BF), ("VV", 256, BF),
-    ("XG", 128, BF), ("X2", 128, BF), ("DD", 128, BF), ("SN", 64, BF), ("SP0", 256, BF), ("SP1", 256, BF), ("SPX", 256, BF),
-    ("D0F", 768, BF), ("D0S", 768, BF), ("D0X", 768, BF), ("TA", 1040, BF), ("TB", 768, BF), ("TC", 768, BF), ("TD", 768, BF),
-    ("OAO", 512, F32), ("YO", 512, F32),
+    ("OA1", 512, BF), ("OA2", 528, BF), ("OAO", 512, F32), ("YO", 512, F32),
 ) + tuple(("F%d" % t, W, BF) for t in range(R)) + tuple((n + "%d" % t, 256, d) for t in range(R) for n, d in (("SQ", CODES), ("SS", PLANE))) \
   + tuple((n + "%d" % t, 512, d) for t in range(R + 1) for n, d in (("XQ", CODES), ("XS", PLANE))):
     SCRATCH[_n] = ("sbuf", [128, _w], _d)
@@ -36,27 +35,23 @@ SEMAPHORES = ["cv", "cs", "ct", "cp", "left"] + ["arr%d" % t for t in range(2 * 
 COUNTER = {"v": "cv", "s": "cs", "t": "ct", "p": "cp"}
 PART = {}
 for _b, _names in (
-    ("IA", (("PI", 8), ("BITS", 8), ("DDI", 32), ("DI4", 32), ("JI", 16), ("JJ", 16))),
-    ("FA", (("N", 88), ("E64", 64), ("K32", 32), ("DU", 64), ("HE", 8), ("W1", 32), ("BP", 48), ("ISO", 64), ("NIS", 64), ("DUM", 64), ("CB", 128), ("CC", 128),
-            ("NDD", 64), ("NDM", 64), ("NWI", 64), ("NW", 64), ("N4", 32), ("NS", 32), ("NT", 64)) + tuple(("T%d" % i, 40) for i in range(10))),
-    ("SC", tuple((n, 1) for n in ("pm", "e", "p31", "qh", "ql", "h1", "A", "B", "e1", "p0", "p1", "zg", "e16", "sO", "sI", "sb", "s1",
-                                  "qh16", "t66", "dl", "zb"))),
-    ("SM", (("SPG", 2), ("DL", 4), ("DK", 2), ("NDL", 4), ("ZWL", 4))),
+    ("IA", (("PI", 8), ("BITS", 8))),
+    ("FA", (("N", 64), ("BP", 48), ("CAP", 129), ("RST", 64), ("HE", 4), ("XE", 4), ("B3", 6), ("BV", 6), ("BV2", 2), ("K32", 32), ("DU", 16), ("C8", 64), ("CBU", 64),
+            ("NDD", 64), ("N4", 32), ("NM", 32), ("CC", 32), ("PP", 32), ("T0", 4), ("T3", 4), ("T4", 32), ("T5", 32))),
+    ("SC", tuple((n, 1) for n in ("pm", "x", "p31", "qh", "h1", "x16", "pm32", "cs", "dl", "nil"))),
+    ("SM", (("SPG", 2), ("NDL", 4), ("ZWL", 4), ("DL", 4))),
 ):
     _a = 0
     for _n, _w in _names:
         PART[_n] = (_b, _a, _w)
         _a += _w
 CYC = 0.00083
-WAKE = 0.2
-ORDER = "00y01s02y03s04y0hv3bv1ev1av08p1kv1nv1mv2yp0ap09p0bp1lv1ov0cp0ep1jv2zv0dp19v1cv18v1pv34v0ls0js1zs1ws20s1fv30v37v24v1yv29v1xs2js21s0up0ip2av26v25v2cv2rv2vs2hs32v33v31v0mv2sv2bv38v3pv35s23s2wv3mv2ds36v2is2gs3qv2xv2qp0wp3nv1dp0ks3rv39v2es2ks3os0vp1ts4bv3sv2fs0sp3ds3cs1rs4dv1ss3ts43v3xv3wv4ct3es3fs3uv3kv3gv3vv0fp4et3zv15p05y06y07y2mv2lv3hv4fs4gs1vs44s41s1us16p4hv4rt1gp0qp0xp4zt46s4kv4iv1qs2ns4lv3jv45s22s2ov0pp0gp0yp53s4av48v49v47v54s55v4ss4pt56v4qs4xt50s4ys27v3iv5lv11p5mv4nt0rp3lv2pv5nv4vt7ds4os4tt5ov57v5av58s0zp51t5pv13p5qv4jv5rv5sv4mv5tv3yv5bv52s4ws0ns59v10p5uv40v12p7ev1bv5vv5cv1hv1iv4us42s17v5dv7fs5ev5ws28v0ov5ys5fs5gs60s2uv0tv5xv5zv2tv7gs5iv5hv5jv61v69v5ks64s63s65s6av7iv6bv68s6cv62v7hs7js6dv6ev7ms66v6kv6fv6hv6nv6gv6lv6mv67p6qv6ov6pv6tv6iv6ws6rv6sv6uv6jv6vv6ys7nv85t6xv70s14p6zv7os7ps7wv7lv71v74s7kv75s73s72v79v7qs78s76v7rv77p7ss7avhnv7xv7ys7zs7tv7bv7uv86v87t88v89t8av83t84v7cv8bs8jt8kv8ft8gv8dt8ev8ht8iv8cv8ls80v7vv8mv81v8uv8wv82v8vt8xt8ns9gt8yv98t8zv9at9hs9it93s9kt9ct8os9js8pv90v99s9et8rv96t94v91v92v8tv8sv9ns8qv9ms9ov9pv95v9ds9bsbss9tva4v9ssa5v9uv9fsa6vbtv97sa7v9vv9qva8va9v9ls9wv9ys9xvbuvaav9rvabv9zs3avbxvacva1va0vbvsbysa2vadvc1sasvatvbwsa3vauvaevavvawvahsc2vaxvafsc4sayvb3vb6vazvb0vajsb9vaivb8vb4vb5vbcvb7vb1vagvbbvbdvbavb2vbfsbevbhsakvbgvbivbjscbvc0vamsalsansaosc5sc3sbkvapvbmsbnsaqpccvblvbovarscmtbzvcdscitcesbpvc6vcfvc7sbqpcktbrvc8vc9vcotcwtcutcavcnvcjvclvcpvcqschvcgvd2scxvcvvcytczvcstctvcrvd0vd1vd9vdbvdatdctd4sd6vd8vdrtd3sddvdttdvtdevdssd7vduvdntd5vdfvdisdztdltdxtdptdjvdosdgve0sdmse2sdkvdhve1se4ve3vdyse5vgxve8vekvejvg7se7se9vemvg8velveaveovg9ve6sdqsgasecveesenvebvedseqvgcvepvgbvervgdsegvefvehvesvf7vf8vetvdwsggsf9veisfavghvfbvfcvewseyseusgqvgjsfivfdvflvfevexvffvfnvfovfmvfjvfrvfgvfkvevvfqvftvfsvfpvfhvezvfwsfusfxvfvvgksfysf0sf2sf1vgfvf3sf6sfzvf4vf5ph3tgrvh9tg3vg0vgisg2sg1sh7tgevg6sgssgtsg4vglvguvgmsgnvgovg5ph5tgpvh4vhavh8vh6vgvvgwvhbshfthgvgyshhthivhdthevhjthkvhcvhlvhmvh1sgzsh2yhovhrvhuvhxvhpthsti0yhvti7shqvhyti1si6yi5yhtvh0yhwvhzvi2si3si8si4y"
-_OLD6 = "00y01s02y03s04y0hv08p19v2yp1fv1av1ds0ps1kv1ov1lv1mv1jv0cp09p1nv0ap0bp2zv0lv3bv1pv0js0ep30v1cv34v1ys0dp1zs37v0mv26v0wp2cv29v1xs0ip25v2av0up24v32v33v21s1ts31v2rv2ds3pv2bv3mv18v23s20s3qv2sv1ss35s36v2gs3nv2is2vs2es2qp0fp3rv4dv1rs1ws0ks3os2ks2fs2hs2js0sp05y4bv4et38v0vp3sv1ev2wv2mv1bv4gs06y39v2lv4ct3tv07y16p4fs2xv1gp3wv3vv15p0qp3ds3uv3cs17s3es3fs1vs2ns43v44s0ns4hv4kv3gv3jv0gp10p3xv0xp2ov11p3hv1qs22s1us3kv4jv4iv0yp4pt4xt0zp3zv46s14p45s53s4lv54s4mv4av48v49v47v55v4rt4zt56v2pv40v4ss3iv4ys13p5lv5mv5av3lv12p4qs41s4vt5nv4nt5ov5bv59s57v3yv50s7ds4ws0rp58s4tt51t5pv5qv4os4us5cv27v5rv5sv42v5ev5dv28v5tv2uv1iv0tv5uv5gs5fs0ov3av2tv52s7ev5vv1hv5hv5iv5jv7fs5wv5ys60s5ks69v6av5xv7gs5zv6cv7ms6bv7iv7hs61v6ev6dv65s64s62s7nv63v6nv6gv6kv6hv6fv7js6pv7ps6ov6tv66v6mv6lv6iv6qv6vv7wv6ys6uv67p6ws7os6jv6sv6rv7xv6zv70s6xv7ys7qs79v7zs71v74s72s80v73v75v7av78s76v68s7lv7kv7bv77p7rv7cv7ssh5v7tv7uv87t88v83t84v89t8av85t86v8bs7vv8dt8ev8ft8gv8jt8kv8ht8iv8cv8ls81v8mv82v8wv8ns8uv8xt9gt8ps8vt9ct8zv98t8os9et8yv9at8tv8rv9kt96t90v8qv93s9hs8sv9it99s91v9fs94v92v9ms9ns95v9dv9ov9pv9bs9qv9ss9js9tva5vbtsa4v9uva7vbuv97sa6v9vva9vbvva8vbws9xv9zs9wvabvaav9rvbyv9ysbxvacvbzsa1va0va2vadvasvarvc2sa3saevauvatvc3vawv9lsavvahsc4sc0vayvazvb2vaxvb5vccvbbvb0vc5sb4vb3vb8vb7vafsajsb6vbesbgsbdvaivbcvbavb9vb1vbisagvbfvc6sbhvakvcdvbjvansalscesc1vamvbnvblvbmsbksaovc7vbqvbovapvbsvaqvcgvbpvcfsc8sbrpcavc9vcbvchvcivcjtckvctscuscvscltcmvcntcovcptcqvcrvcsvcwvd2vd0vd3tdmtcyvcxvd1tdktd5vdetdnsdgtd4vditdlsczvdctdqtdfsd9vdotd6sdpsdhvdavd7vdtsdssdjsd8vdbvdvvduvdysdwvdzvfzseavdxsddse0vebvg0vecve1vedvg1veevg2se3ve5se2vefvegvg4ve4sg3sg5sehvgpveive7ve6ve8vejvexvg8se9seyvg6vezvf0vg9vekvdrsf1venselsepsf2vg7vf3vf8vgasfbvf5vf4vfevfavf9vfdvf6vfcvfhvemvffvfksfgvf7vfjvfmsfivgbsfoseovflvfnveqvfpvesvgiveuvgcsftversfqvetsfrsfsvgdvfwvgjvgesfuvewvgksfvvevvglsgfvggvgmvghvgnvgovfxpfysgqsgrsgtsgsyh1th2vguygzth0vgxtgyvgvtgwvh3vh4vh9vh6vhcvhfvhnshqshath7thiyhjyhdthgthoyhbvh8vhevhhvhkshlyhmshpy"
-_OLD5 = "04y02y00y03s08p2yp0dp0hv01s1cv3bv18v0ls0ap0bp1ov1kv1nv1lv1mv0js1jv1fv2zv19v1ev1pv1ys1av09p34v37v0mv1zv0cp25v29v0ep0up30v24v2av20s1ws23s0ip26v33v2cv2rv2vs1rs32v31v2qp2bv2dv2js35s1xs1ss2sv3pv38v3mv2wv36v2ks2es2gs2is0wp0vp3qv2fs21s0ks2hs1dp0fp3nv39v0sp3rv2xv4bv3os3cs1ts3sv3ts3dv4dv3vv3wv3es4ct2lv3fs22s43v4et3gv2mv27v15p1us4fs3zv3uv05y06y07y4gs2ns44s1vs16p3kv3xv3hv4hv4rt1gp41s0xp4zt0qp4kv4iv46s4lv45s0gp4av2ov48v10p0pp3jv49v1qs53s0rp47v54s55v56v4ss2pv3iv57v4xt0yp4pt50s5lv11p4ys4qs58s7ds5mv4vt1bv3lv4ws4nt5nv5ov0zp4tt5av40v5pv51t4os5qv4jv4us5rv13p5sv4mv5tv3yv5bv59v12p5uv7ev52s0ns42v5vv5cv28v1hv14p7fs17v5ev5ws5dv5ys5gs5fs0ov2uv0tv60s2tv5xv5zv1iv7gs5hv5iv5jv61v69v5ks63s64s65s6av7iv6bv68v6cv62v7hs7js6dv6ev7ms66v6kv6fv6nv6gv6hv67p6lv6mv6qv6pv6ov6tv6iv6ws6rv6sv6uv6jv6vv6ys7nv6xv70s85t6zv7os7lv7ps71v7wv72s75s87t7kv74v73v79v7qs78s76v7rv7av7xv77p7sshnv83t7ys7zs7bv7tv7uv86v88v84v89t8av8bs7cv80v8ft8gv8jt8kv8ht8iv8dt8ev8cv8lv7vv8mv3av81v8uv8wv82v8vt8xt8ns9gt8yv98t8zv9at9hs9it93s9kt9ct8pv90v9et96t8rv94v99s8os9js91v9ns8tv9ms8sv8qv9bs92v9pv9ov95v9ds9tvbssa4v9ssa5v9ls9uv9qv9fsa6vbtva7v9vv9rva8v97sa9vbus9xv9wvaavabv9zsbxv9ysacva0va1vbvsbysadva2vasvatva3vc1sauvaevavvbwsawvafsahsc2vaxvayvajscbvc4sc3sb3vb6vb0vazvagvb7vb4vb5vb8vb9vbfsbhsbcvb1vaivbavbbvb2vbevbdvakvbgvbivamvbjsaosalsansc5sc0varsbkvapvccvbnvblsbmsbovbzvaqpbrvcdscesbpvc6vcfvc7sbqpcktc8vc9vcitcmtclvcavcotcjvcnvcpvcqschvcgvd2scytcwtcxvczvcstctvcutcvvcrvd0vd1vd9vdbvdatdctdrtd4sd6vd3sd5vgxvddvdttdvtdevd8vdssduvdntdisd7vdztdltdxtdptdfvdjve0sdosdgvdkve2sdhve1se3ve4vdmse7se5ve8vg7sdysejvekvdqse6se9vg8vemveavelvg9veovgasebvedsenvecveqvepvgcveesgbvervgdsegvefvehvesvf7vf8vetvdwseivggsf9vfavghvfbveysfcvewseusgqvgjsfdvfivflvfevffvfovfjvfkvfmvfrvfgvfnvevvexvftvfhvfsvfusfqvfwsfpvezvfxvgksfysfvvf3sf2sf0sf1vgfvf6sfzvf4vf5ph3tgrvg3vg0vgish7tgevg1sg2sg6vgssgtsg4vglvguvgmsgnvgovg5ph9th5thfthdth4vgpvhavh8vh6vgwvgvvhhthgvhevhivhbsgyshjthkvhcvhlvhmvh1vgzsh0yh2yhovhrvhuvhxvhpthsti0shvti7shqvhyti5yhtvi1yhwvhzvi2si3si4yi6yi8s"
-_OLD4 = "01s03s0hv08p2zp3cv0bp1lv1pv1nv1qv1mv0js0ls04y1dv1ov0ap02y1kv1hv30v1bv1rv09p1jv00y1gv1ev0cp31v38v2bv27v26v1yv2av20s1zs21s0dp1fp0ep1vs1us25s2ks22v1cv0ip34v2cv35v36s2sv33v2iv3qv32v1ts3nv2dv2ls2ws3rv2tv37v39v2es2js0ks28v3ov3ps2nv3sv2xv3av2fv3ds2hs4cv2yv13p3ev3tv2rp4ev2gs3gs4dt3lv3us3fv06y05y4ft44v1ip4gs3hv07y0pp2os4hs45s0yp3wv3xv10p0gp3iv3vv0sp3kv23s1ws47s46s0mv2mv4kv4wt4ot4qt4iv4yt24s4lv4jv4xs1sv53v40v3yv52v48v55s49v4bv54s4av0zp4rs57v42s0fp0xp56v4zs3mv2pv4ps50t5nv78s5mv41v4st5pv58v59s5ov29v0tp2qv5rv18p5qv3jv5tv5sv5bv4mt4ts5as3zv79v5uv5cv0vv4ut51s4ns1as5vv5dv4vv5wv14p5ev0wv5fv19p0uv5zv5xs5gs5hs0ns5yv43s61s1xs5iv5jv7as7hs60v6av6bv0ov5kv62v6cv6dv7dv64v6ev6fv65v2vv2uv17p5ls66s0qp63s6iv67v69s6gv7es15p11p68p6jv6hv7iv6lv6kv0rp6ov7rv6nv6mv7bs6vv6qv6pv6rs6ts7cs6sv7ks82t6uv7js84t7gv6wv6ys70s7fv3bv6zv6xv7ls7mv7sv71v7ns73s74v72p7us7pv12p7ts75v7ov76v80t7qv16p83v85v81v7yt7zv77v88t89v8ct8dv8et8fv86s8at8bv87v8gs7vv8hv7wv8rv8pv8st7xv8qt8uv97t93t8is8tv95t98v9dt99t8vs8zt9bt91t8xv8js8wv8ks8yv9fv8lv9gv9nv8nv9hs8mv8ov9is96s9lv9kv9jvh6v9mv9cs9as9es9ova0v9zv9pva2v94sa1v9qva4va3v9sv9rva6va5vbhv9us9ts92s90sa7v9wv9vva8v9xvaova9vanvaqvbqsacs9yvbivapvbrvasvarvadvatvauvaasavvbjsbksabvawvayvbmvaesblsb1vaxvb4safvb0vb3vazvajvagvb2vb6vc0vaisahsakvalpb7vbnsb8sb5vc7tamsbtsbssbovb9vbpvc9tcbtbcvbbvc1vbasbdsbgsbvvbevc2vbuvbwsc4vbyvbxvbfpc3sc8vbzvcavccvcdtcevc5vc6vcfscgvcrsctscjtckvchtcivcsscltcmvcntcovcpvcqvcvvd0vcyvcwvcxvd1tcztd3vdctdetd2vditddvdgtd6sdktdhsdatdmtdjsd4vd8td7vd5vdpvdovcuvdrsdqsdbvdsvdtvggvduvd9sdxve9vdlsdyvdwsfqsdnsdvse8vebvdzveavfrvedve0vecve1vfsse2sefveeve3sfvvftsdfsegve4ve5ve6vehvexvewvfwseivezveyvejse7vf1vf0velsf3vf2vf4vensekvfzsfusf5vemvf6vffsf7vfavfdseovf9versfbvfcvessf8vepveqvg0vfgvfevetvfhsfivfyvg9vg2seupfmsfjsfkvg1sgotflvfxvg3sfpsfnvg4vgavgcvfopgqtg5sg7vgmtg6vevsgbsgdvg8vgpvgstgwtgrvgevgytgtvgnvgfvghsguvgxvgzvh2th3vh0th1vgvvh4sh5vhavh7vhgvhbthdvgksglyh8tgisgjyhjyhhthryhkyhcshethpsh9vhivhfvhoyhlshnshqshmy"
-_OLD3 = "00y03s08p02y0hv1dv01s04y0bp39v1iv1lv09p1jv1kv1mv1nv1av18v0ls0vs0ap0dp19v1ov23v1bv0ws2wp0mv1cp24v28v1xv1ys1ws1vs0cp27v22s25v2xv0ep2gs2hs29v1ev3nv31v2av2yv2es2pv30v32v35v0up0jp1zs33s2fs2bs2ts2zv2qv3kv1rs3ms3ov36v34v0ip3lv37v3pv2uv1ss2op3as3bs49v3qv4bv2cs3uv2kv3cv0fp3tv2vv0kv2dv2is3ds3ev3rs3sv2jv4at41v0sp4ct4ds05y4es06y3fv07y0pp1qs2ls20s4fv42s16p4hv21s15p4gv4iv2mv4zv0xp3iv50v3vv1ps44s46v43s51s3xv48v4nt52s45v47v54v53v4vt3jv26v2nv1fp1us3zs0gp10p5jv5kv4xt55v1ts3hv4os4ws4pt4tt5lv57s75s0yp5mv58v5nv11p5ov3gv59v56v5pv5qv4lt0zp4ys4qs4us4jt1hv1gv4ks4rt4ss5av5rv4mv5bv5sv3wv5cv76v3yv13p5tv5ds5es40s0tv17v5uv5ws0ns5ys5fv2rv5gv5hv14s77s5vv0rp7es0qp5xv12p67v68v5is5zv69v6av0ov2sv63v6bv6cv61v62v7av6fv60s64v6dv78s7bs6ev79s66s6gv7fv6iv6lv6hv7gv65p6jv6kv6ov7dv6nv6qs6mv6ss6pv6rv7cv7ov7hs7is6tv7jv7pv6uv6vs6wv6xv70v7ksh3v7qs6yv7mv7rs71v7lv6zp7sv7xt7zt7vt72v7nv81t87t7yv80v7wv82v73v83s8bt84v8cv85t89t88v86v8av74v8ds8ev7uv8ov8mv8pt7tv38v8nt8rv8wt8fs90t8qv96t8xs9at8us98t8yt94t91v8sv8hs92t8vv8gs8tv9dv8lv9cv8jv9fs9es9bs8iv8kv9gv9hv9ks97s9iv9lv9js9wv9mv9xv8zs9yv9nv95s9zva0v9pva1v9ova2v9rsa3v9qsbeva4v99s9sv9tv93sbfv9uva5vakvalvbnsa6vbgs9vsamvanva7sbovaovapva9sbxvaqvabsbhsarvasva8vatvaavbpsauvayvavvacvb3sb0vazvb1sagsafsaxvawvaevadvb4vb5sb2vbisahvajsbyvb6vaipbjvb8vb7vbavb9vbdvbksbzvbbvbqsc1vbmvbcpblvc0sbrvbsvbtsbvvbuvc8tc9vc6tc7vcatcbvc4tc5vccvbwvcdvcitcgtcetcjvchvcfvcktclvc2vcmvc3vcnvcoscqscvvcxvcpscwtcytczvddtd5tdbtd0vdescuvd7td6vd3vd9td1sdftdhtdjtdcsd2vd8sd4vdasdlvgdvdmvctvcsvcrvdnsdosdqvdpvdgsdisdtsdrvduvfnse6vdssdvve5ve8vdwvfove7veavdxvdyvdkse9vfpsecvdzse0sfsvebvfqse2ve1vftsedve3veuvetvfrse4seevewvevvfwsefveyvexvegveiseksf1vezvf0vejvf2vehvf3vf4vf7vfxvelvfasf5vf6vf8vfcsf9vensepvemveosfbvfesfdvfyseqvfzsg6vffverpfuvessfhvfgvfjvfivfvvg0sfkvg7vg1vfmvg8sg9vflpg2sgavg3vg4vg5vgjtgkvgltgmvgntgovgptgqvgbvgrvgcvgsvgesghsgztgvtgfsh0vgwvgiygttggygxtguvgyvh1vh2vh7vh4vhavhdvh8th5thgyhbthethoyhlyhhyhnyhmsh9vh6vhcvhfvhishjyhks"
-_OLD2 = "03s08p0hv02y04s01s00y0ap39v18v1iv09p0ls1jv1mv1nv1lv1kv0bp2wp0us1ev1bv1av0ws1ov0vs23v0dp0mv1cs19v1dv2kv2xv24v25v0cp28v1xs27v2yv30v1ws1ys35v0ep20s1zs1rs22s2es2gs3nv1vs0ip2av0jp2pv2op29v31v3ov2ts33s3kv32v2zv1qs2bs3ms3pv2qv3lv2is3qv36v2hs2cs34v2ls49v3tv2uv2fs0fp4at3rs1ss2ds2jv0kv37v4bv15p4ds3hv3xv2vv4ct3uv3sv3bs3as2mv0sp4es1ps06y05y07y3vv3jv3cs3ds41v0pp4lt4tt4ms3zs4fv16p4hv21s1ts3ev4gv42s0xp4iv1us4xt4pt17s3fv26v2nv4zv50v1fp43v4us44s0gp52s51s4ys4qs57s10p0yp3iv4vt3gv4jt45v4ws46v48v47v54v53v55v56s4ks75s4rt4nt3yv3wv11p5kv5jv40v5mv1gv5lv0zp58v5ov4ss0ns5nv2sv59v5qv5pv14p4os2rv5av5rv0qv5bv5cv12p5sv76v0tv5ds5es5tv0ov38v77s1hv13p5us5wv5fv5hv5ys5gv5xv0rs5vv5is78s68v67v7es5zv6av69v63v6cv62s6bv60v61v7fv79s6ev6fv7hs64v6dv6gv6lv7gs65p7av7bs6iv6hv6nv6mv7ov6kv6jv6ov6qs6ss7cv7is6pv7vt7xt6rv7dv6tv7jv7pv6vv6wv6xs6uv70v7ks7qsh3v6yv7rs71v7lv6zp7mv7sv72v7zt66s7wv7yv80v81t87t8bt82v73v7nv83s84v89t8av85t86v88v8cv74v8ds8ev7uv8mv8ov8nt7tv8pt8qv96t8fs8wt8rv94t97s92t8sv8us9at8yt90t8xv8hs98t8vv8gs8tv9dv8jv9cv8lv9fs8kv9es8iv9bs9hv9gv9ks95s9iv9lv9js9xv9mv9wv9zv9nv93s91s9yva1v99s9ova0v9pva3v9qsa2v9rsbeva4v9sv9tvbfv9uva5v8zsbnsakv9vsalvbgsa6vamvanva7saovbovapva9saqvbxvabsasvarva8vbhsatvaavbpsauvavvayvacvb1sawvaxvazvb3sb0vagvaesafsadvb2vb5sb4vbisahvb6vbjvajsaipbyvb8vb9vb7sbavbksbzvbdvbbvbqsbmvblvbcpc0sbrvbsvbtsc1vbuvc6tc7vc4tc5vcatcbvc8tc9vbvvcgtccvbwvcdvcetcitchvcfvcktcjvclvc2vcmvc3vcnvcoscpscvvcxvcqscwtcrvcytczvdbtddtd0vd7tdcsdhtcuvcsvd1sd3vdjtd9td5tctvdisdftgdvd2vd8sd4vdesdlvdmvdtvdkvdnsdosdpvdqvd6sdasdgsdrvduvfnse5vdssdvve6ve7vdwvfove8ve9vdyvdxveavebvfpse0secvdzsfsvfqsedve1ve2ve3vftseevetve4seuvfrsefvevvewvegsexveyveisezveksf1vf0vehvf2vfwsejvf3vf4vf7vfuvfasf6vf5velvfcsf9vf8vfbvfesfdvepsemseosenvfxvessffvfyseqvg6vfivfhvfjvfgsfvvfkvg7verpfzsfmsg1vg8vflpg0vg2sg9vg3vg4vgavg5vgbvgptgltgcvgntgjtgqvgesgmvgovgkvgxtgrvgyvghsgttguvgzth0vgvtgwvgsvh1sgiygfsh2vggyhevhhyh9vhjvhmyh4vhcyhathbvhfthgvhkthlvhoshqshdyhpsh5thiyh6shrsh8yh7yhny"
-_OLD = "1dv39v0hv1ev08p1iv0bp1lv1jv2wp03s1mv0ap01s1kv1nv18v00y2xv0ep1bv19v1ov1av32v04y0ls0mv02y06y35v2yv24v2kv05y0cp28v2av09p07y2zv0dp27v0us23v0ws1xs1ys31v3nv30v2pv29v25v3ov1zs3kv2qv0jp36v3pv1vs2op1ws22s2bs2ts2is33s34v3lv3qv2uv49v0ip4bv2vv2es2gs2fs20s2jv37v0kv2cs2hs3uv3tv3iv3ms3rs3sv3vv0vs1cp4at4ct1rs1ps3xv2ds41v4ds4es2ls3bs3as0fp4fv4hv0sp3zs1ss0pp3ds3cs1ts16p3ev15p4gv1fp3fv4iv42s3jv4zv2mv1us50v0xp43v17s44s46v51s52s48v1qs45v47v54v0qp21s53v0rp10p0yp55v4nt4pt3hv4xt5mv4vt5lv56v2nv5ov0gp26v4os11p5nv4qs0ns59v4ys57s0zp58s4tt4us4ws4lt5qv5pv12p3gv5av5sv5rv5tv4jt5bv5uv0tv5cv5dv5vv4ms13p4rt4ks4sv14p5wv2rv5iv5fs5es1hv1gv3wv3yv5hv2sv5gv5zs60v5xs5yv6bv6av40s61s7hs78s62v5jv79v66s6dv6cv63s65v64v5kv6fv7as6ev7bs7iv0ov67v6iv68p80t6hv7dv6jv6gv7js69s7es6ov7rv6kv6lv7cv6qv6ts82t7sv6nv6pv6mv6rs6vs84t6uv7ks6sv7ts7fv6wv6xs7ls7gv6zv6yv70v7yt7mv7vv71v72p7ns74v7pv7ov8at88t8et8ct75v81v83v85v7zv76v7qv73s7us86s87v8bv89v8fv8dv77v8gs38v8hv7xv8pv8rv8qt7wv8st8tv93t8is95t8uv8zt94s99t9bthcv8vs8xv9dt97t91t96v8ks8wv8js8yv9fv8ov9gv8mv9hs8lv8nv9is9cs9lv9kv9jv9os90s9mv9pv9nva2v9qva1v9esa4v9rva3va6v9sv92s98s9tva5va8vbkva9v9us9vsa7v9as9yvblv9wv9xvaav9zvbmsaqvarva0sbnsabvasvatvacvbtsauvavvbpvadsawvayvafsaxvb1vahsbuvazvaevbqsb0vb4vagvb7sb3vb2vb5vb6vb9saivb8vbbsbavalsamsajvaksapsbovbcvanvbsvbgvbdvbvsbesbfsaopbwsbrvbhvc3vbjvbyvbipbxvc4vbzsc1vc5sc6sc0vc7vc2vcgtchvc8vcetcctcatcfvcdvcbvc9vcivcuscktclvcqtcrvcmtcnvcotcpvcjvcsscwsctvd0vd1vd3vcvscxvd2tcyvgmvd4td5vdhtdbtd6vdltczvdisddtdftd7sd9vdntdptdjtdmvdcsd8vdesdavdgsdrvdsve0vdtsdusdxvdqvdosdvvdwvdksdyvdzseeve1vfwsedvegve2vfxvefveive3vehvfysfzsekve4ve6se5ve7sejvelvg1vemveavg2senve9ve8vebveovf3vg5sf2vepsecvf5versg6vf4vetsf7vgfvf6veqvg0sfavggvf8vf9vg7sfbvg8sesvghsfcvfgvfdveuvfjsfevffvfivfhvflsewvexseysevvfkvfnsfmvezvf0pgutgstgytg9sfovf1sfrsfssfqsgwtg4vg3vfvsgjvfpvgavftvfupgbsgisgcvgdvgevgvvgtvgzvgxvglvh0vgkvh1vh2th3vh4th8th9vgnsgqsgosgrygpyh5vh6th7vhavhbvhqvhhvhdvhmvhrthithethlyhnthuyhwyhxyhyyhvshjvhsshfvhovhgyhtyhkyhps"
-PLAN = {"seed": 1, "passes": 120, "moves": 16000}
+LINK = 0.24
+PACES = ((0.24, 0.0, 0.92, 0.02, 1.0, 0.35, 0.95, -0.45), (0.27, 0.0, 1.3, 0.02, 0.4, 0.6, 1.4, 0.0))
+HEAT = (0.05, 0.004)
+PLAN = {"seed": 1, "passes": 300, "moves": 110000, "short": (1, 1, 0, 1, 0, 1), "early": 0, "steps": 1, "sums": 3,
+        "xcut": (0, 256, 384, 512),
+        "gcut": (0, 8, 16, 24, 32), "vcut": (0, 4)}
 
 
 def order(ops, seed, passes, moves):
@@ -66,7 +61,6 @@ def order(ops, seed, passes, moves):
     for i in range(n):
         for k in need[i]:
             users[k].append(i)
-    lat = [o["lat"] for o in ops]
     dur = [{q: a[1] for q, a in o["alt"].items()} for o in ops]
     state = [seed]
 
@@ -77,105 +71,159 @@ def order(ops, seed, passes, moves):
     def pick(xs):
         return xs[int(rnd() * len(xs))]
 
-    def lay(rank, before, back, toll):
-        busy = {q: [] for q in "vstpy"}
-        start, end, on = [0.0] * n, [0.0] * n, [""] * n
-        for i in sorted(range(n), key=lambda k: rank[k]):
-            r = max([end[k] + WAKE + 0.03 for k in before[i]] + [0.0]) + (lat[i] if back else 0.0)
-            best = None
-            for q, d in dur[i].items():
-                b, t, lo, hi = busy[q], r, 0, len(busy[q])
-                while lo < hi:
-                    mid = (lo + hi) // 2
-                    if b[mid][1] <= t:
-                        lo = mid + 1
-                    else:
-                        hi = mid
-                while lo < len(b) and b[lo][0] < t + d - 1e-9:
-                    t = b[lo][1]
-                    lo += 1
-                e = t + d + (toll if q == "v" and len(dur[i]) > 1 else 0.0)
-                if best is None or e < best[0]:
-                    best = (e, t, q, d, lo)
-            busy[best[2]].insert(best[4], (best[1], best[1] + best[3]))
-            start[i], end[i], on[i] = best[1], best[1] + best[3] + (0.0 if back else lat[i]), best[2]
-        return start, end, on
-
-    def run(seq, on, wake, slow, trace=False):
+    def lay(rank, signal, wake, pace, margin, soon):
         free = {q: 0.0 for q in "vstpy"}
-        last = {q: -1 for q in "vstpy"}
-        done, why = [0.0] * n, [None] * n
-        for i in seq:
+        left, due = [len(x) for x in need], [0.0] * n
+        pool, seq, on = [i for i in range(n) if not need[i]], [], [""] * n
+
+        def end(x, q):
+            return (free[q] if due[x] <= free[q] else due[x] + wake) + pace[q][x]
+
+        while pool:
+            pool.sort(key=lambda i: rank[i])
+            first, q = min((max(free[k], due[i]), k) for i in pool for k in dur[i])
+            mine = [i for i in pool if q in dur[i]]
+            x = top = [i for i in mine if due[i] <= first + soon][0]
+            if due[top] > free[q]:
+                fits = [i for i in mine if due[i] < due[top] and end(i, q) <= due[top] + wake - margin]
+                x = ([i for i in fits if due[i] <= free[q]] + fits + [top])[0]
+            if x == top:
+                q = min(dur[x], key=lambda k: end(x, k) + (0.05 if k == "v" else 0.0))
+            free[q] = end(x, q)
+            on[x] = q
+            seq.append(x)
+            pool.remove(x)
+            for u in users[x]:
+                left[u] -= 1
+                due[u] = max(due[u], free[q] + lat[x] + signal)
+                if not left[u]:
+                    pool.append(u)
+        return seq, on
+
+    paces = []
+    lats = []
+    for signal, wake, slow, extra, weight, calls, way, load in PACES:
+        paces.append({q: [(d.get(q, 0.0) * slow + (extra if q == "s" else 0.0) if o["kind"] == "call" else d.get(q, 0.0) + calls * (o["kind"] == "send")) for o, d in zip(ops, dur)] for q in "vstpy"})
+        lats.append([way if o["kind"] == "send" else o["lat"] + load * (o["kind"] != "call") for o in ops])
+    lat = lats[0]
+    stones = [i for i in range(n) if ops[i]["kind"] == "send" or ops[i]["name"][:2] == "XQ"]
+
+    def run(seq, on, s, old, at):
+        signal, wake = PACES[s][:2]
+        pace, lat, done, free = paces[s], lats[s], list(old), {}
+        for i in seq[at - 1::-1] if at else ():
+            if on[i] not in free:
+                free[on[i]] = done[i] - lat[i] - signal
+                if len(free) == 5:
+                    break
+        for q in "vstpy":
+            free.setdefault(q, 0.0)
+        for i in seq[at:]:
             q = on[i]
-            s, w = free[q], (last[q], True)
+            a, m = free[q], 0.0
             for k in need[i]:
-                if done[k] + wake > s:
-                    s, w = done[k] + wake, (k, False)
-            why[i], last[q] = w, i
-            free[q] = s + dur[i][q] * slow
-            done[i] = free[q] + lat[i]
-        m = max(done)
-        if not trace:
-            return m
-        i, arcs = done.index(m), []
+                if done[k] > m:
+                    m = done[k]
+            if m > a:
+                a = m + wake
+            a += pace[q][i]
+            free[q] = a
+            done[i] = a + lat[i] + signal
+        return done
+
+    def value(seq, on, olds=None, at=0, limit=1e9, parts=None):
+        total, dones = 0.0, []
+        for s in range(len(PACES)):
+            dones.append(run(seq, on, s, olds[s] if olds else [0.0] * n, at))
+            total += max(dones[s]) * PACES[s][4]
+            if parts and total + sum(parts[s + 1:]) - 0.6 > limit:
+                return None
+        return total + 0.1 * sum(dones[0][i] for i in stones) / len(stones), dones
+
+    def chain(seq, on, dones):
+        s = 0 if rnd() < 0.5 else int(rnd() * len(PACES))
+        done, signal, lat = dones[s], PACES[s][0], lats[s]
+        prev, last = {}, {}
+        for i in seq:
+            prev[i] = last.get(on[i], -1)
+            last[on[i]] = i
+        links, i = [], pick(stones) if rnd() < 0.3 else done.index(max(done))
         while i >= 0:
-            k, queued = why[i]
-            if queued and k >= 0:
-                arcs.append((k, i))
-            i = k
-        return arcs
+            p = prev[i]
+            k = max(need[i], key=lambda z: done[z]) if need[i] else -1
+            idle = k >= 0 and done[k] > (done[p] - signal - lat[p] if p >= 0 else 0.0)
+            if idle or p >= 0:
+                links.append((k if idle else p, i, idle))
+            i = k if idle else p
+        return links
 
-    def value(seq, on):
-        return run(seq, on, WAKE, 1.0) + 0.5 * run(seq, on, 1.4 * WAKE, 1.3)
+    def ahead(seq, lo, hi, x):
+        part, moved = seq[lo:hi], {x}
+        for z in reversed(part):
+            if z in moved:
+                moved.update(need[z])
+        return seq[:lo] + [z for z in part if z in moved] + [z for z in part if z not in moved] + seq[hi:], moved
 
-    def sound(p, before, ids):
-        for i in ids:
-            for k in before[i]:
-                if p[i] <= p[k]:
-                    p[i] = p[k] + 1e-6
-        return p
+    def behind(seq, lo, hi, x):
+        part, moved = seq[lo:hi], {x}
+        for z in part:
+            if z in moved:
+                moved.update(users[z])
+        return seq[:lo] + [z for z in part if z not in moved] + [z for z in part if z in moved] + seq[hi:], moved
 
     tail = [0.0] * n
     for i in range(n - 1, -1, -1):
-        tail[i] = min(dur[i].values()) + lat[i] + max([tail[u] + WAKE for u in users[i]] + [0.0])
+        tail[i] = min(paces[0][q][i] for q in dur[i]) + lat[i] + max([tail[u] + LINK for u in users[i]] + [0.0])
     best, base = None, [-x for x in tail]
     for it in range(passes):
-        toll, amp = pick((0.0, 0.1, 0.2, 0.4)), pick((0.05, 0.15, 0.3))
-        p = sound([x + amp * rnd() for x in base], need, range(n))
-        for rep in range(2):
-            start, end, on = lay(p, need, False, toll)
-            seq = sorted(range(n), key=lambda i: (start[i], i))
-            v = value(seq, on)
-            if best is None or v < best[0]:
-                best, base = (v, seq, on), start
-            end = lay(sound([-x for x in end], users, range(n - 1, -1, -1)), users, True, toll)[1]
-            p = sound([-x for x in end], need, range(n))
-    now, seq, on = best
-    arcs = run(seq, on, WAKE, 1.0, True)
+        amp = pick((0.02, 0.1, 0.3))
+        rank = [x + amp * rnd() for x in base]
+        for k in range(pick((0, 1, 3, 10))):
+            rank[int(rnd() * n)] += 3 * rnd() - 1.5
+        seq, on = lay(rank, PACES[0][0] + pick((0.0, 0.02, 0.04)), PACES[0][1], paces[0], pick((0.0, -0.05, -0.1)), pick((0.15, 0.3, 0.5)))
+        v = value(seq, on)[0]
+        if best is None or v < best[0]:
+            best, base = (v, seq, on), rank
+    seq, on = best[1:]
+    now, dones = value(seq, on)
+    links = chain(seq, on, dones)
     for it in range(moves):
-        a, b = pick(arcs)
-        r = rnd()
-        seq2, on2 = seq, on
+        a, b, idle = pick(links)
+        r, pb = rnd(), seq.index(b)
+        seq2, on2, x, q = seq, on, -1, on[b]
         if r < 0.2 and len(dur[a]) + len(dur[b]) > 2:
             x = a if len(dur[a]) > 1 and (len(dur[b]) == 1 or rnd() < 0.5) else b
-            on2 = list(on)
-            on2[x] = pick([q for q in dur[x] if q != on[x]])
+            q, at = pick([k for k in dur[x] if k != on[x]]), seq.index(x)
+        elif idle:
+            far = pick((20, 60, 150))
+            near = [z for z in (seq[pb + 1:pb + far] if r < 0.75 else seq[max(0, pb - far):pb]) if q in dur[z]]
+            if not near:
+                continue
+            x = pick(near)
+            px = seq.index(x)
+            at = min(pb, px)
+            seq2, moved = ahead(seq, pb, px + 1, x) if r < 0.75 else behind(seq, px, pb, x)
+            if b in moved:
+                continue
+        elif r < 0.6:
+            at = max(0, seq.index(a) - pick((0, 0, 0, 2, 6, 15)))
+            seq2 = ahead(seq, at, pb + 1, b)[0]
         else:
-            p = {x: y for y, x in enumerate(seq)}
-            early = r < 0.6
-            todo = [(b, p[a] - pick((0, 0, 2, 6, 15)) - 0.5)] if early else [(a, p[b] + pick((0, 0, 2, 6, 15, 40)) + 0.5)]
-            while todo:
-                x, v = todo.pop()
-                if p[x] > v if early else p[x] < v:
-                    p[x] = v
-                    todo += [(k, v - 1e-4) for k in need[x]] if early else [(k, v + 1e-4) for k in users[x]]
-            seq2 = sorted(seq, key=p.get)
-        v = value(seq2, on2)
-        if v <= now + 0.01 * rnd():
-            now, seq, on = v, seq2, on2
-            arcs = run(seq, on, WAKE, 1.0, True) if rnd() < 0.7 else run(seq, on, 1.4 * WAKE, 1.3, True)
-            if v < best[0]:
-                best = (v, seq, on)
+            at = seq.index(a)
+            seq2 = behind(seq, at, pb + 1 + pick((0, 0, 0, 2, 6, 15, 40, 80, 160)), a)[0]
+        if x >= 0 and on[x] != q:
+            on2 = list(on)
+            on2[x] = q
+        limit = now - HEAT[0] * (HEAT[1] / HEAT[0]) ** (it / moves) * math.log(rnd() + 1e-9)
+        new = value(seq2, on2, dones, at, limit, [max(d) * p[4] for d, p in zip(dones, PACES)])
+        if new and new[0] <= limit:
+            (now, dones), seq, on = new, seq2, on2
+            links = chain(seq, on, dones)
+            if now < best[0]:
+                best = (now, seq, on)
+        elif rnd() < 0.05:
+            links = chain(seq, on, dones)
+    PLAN["est"] = [max(d) for d in value(best[1], best[2])[1]]
     return [(i, best[2][i]) for i in best[1]]
 
 
@@ -224,10 +272,7 @@ def make_plan(g, T):
     def issue():
         if "seq" not in PLAN:
             PLAN["ops"] = ops
-            if len(ORDER) == 3 * len(ops):
-                PLAN["seq"] = [(int(ORDER[k:k + 2], 36), ORDER[k + 2]) for k in range(0, len(ORDER), 3)]
-            else:
-                PLAN["seq"] = order(ops, PLAN["seed"], PLAN["passes"], PLAN["moves"])
+            PLAN["seq"] = order(ops, PLAN["seed"], PLAN["passes"], PLAN["moves"])
         count = {}
         known = {q: {} for q in eng}
         mark = {}
@@ -280,7 +325,7 @@ def rank_program(g, core, T, topo):
         for v in ins:
             if v[2] < 0:
                 return (0.05 if q == "v" else 0.065) - v[2] * 0.0013
-        return max(64, max(v[2] for v in [out] + ins) * per) * CYC + (0.05 if q == "s" else 0.0)
+        return max(64, max(v[2] for v in [out] + ins) * per) * CYC
 
     def rate(*vs):
         return 0.5 if all(v[3] for v in vs) else 1.0
@@ -317,9 +362,6 @@ def rank_program(g, core, T, topo):
     def cp(out, a):
         note({"v": v_cp(out, a)}, [out], [a])
 
-    def act(out, a, func, scale=1.0):
-        note({"s": s_act(out, a, func, scale)}, [out], [a] + cols(scale))
-
     def move(out, a, scale=1.0, bias=None):
         if bias is not None:
             alt = {"v": v_ts(out, a, scale, OP.mult, bias, OP.add), "s": s_act(out, a, AF.Identity, scale, bias)}
@@ -338,8 +380,8 @@ def rank_program(g, core, T, topo):
     def const(out, c):
         one = f("ONE", 0, out[2])
         alt = {"v": (lambda e: e.memset(out[0], c), cost("v", out, [], rate(out))), "s": s_act(out, one, AF.Copy, c)}
-        if c == 0.0:
-            alt["p"] = (lambda e: e.iota(out[0], [[0, out[2]]], 0, 0, allow_small_or_imprecise_dtypes=True), 0.13 + 2 * CYC * out[2])
+        if c == int(c) and abs(c) < 2 ** 24:
+            alt["p"] = (lambda e: e.iota(out[0], [[0, out[2]]], int(c), 0, allow_small_or_imprecise_dtypes=True), 0.13 + 2 * CYC * out[2])
         note(alt, [out], [one])
 
     def scan(out, d0, d1, init, op0, op1):
@@ -369,132 +411,108 @@ def rank_program(g, core, T, topo):
 
     dma("y", f("NDI"), hbm(T.nd[:, :]), 1.3, "load")
     dma("s", f("UT"), hbm(T.u[:, :]), 1.7, "load")
-    dma("y", f("XT", 0, 1024), hbm(T.x[:, 0:1024]), 2.5, "load")
-    dma("s", f("XT", 1024, 2048), hbm(T.x[:, 1024:2048]), 3.0, "load")
-    dma("y", f("ARI"), hbm(T.ar[:, :]), 3.5, "load")
+    early = PLAN["early"]
+    if early:
+        dma("y", f("ARI"), hbm(T.ar[:, :]), 2.2, "load")
+    dma("s" if early else "y", f("XT", 0, 1024), hbm(T.x[:, 0:1024]), 2.5 + 0.5 * early, "load")
+    dma("y" if early else "s", f("XT", 1024, 2048), hbm(T.x[:, 1024:2048]), 3.0 + 0.5 * early, "load")
+    if not early:
+        dma("y", f("ARI"), hbm(T.ar[:, :]), 3.5, "load")
     for out, src in ((f("WQ", cast=dt.uint8), T.wc), (f("WS"), T.ws), (f("VT"), T.v)):
-        dma("y", out, (src[:, :], f("ARI")[1]), 2.5)
+        dma("y", out, (src[:, :], f("XT" if early else "ARI")[1]), 2.5)
 
     iota(f("PI", 0, 1), [[0, 1]], 0, 1, small=False)
-    iota(f("N"), [[1, 88]])
-    iota(f("E64"), [[0, 2], [1, 2], [0, 16]])
-    iota(f("HE", 0, 4), [[1, 2], [0, 2]])
+    iota(f("N"), [[1, 64]])
+    iota(f("BP"), [[0, 6], [1, 4], [0, 2]])
+    iota(f("HE"), [[16, 2], [0, 2]])
+    iota(f("XE"), [[0, 2], [1, 2]])
+    iota(f("B3"), [[16, 2], [0, 3]])
     iota(f("K32"), [[0, 2], [1, 16]])
-    iota(f("DU"), [[64, 2], [0, 2], [4, 16]], 2048)
-    iota(f("W1"), [[384, 2], [24, 16]], -1)
-    iota(f("BP"), [[0, 6], [1, 4], [0, 2]], MID)
-    iota(f("B4"), [[1, 4]], MID)
+    iota(f("DU"), [[1, 16]], 512)
+    iota(f("C8"), [[8, 64]], 3)
+    iota(f("PP"), [[1, 16], [256, 2]])
+    iota(f("IOT"), [[4, 512]])
     fill(f("ONE"), 1.0)
     ident, one = f("ID"), f("ONE", 0, 128)
     note({"p": (lambda e: e.affine_select(ident[0], one[0], [[-1, 128]], OP.is_equal, 0.0, 0, 1), 0.38)}, [ident], [one])
     const(f("ET"), 0.0)
     move(f("ET", 3, 515, 4), ident)
-    const(f("FOLD"), 2 * BIG)
-    fill(f("FOLD", 0, 256, 16), -2 * BIG)
-    const(f("KEEP"), 1.0)
-    fill(f("KEEP", 0, 256, 8), 0.0)
+    for b in range(4):
+        quant("EQ", "ES", 128 * b, 128 * b + 128, f("ET", 3 - b, 515 - b))
     for t in range(R):
         const(f("F%d" % t, 2048, W), 0.0)
     const(f("YT", 0, 512), 0.0)
     quant("LQ", "LS", 96, 224, f("YT", 0, 512))
-    for a in (0, 544, 1088):
-        const(f("TAB", a, a + 32), 0.0)
-    for n in ("SP0", "SP1", "SPX"):
-        const(f(n), 0.0)
-    for n, j in (("D0F", 0), ("D0S", 0), ("D0X", 0), ("TD", 1), ("TD", 2), ("D0Y", 0), ("D1Y", 1)):
-        const(f(n, j, 768, 3), 0.0)
+    const(f("TAB", 512, 544), 0.0)
+    const(f("TBL", 3, 512, 8), 0.0)
+    const(f("OA2", 512, 528), 0.0)
+    const(f("D0Y", 0, 768, 3), 0.0)
+    const(f("D1Y", 1, 768, 3), 0.0)
     const(f("D1Y", 0, 768, 3), -BIG)
-    fill(f("TA", 1024, 1040), MARK)
-    fill(f("Z", 512, 513), -BIG / 32)
-    fill(f("Z", 513, 528), -1.5 * BIG)
-    fill(f("RX", 52, 103), -2 * BIG)
-    fill(f("RB", 15, 560, 16), -2 * BIG)
+    const(f("TS", 512, 513), -BIG)
+    const(f("TN", 512, 544), 0.0)
+    if PLAN["sums"] > 1:
+        const(f("KEEP", 0, 384), 1.0)
+        const(f("KEEP", 384, 768), 1.0)
+        const(f("KEEP", 0, 768, PLAN["sums"]), 0.0)
+    const(f("CAP"), 2.0 ** 23)
+    const(f("CAP", 0, 64, 16), NONE)
+    const(f("CAP", 64, 129, 16), NONE - 2048)
     for j in range(2):
-        const(f("RA%d" % j, 3 * KS + 32, 4 * KS, 32), 0.0)
-        fill(f("RA%d" % j, 0, 1), BIG)
-        fill(f("RA%d" % j, KS, KS + 1), -BIG)
+        const(f("KY%d" % j, 512, 513), NONE)
 
     pi = f("PI", 0, 1)
-    for j, (sh, m) in enumerate(((0, 15), (4, 1), (0, 31), (3, 1), (0, 7), (0, 1))):
+    for j, (sh, m) in enumerate(((0, 15), (4, 1), (0, 31), (3, 1), (0, 1))):
         ts(f("BITS", j, j + 1), pi, sh, OP.logical_shift_right, m, OP.bitwise_and)
-    cp(f("SC", 0, 6), f("BITS", 0, 6))
-    pm, e = f("pm"), f("e")
-    for n, src, sc, bi in (("A", "e", -32.0, 32.0), ("B", "e", 32.0, None), ("e1", "e", -1.0, 1.0),
-                           ("p0", "p31", 1 / 32.0, None), ("p1", "e", -16.0, f("p0")), ("e16", "e", 16.0, None),
-                           ("sO", "pm", -4096.0, 61440.0 - 67584.0), ("sI", "pm", 4096.0, 63488.0), ("sb", "pm", 8.0, 783.0),
-                           ("s1", "qh", 1.0, f("ql")), ("qh16", "qh", 16.0, None), ("t66", "qh", float(KS), 32.0), ("dl", "h1", 32.0, f("t66")),
-                           ("zb", "pm", 16.0, -497.0)):
+    cp(f("SC", 0, 5), f("BITS", 0, 5))
+    pm, x = f("pm"), f("x")
+    for n, src, sc, bi in (("x16", "x", 16.0, None), ("pm32", "pm", 32.0, None), ("cs", "pm", -STEP, 12 * U + 15 * STEP), ("dl", "qh", 2.0, f("h1")),
+                           ("nil", "pm", 1.0, float(EMPTY))):
         move(f(n), f(src), sc, bi)
+    ts(f("DL", 0, 3), f("N", 0, 25, 12), f("dl"), OP.add, 16.0, OP.mult)
     ts(f("UL"), f("N", 0, 8), 16.0, OP.mult)
-    ts(f("NDL"), f("HE", 0, 4), 16.0, OP.mult, pm, OP.add)
+    ts(f("NDL"), f("HE"), pm, OP.add)
     ts(f("SPG"), f("N", 0, 64, 32), f("p31"), OP.add)
-    ts(f("DL", 0, 3), f("N", 0, 3), 2.0 * KS, OP.mult, f("dl"), OP.add)
-    ts(f("DK", 0, 1), f("dl"), 4.0, OP.add)
-    ts(f("ISO"), f("E64"), e, OP.is_equal)
-    ts(f("NIS"), f("E64"), e, OP.not_equal)
-    tt(f("DUM"), f("DU"), f("NIS"), OP.mult)
-    ts(f("OWN", 0, 32), f("K32"), pm, OP.not_equal, -BIG, OP.mult)
-    for n in (32, 64, 128):
-        move(f("OWN", n, 2 * n), f("OWN", 0, n))
-    for h in range(2):
-        move(f("CB", 32 * h, 32 * h + 32), f("ISO", 0, 32), f("sI"), (12 - 8 * h) * U - 63488.0 - MID)
-        move(f("CB", 64 + 32 * h, 96 + 32 * h), f("ISO", 0, 32), f("sO"), (4 + 8 * h) * U + 67584.0 - MID)
-    move(f("T6", 0, 4), f("HE", 0, 4), 256.0, f("zb"))
-    tt(f("T6", 4, 8), f("T6", 0, 4), f("ISO", 0, 64, 16), OP.mult)
-    ts(f("zg"), pm, 15.0, OP.not_equal, e, OP.mult)
-    move(f("T6", 8, 12), f("NIS", 0, 64, 16), f("zg"), 512.0)
-    tt(f("T6", 12, 16), f("T6", 4, 8), f("T6", 8, 12), OP.add)
-    cp(f("ZWL"), f("T6", 12, 16))
-    iota(f("KU"), [[4096, 136]])
-    ts(f("JI"), f("K32", 0, 32, 2), f("s1"), OP.add, 1.0, OP.add)
-    ts(f("JJ"), f("JI"), 15, OP.bitwise_and)
-    for h in range(2):
-        ts(f("COLG", 8 * h, 8 * h + 8), f("JJ", 8 * h, 8 * h + 8), f("e16"), OP.add, 32.0 * h, OP.add)
-    move(f("T7", 0, 16), f("N", 0, 16), 32.0, f("qh16"))
-    tt(f("T7", 16, 32), f("T7", 0, 16), f("JJ"), OP.add)
-    cp(f("CIRC"), f("T7", 16, 32))
-    iota(f("DDI"), [[0, 2], [-1, 16]], 16, 1, small=False)
-    ts(f("DI4"), f("DDI"), 15, OP.bitwise_and)
-    d = f("DI4")
-    ts(f("T1", 0, 32), d, 3.0, OP.mult)
-    tt(f("T2", 0, 32), f("T1", 0, 32), f("W1"), OP.add)
-    for h in range(2):
-        ts(f("T3", 16 * h, 16 * h + 16), f("DI4", 16 * h, 16 * h + 16), -1.0, OP.mult, f("sb"), OP.add)
-    ts(f("T4", 0, 32), d, 8.0, OP.is_gt)
-    move(f("T3", 16, 32), f("T3", 16, 32), 1.0, 128.0)
-    tt(f("T8", 0, 32), f("T3", 0, 32), f("T4", 0, 32), OP.mult)
-    ts(f("T5", 0, 32), d, 0.0, OP.is_equal, 1024.0, OP.mult)
-    tt(f("T0", 0, 32), f("T2", 0, 32), f("T5", 0, 32), OP.max)
-    tt(f("T1", 0, 32), f("T0", 0, 32), f("T8", 0, 32), OP.max)
-    cp(f("OUT"), f("T1", 0, 32))
-    fill(f("T9", 0, 34, 33), 1024.0)
-    for h in range(2):
-        move(f("T9", 1 + h, 33, 2), f("T1", 16 * h, 16 * h + 16))
-    move(f("T2", 0, 33), f("T9", 0, 33), e)
-    move(f("T3", 0, 33), f("T9", 1, 34), f("e1"))
-    tt(f("T5", 0, 33), f("T3", 0, 33), f("T2", 0, 33), OP.add)
-    cp(f("EXP", 0, 33), f("T5", 0, 33))
-    for b in range(4):
-        quant("EQ", "ES", 128 * b, 128 * b + 128, f("ET", 3 - b, 515 - b))
+    ts(f("BV"), f("B3"), pm, OP.add, 16.0, OP.mult)
+    ts(f("BV2"), f("BV", 2, 4), f("x16"), OP.subtract)
+    ts(f("COL", EMPTY, 544), f("DU"), f("x16"), OP.add, 4.0, OP.mult)
+    move(f("CBU"), f("C8"), U)
+    ts(f("T0"), f("XE"), x, OP.not_equal, 1024.0, OP.mult)
+    tt(f("T3"), f("T0"), f("HE"), OP.add)
+    ts(f("ZWL"), f("T3"), f("pm32"), OP.add, 512.0, OP.min)
+    ts(f("PA"), f("PP"), f("BV", 0, 1), OP.add)
+    ts(f("T4"), f("K32"), pm, OP.is_equal, 1024.0, OP.mult)
+    tt(f("T5"), f("T4"), f("N", 0, 32), OP.add)
+    ts(f("PB"), f("T5"), f("pm32"), OP.add, 512.0, OP.min)
 
     quant("UQ", "US", 0, 128, f("UT"))
     cp(f("UQR", cast=dt.uint32), f("UQ", cast=dt.uint32, ind=("UL",)))
     move(f("USR"), f("US", ind=("UL",)))
     ts(f("NDD"), f("NDI", ind=("NDL",)), 4.0, OP.mult)
-    tt(f("NDM"), f("NDD"), f("ISO"), OP.mult)
-    tt(f("NWI"), f("NDM"), f("DUM"), OP.add)
-    turn(f("NW"), f("NWI"))
+    turn(f("NW"), f("NDD"))
     move(f("N4"), f("NW", ind=("SPG",)))
-    ts(f("SL"), f("N4"), 0.25, OP.mult)
-    for io in range(2):
-        tt(f("CC", 64 * io, 64 * io + 64), f("CB", 64 * io, 64 * io + 64), f("NDM"), OP.add)
     for h in range(2):
-        a, b = f("KU", 34 * h, 34 * h + 16), f("KU", 52 + 50 * h, 84 + 50 * h)
-        tt(a, a, f("N4", 16 * h, 16 * h + 16), OP.add)
-        tt(b, b, f("NW", 32 * h, 32 * h + 32), OP.add)
-    move(f("KT", 0, 52), f("KU", 0, 52), 2.0 ** -24)
-    move(f("KT", 52, 136), f("KU", 52, 136), 2.0 ** -24)
-    ts(f("TA", 2, 768, 3), f("ARI", ind=("CIRC",)), U, OP.mult)
+        ts(f("SL", h, 32, 2), f("N4", 16 * h, 16 * h + 16), 0.25, OP.mult)
+    turn(f("NM"), f("N4"))
+    move(f("CC"), f("NM"), 1.0, f("cs"))
+    ts(f("NL"), f("NM"), 0.25, OP.mult)
+    for a in range(2):
+        move(f("COL", 256 * a, 256 * a + 256), f("IOT", ind=("NL", 16 * a, 16 * a + 16)))
+    if PLAN["steps"]:
+        for h in range(2):
+            ts(f("ARB", 256 * h, 256 * h + 256), f("ARI", 256 * h, 256 * h + 256), U, OP.mult)
+            const(f("ARB", 256 * h, 256 * h + 256, 17), MARK)
+        for j in range(16):
+            turn(f("TAB", j, 512, 16), f("ARB", j, 512, 16))
+    else:
+        ts(f("PD"), f("N", 0, 32), f("pm32"), OP.add)
+        for a in range(2):
+            ts(f("ARB", 256 * a, 256 * a + 256), f("ARI", ind=("PA", 16 * a, 16 * a + 16)), U, OP.mult)
+        for h in range(2):
+            const(f("ARB", 16 * h, 512, 33), MARK)
+        turn(f("OA1"), f("ARB"))
+        for a in range(2):
+            move(f("TAB", 256 * a, 256 * a + 256), f("OA1", ind=("PD", 16 * a, 16 * a + 16)))
 
     nxt = T.cores[(rank + 1) % len(T.cores)]
     rid, pid, _ = topo.addr(nxt)
@@ -514,68 +532,43 @@ def rank_program(g, core, T, topo):
             e.remote_dma(lq[0], q[0], T.sem[sem], T.sem["left"], pid, rid, mask)
             e.remote_dma(ls[0], s[0], T.sem[sem], T.sem["left"], pid, rid, mask)
             return sem, 2 * len(engines), 2 * len(engines)
-        note({"p": (go, 0.6 if t or j else 2.1)}, [lq, ls], [q, s], 1.5, "send")
+        note({"p": (go, 0.0 if t or j else 1.5)}, [lq, ls], [q, s], 0.0, "send")
 
-    def table():
-        move(f("TA", 768, 1024), f("TA", 2, 768, 3), -1.0)
-        for a, b in ((0, 16), (16, 33)):
-            move(f("EX", 16 * a, 16 * b), f("TA", ind=("EXP", a, b)))
-        for h in range(2):
-            lo = 32 + 544 * h
-            for a in range(2):
-                turn(f("TAB", lo + 256 * a, lo + 256 * a + 256), f("EX", 16 * h + 256 * a, 16 * h + 256 * a + 256))
-
-    def choose(j, src):
-        n, at = 16 + 16 * j, 52 * j
-        buf, st = ("RX", 1) if j else ("RB", 16)
-        for h in range(2 * j):
-            a = at + 1 + (n + 18) * h
-            scan(f("RX", a, a + n), src(h), src(h), -2 * BIG, OP.max, OP.max)
-        for h in range(2):
-            lo, hi = at + (n + 1) * h, at + n + 1 + (n + 18) * h
-            below(f("JK", lo, hi), f(buf, st * lo + st - 1, st * hi, st), f(buf, st * hi - 1, st * hi), f("IX", 2 * j + h, 2 * j + h + 1))
-        for k, a in enumerate("AB"):
-            ts(f("L4", 4 * j + k, 4 * j + 4, 2), f("IX", 2 * j, 2 * j + 2), f("p%d" % j), OP.add, f(a), OP.mult)
-        w = 2 * n + 18
-        scan(f("SK", at, at + w), f("JK", at, at + w), f("KT", at, at + w), 0.0, OP.max, OP.min)
-        move(f("RA%d" % j, 2 * KS + 32, 2 * KS + 65, 32), f("SK", at + n - 1, at + w, n + 18), 2.0 ** 24, -float(MID))
+    def chosen(j):
+        return ("L2", 0, 2) if j else ("L1", 2, 4)
 
     def slots(j, t):
-        ft, gk, ky, ra, rc = "F%d" % t, "GK%d" % j, "KY%d" % j, "RA%d" % j, "RC%d" % j
-        l4 = ("L4", 4 * j, 4 * j + 4)
-        sides = ((0, OP.min, OP.max, BIG), (1, OP.max, OP.min, -BIG))
-        for io in range(2):
-            tt(f(gk, 64 * io, 64 * io + 64), f("TAB", ind=l4), f("CC", 64 * io, 64 * io + 64), OP.add)
-        for io in range(2):
-            turn(f(ky, 64 * io, 64 * io + 64), f(gk, 64 * io, 64 * io + 64))
-        for io, a, b, big in sides:
-            k = f(ky, 64 * io, 64 * io + 64)
-            scan(f(ra, KS * io + 1, KS * io + 65), k, k, big, a, a)
-        for io, a, b, big in sides:
-            scan(f(rc, KS * io + 1, KS * io + 65) if j else f(ra, KS * (4 + io) + 1, KS * (4 + io) + 65), f(ky, 64 * io, 64 * io + 64), f(ra, KS * io, KS * io + 64), big, a, b)
+        ft, gk, ky = "F%d" % t, "GK%d" % j, "KY%d" % j
+        short = PLAN["short"][2 * t + j]
         lo, y = 48 * j, 384 * j
-        if j:
-            tt(f("DI", 64, 80), f(ra, 128, 4 * KS, ind=("DK", 0, 1)), f("BP", 0, 16), OP.add)
+        move(f(gk, 0, 32), f("COL", ind=chosen(j)))
+        for io, tab in enumerate(("TAB", "TN")):
+            tt(f(gk, 32 + 32 * io, 64 + 32 * io), f(tab, ind=chosen(j)), f("CC"), OP.add)
+            if short:
+                move(f(gk, 96 + 32 * io, 128 + 32 * io), f(tab, ind=chosen(j)), 1.0, f("cs"))
+        w = 64 + 64 * short
+        turn(f(ky, 0, 32 + w), f(gk, 0, 32 + w))
+        k = f(ky, 32, 32 + w)
+        scan(f(ky, 513, 513 + w), k, f("CAP", 1, 1 + w), NONE, OP.max, OP.min)
+        scan(f(ky, 177, 177 + w), f("CAP", 0, w), k, BIG, OP.min, OP.max)
+        scan(f(ky, 369, 369 + w), k, f(ky, 512, 512 + w), NONE, OP.max, OP.min)
+        if short:
+            for h in range(2):
+                ts(f("LL", lo + h, lo + 8, 2), f("N", 0, 4), f(ky, 16 * h, 16 * h + 1), OP.add)
+            for top in range(2):
+                for n in range(4):
+                    a, c = lo + 16 + 16 * top + 8 * (n // 2), 192 + 192 * top + 16 * n
+                    ts(f("LL", a + n % 2, a + 8, 2), f("N", 0, 4), f(ky, c, c + 1), OP.add, f(ky, c + 64, c + 65), OP.subtract)
         else:
-            tt(f("DI", 0, 48), f(ra, ind=("DL", 0, 3)), f("BP", 0, 48), OP.add)
-        a, n = (64, 8) if j else (0, 48)
-        ts(f("DM", a, a + n), f("DI", a, a + n), 4095, OP.bitwise_and)
-        cp(f("LL", a, a + n), f("DM", a, a + n))
-        for io in range(2 * j):
-            ts(f("HI", 4 + 2 * io, 6 + 2 * io), f(ra, KS * io + 32, KS * io + 65, 32), 1.5 * 2.0 ** 35, OP.add, -1.5 * 2.0 ** 35, OP.add)
-            for h in range(2):
-                c = KS * io + 32 * h + 32
-                ts(f("LL", lo + 8 * io + h, lo + 8 + 8 * io, 2), f("B4"), f(ra, c, c + 1), OP.add, f("HI", 4 + 2 * io + h, 5 + 2 * io + h), OP.subtract)
-        for io in range(2 * j):
-            ts(f("HI", 2 * io, 2 * io + 2), f(rc, KS * io + 32, KS * io + 65, 32), 1.5 * 2.0 ** 35, OP.add, -1.5 * 2.0 ** 35, OP.add)
-            for h in range(2):
-                c = KS * io + 32 * h + 32
-                ts(f("LL", lo + 32 + 8 * io + h, lo + 40 + 8 * io, 2), f("B4"), f(rc, c, c + 1), OP.add, f("HI", 2 * io + h, 2 * io + h + 1), OP.subtract)
+            di, dm = f("DI", lo, lo + 48), f("DM", lo, lo + 48)
+            tt(di, f(ky, 0, 512, ind=("DL", 0, 3)), f("BP"), OP.add)
+            ts(dm, di, 4095, OP.bitwise_and)
+            cp(f("LL", lo, lo + 48), dm)
         for io in range(2):
             ab = f("AB", 256 * j + 128 * io, 256 * j + 128 * io + 128)
-            move(ab, f(ft, ind=("LL", lo + 8 * io, lo + 8 * io + 8)))
+            move(ab, f(ft, ind=("LL", lo + 16 + 8 * io, lo + 24 + 8 * io)))
             tt(f("D0Y", y + 1 + io, y + 384, 3), f(ft, ind=("LL", lo + 32 + 8 * io, lo + 40 + 8 * io)), ab, OP.add)
-        move(f("D1Y", y + 2, y + 384, 3), f(ft, ind=("LL", lo + 16, lo + 24)), -2.0)
+        move(f("D1Y", y + 2, y + 384, 3), f(ft, ind=("LL", lo, lo + 8)), -2.0)
         scan(f("YS", y, y + 384), f("D0Y", y, y + 384), f("D1Y", y, y + 384), 0.0, OP.max, OP.add)
         for b in range(4):
             move(f("YT", 512 * j + b, 512 * j + 128, 4), f("YS", y + 96 * b + 2, y + 96 * b + 96, 3), 0.5)
@@ -590,78 +583,93 @@ def rank_program(g, core, T, topo):
             lo = 128 * j + 32 * b
             mm(f("PS", at, at + 128), f("WQ", 128 * b, 128 * b + 128), f("WS", 128 * b, 128 * b + 128), f("LQ", c, c + 128), f("LS", c, c + 128))
             tt(f("V32", lo, lo + 32), f("PS", at + 96 * j, at + 96 * j + 32), f("YW", lo, lo + 32), OP.add)
-        move(f("VV", 128 * j, 128 * j + 128), f("V32", 128 * j, 128 * j + 128), 0.03125)
-        cp(f("F%d" % t, ind=("LL", 48 * j + 16, 48 * j + 24)), f("VV", 128 * j, 128 * j + 128))
+        cut = PLAN["vcut"] if j else (0, 4)
+        for a, b in zip(cut, cut[1:]):
+            lo, hi = 128 * j + 32 * a, 128 * j + 32 * b
+            move(f("VV", lo, hi), f("V32", lo, hi), 0.03125)
+            cp(f("F%d" % t, ind=("LL", 48 * j + 2 * a, 48 * j + 2 * b)), f("VV", lo, hi))
 
-    def operands(j, d0, d1):
-        x = f("X2", 64 * j, 64 * j + 64)
-        move(f("XG", 64 * j, 64 * j + 64), f("TAB", ind=("L4", 4 * j, 4 * j + 4)))
-        turn(x, f("XG", 64 * j, 64 * j + 64))
-        move(f("SP%d" % j, 0, 256, 8), f("X2", 64 * j, 64 * j + 64, ind=("SPG",)), -0.5)
-        move(f(d0, 2, 768, 3), f("X2", 64 * j, 64 * j + 64, ind=("COLG",)), 1.0 / U)
-        o, i = f(d0, 1, 768, 3), f(d0, 2, 768, 3)
-        note({"v": v_ts(o, i, 1.0, OP.min, -1.0, OP.max), "s": s_act(o, i, AF.Sign)}, [o], [i])
-        scan(f(d1, 0, 768, 3), f("KEEP"), f("SP%d" % j), 0.0, OP.mult, OP.add)
-        act(f(d1, 1, 768, 3), f(d1, 0, 768, 3), AF.Abs)
-
-    def steps(dst, d0, src):
-        for h in range(2):
-            lo, hi = 384 * h, 384 * h + 384
-            scan(f(dst, lo, hi), f(d0, lo, hi), f(src, lo, hi), 0.0, OP.mult, OP.add)
+    def arrows(last):
+        xg, d4, a2, n2, na = f("XG"), f("XW", 0, 64), f("XW", 64, 128), f("XW", 128, 192), f("XW", 192, 256)
+        for j in range(2):
+            move(f("XG", 32 * j, 32 * j + 32), f("TAB", ind=chosen(j)))
+        ts(d4, xg, MARK, OP.is_equal, 4 * U, OP.mult)
+        note({"v": v_ts(a2, xg, 0.0, OP.max, 2.0, OP.mult), "s": s_act(a2, xg, AF.Relu, 2.0)}, [a2], [xg])
+        ts(n2, xg, 0.0, OP.min, 2.0, OP.mult)
+        tt(na, d4, a2, OP.subtract)
+        pos = f("TBL", 5, 512, 8)
+        tt(pos, n2, d4, OP.add)
+        for k, src, c in ((0, na, -1.5), (1, na, -1.0), (2, na, -0.5), (4, pos, 0.5), (6, pos, 1.5)):
+            move(f("TBL", k, 512, 8), src, c)
+        tt(f("TBL", 7, 512, 8), na, pos, OP.subtract)
+        tt(f("XI", 0, 64), xg, f("CBU"), OP.add)
+        tt(f("XI", 64, 128), f("XI", 0, 64), d4, OP.add)
+        ts(f("LA"), f("XI", 64, 128), 1.0 / U, OP.mult)
+        n = PLAN["sums"]
+        for a in range(2):
+            lo, hi = 256 * a, 256 * a + 256
+            e1, e2 = [f("TBL", ind=("LA", 32 * j + 16 * a, 32 * j + 16 * a + 16)) for j in range(2)]
+            if n == 1:
+                tt(f("T1", lo, hi), e1, f("TAB", lo, hi), OP.add)
+                tt(f("T2", lo, hi), e2, f("T1", lo, hi), OP.add)
+            else:
+                if n == 2:
+                    tt(f("T1", 2 * lo, 2 * hi, 2), e1, f("TAB", lo, hi), OP.add)
+                else:
+                    move(f("T1", 3 * lo, 3 * hi, 3), f("TAB", lo, hi))
+                    move(f("T1", 3 * lo + 1, 3 * hi, 3), e1)
+                move(f("T1", n * lo + n - 1, n * hi, n), e2)
+                scan(f("T2", n * lo, n * hi), f("KEEP", 0, 256 * n), f("T1", n * lo, n * hi), 0.0, OP.mult, OP.add)
+        for lo, hi in PLAN.get("clip", ((0, 256), (256, 512))):
+            ts(f("TAB", lo, hi), f("T2", n * lo + n - 1, n * hi, n), 3 * U, OP.min, -3 * U, OP.max)
+        if last:
+            for a in range(2):
+                move(f("OA1", 256 * a, 256 * a + 256), f("TAB", ind=("PA", 16 * a, 16 * a + 16)))
+            turn(f("OA2", 0, 512), f("OA1"))
+            for h in range(2):
+                move(f("OAO", 256 * h, 256 * h + 256), f("OA2", ind=("PB", 16 * h, 16 * h + 16)), 1.0 / U)
+                dma("y", hbm(T.oa[:, 256 * h:256 * h + 256]), f("OAO", 256 * h, 256 * h + 256), 2.2)
 
     for t in range(R):
         ft, xq, xs = "F%d" % t, "XQ%d" % t, "XS%d" % t
         src = "F%d" % (t - 1) if t else "XT"
-        table()
         for a in range(2):
-            quant(xq, xs, 256 * a, 256 * a + 256, f(src, 1024 * a, 1024 * a + 1024))
-            mm(f("PS", 512 * a, 512 * a + 256), f("UQR"), f("USR"), f(xq, 256 * a, 256 * a + 256), f(xs, 256 * a, 256 * a + 256))
-        for a in range(2):
-            if t:
-                tt(f("PW", 256 * a, 256 * a + 256), f("PS", 512 * a, 512 * a + 256), f("CM", 256 * a, 256 * a + 256), OP.add)
-            else:
-                move(f("PW", 256 * a, 256 * a + 256), f("PS", 512 * a, 512 * a + 256))
-        for h in range(2):
-            o, i = f("SG", 256 * h, 256 * h + 256), f("PW", ind=("SL", 16 * h, 16 * h + 16))
-            if t:
-                move(o, i)
-            else:
-                tt(o, i, f("OWN", 0, 256), OP.add)
-            scan(f("RB", 544 * h + 16, 544 * h + 272), o, o, -2 * BIG, OP.max, OP.max)
-            scan(f("Z", 256 * h, 256 * h + 256), f("FOLD"), o, 0.0, OP.min, OP.max)
+            o, i = f("TZ", 256 * a, 256 * a + 256), f("TAB", 256 * a, 256 * a + 256)
+            note({"s": s_act(o, i, AF.Abs, 2.0 ** 90), "v": v_ts(o, i, 0.0, OP.not_equal, BIG, OP.mult)}, [o], [i])
+            move(f("TN", 256 * a, 256 * a + 256), i, -1.0)
+        XCUT, GCUT = PLAN["xcut"], PLAN["gcut"]
+        for a, (lo, hi) in enumerate(zip(XCUT, XCUT[1:])):
+            quant(xq, xs, lo, hi, f(src, 4 * lo, 4 * hi))
+            mm(f("PS", 512 * a, 512 * a + hi - lo), f("UQR"), f("USR"), f(xq, lo, hi), f(xs, lo, hi))
+            move(f("PW", lo, hi), f("PS", 512 * a, 512 * a + hi - lo))
+        for lo, hi in zip(GCUT, GCUT[1:]):
+            move(f("SG", 16 * lo, 16 * hi), f("PW", ind=("SL", lo, hi)))
+            turn(f("TS", 16 * lo, 16 * hi), f("SG", 16 * lo, 16 * hi))
         for a in range(2):
             for b in range(4):
-                at = 1024 + 512 * b if a == 0 else (3072, 3584, 0, 512)[b]
+                at = 2048 + 512 * b if a == 0 else (1536, 0, 512, 1024)[b]
                 mm(f("PS", at, at + 256), f("EQ", 128 * b, 128 * b + 128), f("ES", 128 * b, 128 * b + 128), f(xq, 256 * a, 256 * a + 256), f(xs, 256 * a, 256 * a + 256))
                 move(f(ft, 1024 * a + b, 1024 * a + 1024, 4), f("PS", at, at + 256))
-        choose(0, lambda h: f("Z", 256 * h + 15, 256 * h + 256, 16))
-        move(f("ZW"), f("Z", ind=("ZWL",)))
-        ts(f("GM"), f("TAB", ind=("L4", 0, 4)), 0.0, OP.not_equal, BIG, OP.mult)
-        turn(f("GT"), f("GM"))
-        tt(f("S2"), f("ZW"), f("GT"), OP.subtract)
-        choose(1, lambda h: f("S2", 32 * h, 32 * h + 32))
+        move(f("ZW"), f("TS", ind=("ZWL",)))
+        turn(f("ZM"), f("ZW"))
+        for e in range(2):
+            s, r = f("TS", 16 * e, 512, 32), 16 * e
+            scan(f("RX", r, r + 16), s, s, -BIG, OP.max, OP.max)
+            below(f("JK", r, r + 16), f("RX", r, r + 16), f("RX", r + 15, r + 16), f("IX", e, e + 1))
+            ts(f("L1", 3 * e, 3 * e + 3), f("BV", 3 * e, 3 * e + 3), f("IX", e, e + 1), OP.add)
+        for e in range(2):
+            lo = 32 * e
+            tt(f("GM", lo, lo + 32), f("TZ", ind=("L1", 4 * e, 4 * e + 2)), f("ZM", lo, lo + 32), OP.subtract)
+            s, r = f("GT", lo, lo + 32), 32 + lo
+            turn(s, f("GM", lo, lo + 32))
+            scan(f("RX", r, r + 32), s, s, 4 * BIG, OP.min, OP.min)
+            below(f("JK", r, r + 32), f("RX", r, r + 32), f("RX", r + 31, r + 32), f("IX", 2 + e, 3 + e))
+        ts(f("IX", 4, 6), f("RX", 63, 96, 32), 1.0e23, OP.is_gt, f("nil"), OP.mult)
+        for e in range(2):
+            ts(f("L2", e, e + 1), f("BV2", e, e + 1), f("IX", 2 + e, 3 + e), OP.subtract, f("IX", 4 + e, 5 + e), OP.max)
         slots(0, t)
         slots(1, t)
-        if t == 0:
-            for a in range(4):
-                cp(f("CM", ind=("SL", 8 * a, 8 * a + 8)), f("OWN", 0, 128))
-        operands(0, "D0F", "TA")
-        steps("TB", "D0F", "TA")
-        operands(1, "D0S", "TB")
-        steps("TC", "D0S", "TB")
-        ts(f("TD", 0, 768, 3), f("TC", 2, 768, 3), 3.0 * U, OP.min, -3.0 * U, OP.max)
-        ts(f("DD"), f("X2"), MARK, OP.is_equal, -2.0, OP.mult)
-        tt(f("SN"), f("DD", 0, 64), f("DD", 64, 128), OP.add)
-        move(f("SPX", 0, 256, 8), f("SN", ind=("SPG",)), 1.0, 1.0)
-        move(f("D0X", 1, 768, 3), f("SN", ind=("COLG",)), 1.0, 1.0)
-        scan(f("D0X", 2, 768, 3), f("KEEP"), f("SPX"), 0.0, OP.mult, OP.add)
-        steps("TA", "D0X", "TD")
-        if t == R - 1:
-            fill(f("TA", 1024, 1040), 0.0)
-            move(f("TA", 768, 1024), f("TA", 2, 768, 3), -1.0)
-            for a in range(2):
-                move(f("OAO", 256 * a, 256 * a + 256), f("TA", ind=("OUT", 16 * a, 16 * a + 16)), 1.0 / U)
-                dma("y", hbm(T.oa[:, 256 * a:256 * a + 256]), f("OAO", 256 * a, 256 * a + 256), 2.2)
+        arrows(t == R - 1)
         anew(0, t)
         anew(1, t)
 

import math
from concourse.mybir import dt, AluOpType, ActivationFunctionType

OP = AluOpType
AF = ActivationFunctionType
R = 3
W = 2176
U = 65536.0
STEP = U / 16
MARK = 0.125
BIG = 1.0e29
NONE = 12 * U + 15 * STEP + 2048
EMPTY = 528

CODES, PLANE, BF, F32, I32, U16 = "float8_e4m3fn_x4", "uint8", "bfloat16", "float32", "int32", "uint16"
SCRATCH = {"PS": ("psum", [128, 4096], F32)}
for _n, _w, _d in (
    ("XT", 2048, BF), ("UT", 512, BF), ("VT", 512, BF), ("ET", 528, BF), ("ONE", 528, BF), ("ID", 128, BF),
    ("UQ", 128, CODES), ("US", 128, PLANE), ("UQR", 128, CODES), ("USR", 128, PLANE), ("VQ", 128, CODES), ("VS", 128, PLANE),
    ("WQ", 512, CODES), ("WS", 512, PLANE), ("EQ", 512, CODES), ("ES", 512, PLANE), ("LQ", 320, CODES), ("LS", 320, PLANE),
    ("NDI", 32, I32), ("ARI", 512, I32), ("IA", 16, I32), ("FA", 864, F32), ("SC", 32, F32), ("SM", 32, U16),
    ("UL", 8, U16), ("SL", 32, U16), ("NL", 32, U16), ("PA", 32, U16), ("PB", 32, U16), ("PD", 32, U16), ("LA", 64, U16), ("L1", 8, U16), ("L2", 2, U16), ("LL", 96, U16),
    ("NW", 64, F32), ("IOT", 512, F32), ("COL", 544, F32), ("ARB", 512, BF),
    ("PW", 512, F32), ("SG", 512, F32), ("TS", 528, F32), ("RX", 96, F32), ("JK", 96, BF), ("IX", 8, F32),
    ("ZW", 64, F32), ("ZM", 64, F32), ("GM", 64, F32), ("GT", 64, F32),
    ("TAB", 544, BF), ("TZ", 512, BF), ("T1", 1536, BF), ("T2", 1536, BF), ("KEEP", 768, BF), ("TBL", 512, BF), ("XG", 64, BF), ("XW", 256, BF), ("XI", 128, F32),
    ("GK0", 160, F32), ("GK1", 160, F32), ("KY0", 648, F32), ("KY1", 648, F32), ("TN", 544, BF), ("DI", 96, I32), ("DM", 96, I32),
    ("AB", 512, BF), ("D0Y", 768, BF), ("D1Y", 768, BF), ("YS", 768, BF), ("YT", 640, BF), ("YW", 256, BF), ("V32", 256, BF), ("VV", 256, BF),
    ("OA1", 512, BF), ("OA2", 528, BF), ("OAO", 512, F32), ("YO", 512, F32),
) + tuple(("F%d" % t, W, BF) for t in range(R)) + tuple((n + "%d" % t, 256, d) for t in range(R) for n, d in (("SQ", CODES), ("SS", PLANE))) \
  + tuple((n + "%d" % t, 512, d) for t in range(R + 1) for n, d in (("XQ", CODES), ("XS", PLANE))):
    SCRATCH[_n] = ("sbuf", [128, _w], _d)

SEMAPHORES = ["cv", "cs", "ct", "cp", "left"] + ["arr%d" % t for t in range(2 * R)] + ["dm%d" % i for i in range(32)]
COUNTER = {"v": "cv", "s": "cs", "t": "ct", "p": "cp"}
PART = {}
for _b, _names in (
    ("IA", (("PI", 8), ("BITS", 8))),
    ("FA", (("N", 64), ("BP", 48), ("CAP", 129), ("RST", 64), ("HE", 4), ("XE", 4), ("B3", 6), ("BV", 6), ("BV2", 2), ("K32", 32), ("DU", 16), ("C8", 64), ("CBU", 64),
            ("NDD", 64), ("N4", 32), ("NM", 32), ("CC", 32), ("PP", 32), ("T0", 4), ("T3", 4), ("T4", 32), ("T5", 32))),
    ("SC", tuple((n, 1) for n in ("pm", "x", "p31", "qh", "h1", "x16", "pm32", "cs", "dl", "nil"))),
    ("SM", (("SPG", 2), ("NDL", 4), ("ZWL", 4), ("DL", 4))),
):
    _a = 0
    for _n, _w in _names:
        PART[_n] = (_b, _a, _w)
        _a += _w
CYC = 0.00083
LINK = 0.24
PACES = ((0.24, 0.0, 0.92, 0.02, 1.0, 0.35, 0.95, -0.45), (0.27, 0.0, 1.3, 0.02, 0.4, 0.6, 1.4, 0.0))
HEAT = (0.05, 0.004)
PLAN = {"seed": 1, "passes": 300, "moves": 110000, "short": (1, 1, 0, 1, 0, 1), "early": 0, "steps": 1, "sums": 3,
        "xcut": (0, 256, 384, 512),
        "gcut": (0, 8, 16, 24, 32), "vcut": (0, 4)}


def order(ops, seed, passes, moves):
    n = len(ops)
    need = [o["need"] for o in ops]
    users = [[] for _ in ops]
    for i in range(n):
        for k in need[i]:
            users[k].append(i)
    dur = [{q: a[1] for q, a in o["alt"].items()} for o in ops]
    state = [seed]

    def rnd():
        state[0] = (state[0] * 1103515245 + 12345) % 2147483648
        return state[0] / 2147483648.0

    def pick(xs):
        return xs[int(rnd() * len(xs))]

    def lay(rank, signal, wake, pace, margin, soon):
        free = {q: 0.0 for q in "vstpy"}
        left, due = [len(x) for x in need], [0.0] * n
        pool, seq, on = [i for i in range(n) if not need[i]], [], [""] * n

        def end(x, q):
            return (free[q] if due[x] <= free[q] else due[x] + wake) + pace[q][x]

        while pool:
            pool.sort(key=lambda i: rank[i])
            first, q = min((max(free[k], due[i]), k) for i in pool for k in dur[i])
            mine = [i for i in pool if q in dur[i]]
            x = top = [i for i in mine if due[i] <= first + soon][0]
            if due[top] > free[q]:
                fits = [i for i in mine if due[i] < due[top] and end(i, q) <= due[top] + wake - margin]
                x = ([i for i in fits if due[i] <= free[q]] + fits + [top])[0]
            if x == top:
                q = min(dur[x], key=lambda k: end(x, k) + (0.05 if k == "v" else 0.0))
            free[q] = end(x, q)
            on[x] = q
            seq.append(x)
            pool.remove(x)
            for u in users[x]:
                left[u] -= 1
                due[u] = max(due[u], free[q] + lat[x] + signal)
                if not left[u]:
                    pool.append(u)
        return seq, on

    paces = []
    lats = []
    for signal, wake, slow, extra, weight, calls, way, load in PACES:
        paces.append({q: [(d.get(q, 0.0) * slow + (extra if q == "s" else 0.0) if o["kind"] == "call" else d.get(q, 0.0) + calls * (o["kind"] == "send")) for o, d in zip(ops, dur)] for q in "vstpy"})
        lats.append([way if o["kind"] == "send" else o["lat"] + load * (o["kind"] != "call") for o in ops])
    lat = lats[0]
    stones = [i for i in range(n) if ops[i]["kind"] == "send" or ops[i]["name"][:2] == "XQ"]

    def run(seq, on, s, old, at):
        signal, wake = PACES[s][:2]
        pace, lat, done, free = paces[s], lats[s], list(old), {}
        for i in seq[at - 1::-1] if at else ():
            if on[i] not in free:
                free[on[i]] = done[i] - lat[i] - signal
                if len(free) == 5:
                    break
        for q in "vstpy":
            free.setdefault(q, 0.0)
        for i in seq[at:]:
            q = on[i]
            a, m = free[q], 0.0
            for k in need[i]:
                if done[k] > m:
                    m = done[k]
            if m > a:
                a = m + wake
            a += pace[q][i]
            free[q] = a
            done[i] = a + lat[i] + signal
        return done

    def value(seq, on, olds=None, at=0, limit=1e9, parts=None):
        total, dones = 0.0, []
        for s in range(len(PACES)):
            dones.append(run(seq, on, s, olds[s] if olds else [0.0] * n, at))
            total += max(dones[s]) * PACES[s][4]
            if parts and total + sum(parts[s + 1:]) - 0.6 > limit:
                return None
        return total + 0.1 * sum(dones[0][i] for i in stones) / len(stones), dones

    def chain(seq, on, dones):
        s = 0 if rnd() < 0.5 else int(rnd() * len(PACES))
        done, signal, lat = dones[s], PACES[s][0], lats[s]
        prev, last = {}, {}
        for i in seq:
            prev[i] = last.get(on[i], -1)
            last[on[i]] = i
        links, i = [], pick(stones) if rnd() < 0.3 else done.index(max(done))
        while i >= 0:
            p = prev[i]
            k = max(need[i], key=lambda z: done[z]) if need[i] else -1
            idle = k >= 0 and done[k] > (done[p] - signal - lat[p] if p >= 0 else 0.0)
            if idle or p >= 0:
                links.append((k if idle else p, i, idle))
            i = k if idle else p
        return links

    def ahead(seq, lo, hi, x):
        part, moved = seq[lo:hi], {x}
        for z in reversed(part):
            if z in moved:
                moved.update(need[z])
        return seq[:lo] + [z for z in part if z in moved] + [z for z in part if z not in moved] + seq[hi:], moved

    def behind(seq, lo, hi, x):
        part, moved = seq[lo:hi], {x}
        for z in part:
            if z in moved:
                moved.update(users[z])
        return seq[:lo] + [z for z in part if z not in moved] + [z for z in part if z in moved] + seq[hi:], moved

    tail = [0.0] * n
    for i in range(n - 1, -1, -1):
        tail[i] = min(paces[0][q][i] for q in dur[i]) + lat[i] + max([tail[u] + LINK for u in users[i]] + [0.0])
    best, base = None, [-x for x in tail]
    for it in range(passes):
        amp = pick((0.02, 0.1, 0.3))
        rank = [x + amp * rnd() for x in base]
        for k in range(pick((0, 1, 3, 10))):
            rank[int(rnd() * n)] += 3 * rnd() - 1.5
        seq, on = lay(rank, PACES[0][0] + pick((0.0, 0.02, 0.04)), PACES[0][1], paces[0], pick((0.0, -0.05, -0.1)), pick((0.15, 0.3, 0.5)))
        v = value(seq, on)[0]
        if best is None or v < best[0]:
            best, base = (v, seq, on), rank
    seq, on = best[1:]
    now, dones = value(seq, on)
    links = chain(seq, on, dones)
    for it in range(moves):
        a, b, idle = pick(links)
        r, pb = rnd(), seq.index(b)
        seq2, on2, x, q = seq, on, -1, on[b]
        if r < 0.2 and len(dur[a]) + len(dur[b]) > 2:
            x = a if len(dur[a]) > 1 and (len(dur[b]) == 1 or rnd() < 0.5) else b
            q, at = pick([k for k in dur[x] if k != on[x]]), seq.index(x)
        elif idle:
            far = pick((20, 60, 150))
            near = [z for z in (seq[pb + 1:pb + far] if r < 0.75 else seq[max(0, pb - far):pb]) if q in dur[z]]
            if not near:
                continue
            x = pick(near)
            px = seq.index(x)
            at = min(pb, px)
            seq2, moved = ahead(seq, pb, px + 1, x) if r < 0.75 else behind(seq, px, pb, x)
            if b in moved:
                continue
        elif r < 0.6:
            at = max(0, seq.index(a) - pick((0, 0, 0, 2, 6, 15)))
            seq2 = ahead(seq, at, pb + 1, b)[0]
        else:
            at = seq.index(a)
            seq2 = behind(seq, at, pb + 1 + pick((0, 0, 0, 2, 6, 15, 40, 80, 160)), a)[0]
        if x >= 0 and on[x] != q:
            on2 = list(on)
            on2[x] = q
        limit = now - HEAT[0] * (HEAT[1] / HEAT[0]) ** (it / moves) * math.log(rnd() + 1e-9)
        new = value(seq2, on2, dones, at, limit, [max(d) * p[4] for d, p in zip(dones, PACES)])
        if new and new[0] <= limit:
            (now, dones), seq, on = new, seq2, on2
            links = chain(seq, on, dones)
            if now < best[0]:
                best = (now, seq, on)
        elif rnd() < 0.05:
            links = chain(seq, on, dones)
    PLAN["est"] = [max(d) for d in value(best[1], best[2])[1]]
    return [(i, best[2][i]) for i in best[1]]


def make_plan(g, T):
    eng = {"v": g.vector, "s": g.scalar, "t": g.tensor, "p": g, "y": g.sync}
    ops = []
    hist = {}

    def view(name, lo=0, hi=None, step=1, ind=None, cast=None):
        if name in PART:
            name, at, width = PART[name]
            lo, hi = lo + at, (width if hi is None else hi) + at
        t = T[name]
        hi = int(t.shape[1]) if hi is None else hi
        ap = t[:, lo:hi:step] if step != 1 else t[:, lo:hi]
        deps = [(name, lo, hi, step)]
        n = (hi - lo + step - 1) // step
        if cast is not None:
            ap = ap.bitcast(cast)
        if ind is not None:
            o = view(*ind)
            ap = ap.indirect(o[0])
            deps.append(o[1][0])
            n = -16 * o[2]
        return ap, deps, n, SCRATCH[name][2] in (BF, U16), name == "PS"

    def bank(d):
        return (d[0], d[1] // 512 * 512, (d[2] + 511) // 512 * 512, 1) if d[0] == "PS" else d

    def note(alt, outs, ins, lat=0.0, kind="call"):
        reads = [d for v in ins for d in v[1] if d[0] != "PS"] + [d for v in outs for d in v[1][1:]]
        writes = [bank(v[1][0]) for v in outs if v[1]] + [bank(d) for v in ins for d in v[1] if d[0] == "PS"]
        me = len(ops)
        need = set()
        for acc, wr in ((reads, False), (writes, True)):
            for name, lo, hi, st in acc:
                for (a, b, s2, w, k) in hist.get(name, []):
                    if a < hi and lo < b and (w or wr) and (st != s2 or (lo - a) % st == 0):
                        need.add(k)
        for name, lo, hi, st in writes:
            hist[name] = [h for h in hist.get(name, []) if not (lo <= h[0] and h[1] <= hi and (st == 1 or st == h[2] and (lo - h[0]) % st == 0))] + [(lo, hi, st, True, me)]
        for name, lo, hi, st in reads:
            hist.setdefault(name, []).append((lo, hi, st, False, me))
        ops.append({"alt": alt, "need": sorted(need), "lat": lat, "kind": kind, "name": "%s%d" % outs[0][1][0][:2] if outs[0][1] else "out"})

    def issue():
        if "seq" not in PLAN:
            PLAN["ops"] = ops
            PLAN["seq"] = order(ops, PLAN["seed"], PLAN["passes"], PLAN["moves"])
        count = {}
        known = {q: {} for q in eng}
        mark = {}

        def wait(q, sem, val):
            if known[q].get(sem, 0) < val:
                known[q][sem] = val
                eng[q].wait_ge(T.sem[sem], val)

        ndma = 0
        loads = sorted(x for x in PLAN["seq"] if ops[x[0]]["kind"] == "load")
        for i, q in loads + [x for x in PLAN["seq"] if ops[x[0]]["kind"] != "load"]:
            o = ops[i]
            fn = o["alt"][q][0]
            need = {}
            for k in o["need"]:
                sem, val = mark[k]
                need[sem] = max(need.get(sem, 0), val)
            for sem in need:
                wait(q, sem, need[sem])
            if o["kind"] == "call":
                sem = COUNTER[q]
                count[sem] = count.get(sem, 0) + 1
                fn(eng[q]).then_inc(T.sem[sem], 1)
            elif o["kind"] == "send":
                sem, come, gone = fn(eng[q])
                count[sem] = come
                count["left"] = count.get("left", 0) + gone
            else:
                sem = "dm%d" % ndma
                ndma += 1
                count[sem] = 16
                fn(eng[q]).then_inc(T.sem[sem], 16)
            mark[i] = (sem, count[sem])
        for sem in count:
            wait("p", sem, count[sem])

    return view, note, issue


def rank_program(g, core, T, topo):
    rank = T.rank_of(core)
    if rank is None:
        return
    f, note, issue = make_plan(g, T)

    def cost(q, out, ins, per):
        if out[2] < 0:
            return 0.05 - out[2] * 0.0032
        for v in ins:
            if v[2] < 0:
                return (0.05 if q == "v" else 0.065) - v[2] * 0.0013
        return max(64, max(v[2] for v in [out] + ins) * per) * CYC

    def rate(*vs):
        return 0.5 if all(v[3] for v in vs) else 1.0

    def num(s):
        return s[0] if isinstance(s, tuple) else s

    def cols(*ss):
        return [s for s in ss if isinstance(s, tuple)]

    def tt(out, a, b, op):
        note({"v": (lambda e: e.tensor_tensor(out[0], a[0], b[0], op), cost("v", out, [a, b], 1.0 if a[4] or b[4] else 2.0))}, [out], [a, b])

    def v_ts(out, a, s1, op0, s2=None, op1=None):
        c = cost("v", out, [a], rate(out, a))
        if op1 is None:
            return (lambda e: e.tensor_scalar(out[0], a[0], num(s1), None, op0), c)
        return (lambda e: e.tensor_scalar(out[0], a[0], num(s1), num(s2), op0, op1), c)

    def v_cp(out, a):
        return (lambda e: e.tensor_copy(out[0], a[0]), cost("v", out, [a], rate(out, a)))

    def s_act(out, a, func, scale=1.0, bias=None):
        c = cost("s", out, [a], 1.0)
        if bias is not None:
            return (lambda e: e.activation(out[0], a[0], func, bias=num(bias), scale=num(scale)), c)
        if isinstance(scale, tuple) or scale != 1.0:
            return (lambda e: e.activation(out[0], a[0], func, scale=num(scale)), c)
        return (lambda e: e.activation(out[0], a[0], func), c)

    def ts(out, a, s1, op0, s2=None, op1=None):
        note({"v": v_ts(out, a, s1, op0, s2, op1)}, [out], [a] + cols(s1, s2))

    def cp(out, a):
        note({"v": v_cp(out, a)}, [out], [a])

    def move(out, a, scale=1.0, bias=None):
        if bias is not None:
            alt = {"v": v_ts(out, a, scale, OP.mult, bias, OP.add), "s": s_act(out, a, AF.Identity, scale, bias)}
        elif isinstance(scale, tuple) or scale != 1.0:
            alt = {"v": v_ts(out, a, scale, OP.mult), "s": s_act(out, a, AF.Copy, scale)}
        else:
            alt = {"v": v_cp(out, a), "s": s_act(out, a, AF.Copy)}
        note(alt, [out], [a] + cols(scale, bias))

    def below(out, a, last, n):
        note({"s": (lambda e: e.activation(out[0], a[0], AF.Sign, bias=last[0], scale=-1.0, accum_out=n[0]), cost("s", out, [a], 1.0) + 0.02)}, [out, n], [a, last])

    def fill(out, c):
        note({"v": (lambda e: e.memset(out[0], c), cost("v", out, [], rate(out)))}, [out], [])

    def const(out, c):
        one = f("ONE", 0, out[2])
        alt = {"v": (lambda e: e.memset(out[0], c), cost("v", out, [], rate(out))), "s": s_act(out, one, AF.Copy, c)}
        if c == int(c) and abs(c) < 2 ** 24:
            alt["p"] = (lambda e: e.iota(out[0], [[0, out[2]]], int(c), 0, allow_small_or_imprecise_dtypes=True), 0.13 + 2 * CYC * out[2])
        note(alt, [out], [one])

    def scan(out, d0, d1, init, op0, op1):
        note({"v": (lambda e: e.tensor_tensor_scan(out[0], d0[0], d1[0], init, op0, op1), cost("v", out, [d0, d1], rate(out, d0, d1)))}, [out], [d0, d1])

    def turn(out, a):
        note({"v": (lambda e: e.transpose(out[0], a[0]), cost("v", out, [a], rate(out, a)))}, [out], [a])

    def quant(qn, sn, lo, hi, a):
        q, s = f(qn, lo, hi), f(sn, lo, hi)
        note({"v": (lambda e: e.quantize_mx(q[0], s[0], a[0]), 0.012 + 0.00022 * a[2])}, [q, s], [a])

    def mm(out, l, ls, r, rs):
        note({"t": (lambda e: e.matmul_mx(out[0], l[0], ls[0], r[0], rs[0], True, True), (r[2] + 16) * 0.0005)}, [out], [l, ls, r, rs])

    def iota(out, pattern, base=0, cm=0, small=True):
        if small:
            note({"p": (lambda e: e.iota(out[0], pattern, base, cm, allow_small_or_imprecise_dtypes=True), 0.13 + 2 * CYC * out[2])}, [out], [])
        else:
            note({"p": (lambda e: e.iota(out[0], pattern, base, cm), 0.13 + 2 * CYC * out[2])}, [out], [])

    def dma(q, out, in_, lat=1.2, kind="dma", busy=0.15):
        note({k: (lambda e: e.dma_start(out[0], in_[0]), busy) for k in q}, [out], [in_], lat, kind)

    def hbm(ap):
        return (ap, [])

    dma("y", f("NDI"), hbm(T.nd[:, :]), 1.3, "load")
    dma("s", f("UT"), hbm(T.u[:, :]), 1.7, "load")
    early = PLAN["early"]
    if early:
        dma("y", f("ARI"), hbm(T.ar[:, :]), 2.2, "load")
    dma("s" if early else "y", f("XT", 0, 1024), hbm(T.x[:, 0:1024]), 2.5 + 0.5 * early, "load")
    dma("y" if early else "s", f("XT", 1024, 2048), hbm(T.x[:, 1024:2048]), 3.0 + 0.5 * early, "load")
    if not early:
        dma("y", f("ARI"), hbm(T.ar[:, :]), 3.5, "load")
    for out, src in ((f("WQ", cast=dt.uint8), T.wc), (f("WS"), T.ws), (f("VT"), T.v)):
        dma("y", out, (src[:, :], f("XT" if early else "ARI")[1]), 2.5)

    iota(f("PI", 0, 1), [[0, 1]], 0, 1, small=False)
    iota(f("N"), [[1, 64]])
    iota(f("BP"), [[0, 6], [1, 4], [0, 2]])
    iota(f("HE"), [[16, 2], [0, 2]])
    iota(f("XE"), [[0, 2], [1, 2]])
    iota(f("B3"), [[16, 2], [0, 3]])
    iota(f("K32"), [[0, 2], [1, 16]])
    iota(f("DU"), [[1, 16]], 512)
    iota(f("C8"), [[8, 64]], 3)
    iota(f("PP"), [[1, 16], [256, 2]])
    iota(f("IOT"), [[4, 512]])
    fill(f("ONE"), 1.0)
    ident, one = f("ID"), f("ONE", 0, 128)
    note({"p": (lambda e: e.affine_select(ident[0], one[0], [[-1, 128]], OP.is_equal, 0.0, 0, 1), 0.38)}, [ident], [one])
    const(f("ET"), 0.0)
    move(f("ET", 3, 515, 4), ident)
    for b in range(4):
        quant("EQ", "ES", 128 * b, 128 * b + 128, f("ET", 3 - b, 515 - b))
    for t in range(R):
        const(f("F%d" % t, 2048, W), 0.0)
    const(f("YT", 0, 512), 0.0)
    quant("LQ", "LS", 96, 224, f("YT", 0, 512))
    const(f("TAB", 512, 544), 0.0)
    const(f("TBL", 3, 512, 8), 0.0)
    const(f("OA2", 512, 528), 0.0)
    const(f("D0Y", 0, 768, 3), 0.0)
    const(f("D1Y", 1, 768, 3), 0.0)
    const(f("D1Y", 0, 768, 3), -BIG)
    const(f("TS", 512, 513), -BIG)
    const(f("TN", 512, 544), 0.0)
    if PLAN["sums"] > 1:
        const(f("KEEP", 0, 384), 1.0)
        const(f("KEEP", 384, 768), 1.0)
        const(f("KEEP", 0, 768, PLAN["sums"]), 0.0)
    const(f("CAP"), 2.0 ** 23)
    const(f("CAP", 0, 64, 16), NONE)
    const(f("CAP", 64, 129, 16), NONE - 2048)
    for j in range(2):
        const(f("KY%d" % j, 512, 513), NONE)

    pi = f("PI", 0, 1)
    for j, (sh, m) in enumerate(((0, 15), (4, 1), (0, 31), (3, 1), (0, 1))):
        ts(f("BITS", j, j + 1), pi, sh, OP.logical_shift_right, m, OP.bitwise_and)
    cp(f("SC", 0, 5), f("BITS", 0, 5))
    pm, x = f("pm"), f("x")
    for n, src, sc, bi in (("x16", "x", 16.0, None), ("pm32", "pm", 32.0, None), ("cs", "pm", -STEP, 12 * U + 15 * STEP), ("dl", "qh", 2.0, f("h1")),
                           ("nil", "pm", 1.0, float(EMPTY))):
        move(f(n), f(src), sc, bi)
    ts(f("DL", 0, 3), f("N", 0, 25, 12), f("dl"), OP.add, 16.0, OP.mult)
    ts(f("UL"), f("N", 0, 8), 16.0, OP.mult)
    ts(f("NDL"), f("HE"), pm, OP.add)
    ts(f("SPG"), f("N", 0, 64, 32), f("p31"), OP.add)
    ts(f("BV"), f("B3"), pm, OP.add, 16.0, OP.mult)
    ts(f("BV2"), f("BV", 2, 4), f("x16"), OP.subtract)
    ts(f("COL", EMPTY, 544), f("DU"), f("x16"), OP.add, 4.0, OP.mult)
    move(f("CBU"), f("C8"), U)
    ts(f("T0"), f("XE"), x, OP.not_equal, 1024.0, OP.mult)
    tt(f("T3"), f("T0"), f("HE"), OP.add)
    ts(f("ZWL"), f("T3"), f("pm32"), OP.add, 512.0, OP.min)
    ts(f("PA"), f("PP"), f("BV", 0, 1), OP.add)
    ts(f("T4"), f("K32"), pm, OP.is_equal, 1024.0, OP.mult)
    tt(f("T5"), f("T4"), f("N", 0, 32), OP.add)
    ts(f("PB"), f("T5"), f("pm32"), OP.add, 512.0, OP.min)

    quant("UQ", "US", 0, 128, f("UT"))
    cp(f("UQR", cast=dt.uint32), f("UQ", cast=dt.uint32, ind=("UL",)))
    move(f("USR"), f("US", ind=("UL",)))
    ts(f("NDD"), f("NDI", ind=("NDL",)), 4.0, OP.mult)
    turn(f("NW"), f("NDD"))
    move(f("N4"), f("NW", ind=("SPG",)))
    for h in range(2):
        ts(f("SL", h, 32, 2), f("N4", 16 * h, 16 * h + 16), 0.25, OP.mult)
    turn(f("NM"), f("N4"))
    move(f("CC"), f("NM"), 1.0, f("cs"))
    ts(f("NL"), f("NM"), 0.25, OP.mult)
    for a in range(2):
        move(f("COL", 256 * a, 256 * a + 256), f("IOT", ind=("NL", 16 * a, 16 * a + 16)))
    if PLAN["steps"]:
        for h in range(2):
            ts(f("ARB", 256 * h, 256 * h + 256), f("ARI", 256 * h, 256 * h + 256), U, OP.mult)
            const(f("ARB", 256 * h, 256 * h + 256, 17), MARK)
        for j in range(16):
            turn(f("TAB", j, 512, 16), f("ARB", j, 512, 16))
    else:
        ts(f("PD"), f("N", 0, 32), f("pm32"), OP.add)
        for a in range(2):
            ts(f("ARB", 256 * a, 256 * a + 256), f("ARI", ind=("PA", 16 * a, 16 * a + 16)), U, OP.mult)
        for h in range(2):
            const(f("ARB", 16 * h, 512, 33), MARK)
        turn(f("OA1"), f("ARB"))
        for a in range(2):
            move(f("TAB", 256 * a, 256 * a + 256), f("OA1", ind=("PD", 16 * a, 16 * a + 16)))

    nxt = T.cores[(rank + 1) % len(T.cores)]
    rid, pid, _ = topo.addr(nxt)
    engines = topo.engines(core, nxt)[:8]
    mask = sum(1 << k for k in engines)

    def landing(t, j):
        return 224 + 32 * t if j else 64 - 32 * t

    def send(t, j):
        a, b = 224 * j, landing(t, j)
        q, s = f("SQ%d" % t, a, a + 32, cast=dt.uint8), f("SS%d" % t, a, a + 32)
        lq, ls = f("LQ", b, b + 32, cast=dt.uint8), f("LS", b, b + 32)
        sem = "arr%d" % (2 * t + j)

        def go(e):
            e.remote_dma(lq[0], q[0], T.sem[sem], T.sem["left"], pid, rid, mask)
            e.remote_dma(ls[0], s[0], T.sem[sem], T.sem["left"], pid, rid, mask)
            return sem, 2 * len(engines), 2 * len(engines)
        note({"p": (go, 0.0 if t or j else 1.5)}, [lq, ls], [q, s], 0.0, "send")

    def chosen(j):
        return ("L2", 0, 2) if j else ("L1", 2, 4)

    def slots(j, t):
        ft, gk, ky = "F%d" % t, "GK%d" % j, "KY%d" % j
        short = PLAN["short"][2 * t + j]
        lo, y = 48 * j, 384 * j
        move(f(gk, 0, 32), f("COL", ind=chosen(j)))
        for io, tab in enumerate(("TAB", "TN")):
            tt(f(gk, 32 + 32 * io, 64 + 32 * io), f(tab, ind=chosen(j)), f("CC"), OP.add)
            if short:
                move(f(gk, 96 + 32 * io, 128 + 32 * io), f(tab, ind=chosen(j)), 1.0, f("cs"))
        w = 64 + 64 * short
        turn(f(ky, 0, 32 + w), f(gk, 0, 32 + w))
        k = f(ky, 32, 32 + w)
        scan(f(ky, 513, 513 + w), k, f("CAP", 1, 1 + w), NONE, OP.max, OP.min)
        scan(f(ky, 177, 177 + w), f("CAP", 0, w), k, BIG, OP.min, OP.max)
        scan(f(ky, 369, 369 + w), k, f(ky, 512, 512 + w), NONE, OP.max, OP.min)
        if short:
            for h in range(2):
                ts(f("LL", lo + h, lo + 8, 2), f("N", 0, 4), f(ky, 16 * h, 16 * h + 1), OP.add)
            for top in range(2):
                for n in range(4):
                    a, c = lo + 16 + 16 * top + 8 * (n // 2), 192 + 192 * top + 16 * n
                    ts(f("LL", a + n % 2, a + 8, 2), f("N", 0, 4), f(ky, c, c + 1), OP.add, f(ky, c + 64, c + 65), OP.subtract)
        else:
            di, dm = f("DI", lo, lo + 48), f("DM", lo, lo + 48)
            tt(di, f(ky, 0, 512, ind=("DL", 0, 3)), f("BP"), OP.add)
            ts(dm, di, 4095, OP.bitwise_and)
            cp(f("LL", lo, lo + 48), dm)
        for io in range(2):
            ab = f("AB", 256 * j + 128 * io, 256 * j + 128 * io + 128)
            move(ab, f(ft, ind=("LL", lo + 16 + 8 * io, lo + 24 + 8 * io)))
            tt(f("D0Y", y + 1 + io, y + 384, 3), f(ft, ind=("LL", lo + 32 + 8 * io, lo + 40 + 8 * io)), ab, OP.add)
        move(f("D1Y", y + 2, y + 384, 3), f(ft, ind=("LL", lo, lo + 8)), -2.0)
        scan(f("YS", y, y + 384), f("D0Y", y, y + 384), f("D1Y", y, y + 384), 0.0, OP.max, OP.add)
        for b in range(4):
            move(f("YT", 512 * j + b, 512 * j + 128, 4), f("YS", y + 96 * b + 2, y + 96 * b + 96, 3), 0.5)
        quant("SQ%d" % t, "SS%d" % t, 128 * j, 128 * j + 128, f("YT", 128 * j, 128 * j + 512))
        send(t, j)
        move(f("YW", 128 * j, 128 * j + 128), f("YS", y + 2, y + 384, 3), 16.0)

    def anew(j, t):
        c = landing(t, j) - 96 * j
        for b in range(4):
            at = (0, 512, 3072, 3584)[b] if j == 0 else 1024 + 512 * b
            lo = 128 * j + 32 * b
            mm(f("PS", at, at + 128), f("WQ", 128 * b, 128 * b + 128), f("WS", 128 * b, 128 * b + 128), f("LQ", c, c + 128), f("LS", c, c + 128))
            tt(f("V32", lo, lo + 32), f("PS", at + 96 * j, at + 96 * j + 32), f("YW", lo, lo + 32), OP.add)
        cut = PLAN["vcut"] if j else (0, 4)
        for a, b in zip(cut, cut[1:]):
            lo, hi = 128 * j + 32 * a, 128 * j + 32 * b
            move(f("VV", lo, hi), f("V32", lo, hi), 0.03125)
            cp(f("F%d" % t, ind=("LL", 48 * j + 2 * a, 48 * j + 2 * b)), f("VV", lo, hi))

    def arrows(last):
        xg, d4, a2, n2, na = f("XG"), f("XW", 0, 64), f("XW", 64, 128), f("XW", 128, 192), f("XW", 192, 256)
        for j in range(2):
            move(f("XG", 32 * j, 32 * j + 32), f("TAB", ind=chosen(j)))
        ts(d4, xg, MARK, OP.is_equal, 4 * U, OP.mult)
        note({"v": v_ts(a2, xg, 0.0, OP.max, 2.0, OP.mult), "s": s_act(a2, xg, AF.Relu, 2.0)}, [a2], [xg])
        ts(n2, xg, 0.0, OP.min, 2.0, OP.mult)
        tt(na, d4, a2, OP.subtract)
        pos = f("TBL", 5, 512, 8)
        tt(pos, n2, d4, OP.add)
        for k, src, c in ((0, na, -1.5), (1, na, -1.0), (2, na, -0.5), (4, pos, 0.5), (6, pos, 1.5)):
            move(f("TBL", k, 512, 8), src, c)
        tt(f("TBL", 7, 512, 8), na, pos, OP.subtract)
        tt(f("XI", 0, 64), xg, f("CBU"), OP.add)
        tt(f("XI", 64, 128), f("XI", 0, 64), d4, OP.add)
        ts(f("LA"), f("XI", 64, 128), 1.0 / U, OP.mult)
        n = PLAN["sums"]
        for a in range(2):
            lo, hi = 256 * a, 256 * a + 256
            e1, e2 = [f("TBL", ind=("LA", 32 * j + 16 * a, 32 * j + 16 * a + 16)) for j in range(2)]
            if n == 1:
                tt(f("T1", lo, hi), e1, f("TAB", lo, hi), OP.add)
                tt(f("T2", lo, hi), e2, f("T1", lo, hi), OP.add)
            else:
                if n == 2:
                    tt(f("T1", 2 * lo, 2 * hi, 2), e1, f("TAB", lo, hi), OP.add)
                else:
                    move(f("T1", 3 * lo, 3 * hi, 3), f("TAB", lo, hi))
                    move(f("T1", 3 * lo + 1, 3 * hi, 3), e1)
                move(f("T1", n * lo + n - 1, n * hi, n), e2)
                scan(f("T2", n * lo, n * hi), f("KEEP", 0, 256 * n), f("T1", n * lo, n * hi), 0.0, OP.mult, OP.add)
        for lo, hi in PLAN.get("clip", ((0, 256), (256, 512))):
            ts(f("TAB", lo, hi), f("T2", n * lo + n - 1, n * hi, n), 3 * U, OP.min, -3 * U, OP.max)
        if last:
            for a in range(2):
                move(f("OA1", 256 * a, 256 * a + 256), f("TAB", ind=("PA", 16 * a, 16 * a + 16)))
            turn(f("OA2", 0, 512), f("OA1"))
            for h in range(2):
                move(f("OAO", 256 * h, 256 * h + 256), f("OA2", ind=("PB", 16 * h, 16 * h + 16)), 1.0 / U)
                dma("y", hbm(T.oa[:, 256 * h:256 * h + 256]), f("OAO", 256 * h, 256 * h + 256), 2.2)

    for t in range(R):
        ft, xq, xs = "F%d" % t, "XQ%d" % t, "XS%d" % t
        src = "F%d" % (t - 1) if t else "XT"
        for a in range(2):
            o, i = f("TZ", 256 * a, 256 * a + 256), f("TAB", 256 * a, 256 * a + 256)
            note({"s": s_act(o, i, AF.Abs, 2.0 ** 90), "v": v_ts(o, i, 0.0, OP.not_equal, BIG, OP.mult)}, [o], [i])
            move(f("TN", 256 * a, 256 * a + 256), i, -1.0)
        XCUT, GCUT = PLAN["xcut"], PLAN["gcut"]
        for a, (lo, hi) in enumerate(zip(XCUT, XCUT[1:])):
            quant(xq, xs, lo, hi, f(src, 4 * lo, 4 * hi))
            mm(f("PS", 512 * a, 512 * a + hi - lo), f("UQR"), f("USR"), f(xq, lo, hi), f(xs, lo, hi))
            move(f("PW", lo, hi), f("PS", 512 * a, 512 * a + hi - lo))
        for lo, hi in zip(GCUT, GCUT[1:]):
            move(f("SG", 16 * lo, 16 * hi), f("PW", ind=("SL", lo, hi)))
            turn(f("TS", 16 * lo, 16 * hi), f("SG", 16 * lo, 16 * hi))
        for a in range(2):
            for b in range(4):
                at = 2048 + 512 * b if a == 0 else (1536, 0, 512, 1024)[b]
                mm(f("PS", at, at + 256), f("EQ", 128 * b, 128 * b + 128), f("ES", 128 * b, 128 * b + 128), f(xq, 256 * a, 256 * a + 256), f(xs, 256 * a, 256 * a + 256))
                move(f(ft, 1024 * a + b, 1024 * a + 1024, 4), f("PS", at, at + 256))
        move(f("ZW"), f("TS", ind=("ZWL",)))
        turn(f("ZM"), f("ZW"))
        for e in range(2):
            s, r = f("TS", 16 * e, 512, 32), 16 * e
            scan(f("RX", r, r + 16), s, s, -BIG, OP.max, OP.max)
            below(f("JK", r, r + 16), f("RX", r, r + 16), f("RX", r + 15, r + 16), f("IX", e, e + 1))
            ts(f("L1", 3 * e, 3 * e + 3), f("BV", 3 * e, 3 * e + 3), f("IX", e, e + 1), OP.add)
        for e in range(2):
            lo = 32 * e
            tt(f("GM", lo, lo + 32), f("TZ", ind=("L1", 4 * e, 4 * e + 2)), f("ZM", lo, lo + 32), OP.subtract)
            s, r = f("GT", lo, lo + 32), 32 + lo
            turn(s, f("GM", lo, lo + 32))
            scan(f("RX", r, r + 32), s, s, 4 * BIG, OP.min, OP.min)
            below(f("JK", r, r + 32), f("RX", r, r + 32), f("RX", r + 31, r + 32), f("IX", 2 + e, 3 + e))
        ts(f("IX", 4, 6), f("RX", 63, 96, 32), 1.0e23, OP.is_gt, f("nil"), OP.mult)
        for e in range(2):
            ts(f("L2", e, e + 1), f("BV2", e, e + 1), f("IX", 2 + e, 3 + e), OP.subtract, f("IX", 4 + e, 5 + e), OP.max)
        slots(0, t)
        slots(1, t)
        arrows(t == R - 1)
        anew(0, t)
        anew(1, t)

    quant("VQ", "VS", 0, 128, f("VT"))
    for a in range(4):
        lo, hi = 128 * a, 128 * a + 128
        quant("XQ3", "XS3", lo, hi, f("F2", 512 * a, 512 * a + 512))
        mm(f("PS", 512 * a, 512 * a + 128), f("VQ"), f("VS"), f("XQ3", lo, hi), f("XS3", lo, hi))
        move(f("YO", lo, hi), f("PS", 4 * lo, 4 * lo + 128))
    for lo, hi in ((0, 256), (256, 512)):
        dma("ys", hbm(T.oc[:, 4 * lo:4 * hi]), f("XQ3", lo, hi, cast=dt.uint8), 1.6)
    for lo, hi in ((0, 256), (256, 384), (384, 512)):
        dma("ys", hbm(T.y[:, lo:hi]), f("YO", lo, hi), 1.0 + (hi - lo) / 400.0)
    for k in range(4):
        dma("ys", hbm(T.osc[4 * k:4 * k + 4, :]), (T.XS3[32 * k:32 * k + 4, 0:512], [("XS3", 0, 512, 1)]))
    issue()
